import numpy as np, ml_dtypes
CORES = [51,54,179,182]
N = 4
BF = ml_dtypes.bfloat16
def gentries(a):
    return np.ascontiguousarray(a.reshape(8, 16, -1).transpose(0, 2, 1)).reshape(8, -1)
def gtable(e):
    e = np.asarray(e); return np.ascontiguousarray(e.reshape(8, -1, 16).transpose(0, 2, 1)).reshape(128, -1).astype(np.int32)
W, K, NK, RO = 1024, 256, 4, 3
def sign(rng, *shape):
    return (2 * rng.integers(0, 2, shape) - 1).astype(np.float32)
def unit(rng, *shape):
    return rng.random(shape, dtype=np.float32)
def parts(rng, lo=-1, hi=0, gap=0.3):
    col = np.exp2(rng.integers(lo, hi + 1, (N, 8, 1, W))).astype(np.float32) * (unit(rng, N, 8, 1, W) >= gap)
    b = sign(rng, N, 8, 16, W) * (np.float32(0.75) + np.float32(0.5) * unit(rng, N, 8, 16, W)) * col
    w = sign(rng, N, 8, 16, W) * (np.float32(0.25) + np.float32(0.25) * unit(rng, N, 8, 16, W))
    rec = np.float32(0.25) + np.float32(0.75) * unit(rng, N, 8, 16, W)
    t = np.exp2(rng.integers(-8, -3, (N, 8, 1, 1))) * (0.7 + 0.6 * rng.random((N, 8, 16, 1)))
    p = np.argsort(rng.random((N, 8, NK + 2, W)), axis=-1)
    d = np.ascontiguousarray(np.argsort(rng.random((N, 8, W)), axis=-1)[..., :K])
    return b, w, rec, t, p, d
def pack(b, w, rec, t, p, d):
    return {"b0": b.reshape(N, 128, W).astype(BF), "w": w.reshape(N, 128, W).astype(BF), "rec": rec.reshape(N, 128, W).astype(BF), "th": t.reshape(N, 128, 1).astype(np.float32),
            "hop": np.ascontiguousarray(p[:, :, :NK].reshape(N, 8, NK * W)).astype(np.int32), "up": np.ascontiguousarray(p[:, :, NK]).astype(np.int32),
            "dn": np.ascontiguousarray(p[:, :, NK + 1]).astype(np.int32), "wk": np.stack([gtable(a) for a in d])}
def rest(rng, d):
    m = np.ones(W, bool); m[d] = False
    return rng.permutation(np.flatnonzero(m))
def goal(q, g, i):
    return (q, g) if i < NK else ((q + 1) % N, (g + 1) % 8) if i == NK else ((q - 1) % N, g)
def route(rng, d, y, shut, src=(), dst=()):
    y = y.copy(); f = y < 0; ok = ~shut; ok[y[~f]] = False
    y[f] = rng.permutation(np.flatnonzero(ok))[:np.count_nonzero(f)]
    d = np.concatenate([d, np.asarray(src, np.int64)]); y = np.concatenate([y, np.asarray(dst, np.int64)])
    p = np.zeros(W, np.int64); p[d] = y; a = np.ones(W, bool); a[d] = False; v = np.ones(W, bool); v[y] = False
    p[a] = rng.permutation(np.flatnonzero(v))
    return p
def odd(rng, *shape):
    return (2 * rng.integers(65, 127, shape) + 1).astype(np.float32)
def choose(ok, *v):
    i = np.argmax(ok, axis=0)[None]
    return [np.take_along_axis(a, i, 0)[0] for a in v]
def setup_inputs(rng):
    return pack(*parts(rng))
def setup_inputs_spread(rng):
    b, w, rec, t, p, d = parts(rng, -1, 1)
    w = sign(rng, N, 8, 16, W) * np.exp2(-4 + 3 * unit(rng, N, 8, 16, W)); rec = 0.0625 + 0.9375 * unit(rng, N, 8, 16, W)
    t = np.exp2(-11 + 9 * rng.random((N, 8, 16, 1)))
    return pack(b, w, rec, t, p, d)
def setup_inputs_ends(rng):
    M = K // 4; h = K // 2; s = sign(rng, 16)[:, None]; j = np.arange(M)
    size = rng.choice(np.array([64.0, 64.0, 2.0 ** -20, 0.0]), (N, 8, 1, W)).astype(np.float32)
    b = sign(rng, N, 8, 16, W) * size
    w = sign(rng, N, 8, 16, W) * rng.choice(np.array([0.5, 0.0625]), (N, 8, 1, W)).astype(np.float32)
    rec = np.where(unit(rng, N, 8, 16, W) < 0.5, np.float32(1), np.float32(0.0625))
    t = np.zeros((N, 8, 16, 1)); p = np.zeros((N, 8, NK + 2, W), np.int64); d = np.zeros((N, 8, K), np.int64); x = np.zeros((N, 8, 3, M), np.int64)
    for q in range(N):
        for g in range(8):
            d[q, g] = rng.permutation(np.concatenate([np.arange(h), W - h - g % 2 + np.arange(h)]))
            r = rest(rng, d[q, g]); r = r[np.argsort(r != W - 1, kind="stable")][:3 * M].reshape(3, M)
            x[q, g] = r if g % 4 == 3 else r[::-1]
            a = d[q, g, K - M:]; b[q, g][:, a] = 64 * s; w[q, g][:, a] = 0.5; rec[q, g][:, a] = 1
            b[q, g][:, x[q, g, 0]] = s * np.array([-64.0, 0.0, 64.0])[j % 3]
            b[q, g][:, x[q, g, 1]] = s * np.array([64.0, 0.0, 64.0])[j % 3]
            b[q, g][:, x[q, g, 2]] = -s * np.array([64.0, 0.0, 64.0, 63.75, 0.0, 64.0])[j % 6]
            xx = x[q, g].reshape(-1); w[q, g][:, xx] = 0.5; rec[q, g][:, xx] = 1
            n = (9, 16, 8, 10, 9, 12, 9, 16)[(g + q) % 8]
            t[q, g, :, 0] = np.where(rng.permutation(16) < n, 2.0 ** -20, 64.0)
    for q in range(N):
        for g in range(8):
            for i in range(NK + 2):
                xx = x[goal(q, g, i)]; y = np.full(K, -1); y[K - M:] = xx[0]; shut = np.zeros(W, bool); shut[xx.reshape(-1)] = True
                p[q, g, i] = route(rng, d[q, g], y, shut, x[q, g, :2].reshape(-1), xx[1:].reshape(-1))
    return pack(b, w, rec, t, p, d)
def setup_inputs_corners(rng):
    b, w, rec, t, p, d = parts(rng, 0, 0, 0.1); M = K // 2; L = K // 8; U = K // 16; e = np.float32(2.0 ** -9); e1 = np.float32(2.0 ** -8)
    x = np.zeros((N, 8, NK, M), np.int64); z = np.zeros((N, 8, 3, L), np.int64); xn = np.zeros((N, 8, 2, U), np.int64); shut = np.zeros((N, 8, W), bool)
    kind = (np.arange(N)[:, None] + np.arange(8)[None, :]) % 8; need = np.array([8, 9, 8, 9, 7, 10, 0, 16])[kind]
    late = (kind == 2) | (kind == 3); low = (need < 9)[:, :, None]
    tb = odd(rng, 64, N, 8, 16) * e1; tr = odd(rng, 64, N, 8, 16) * e1; tw = odd(rng, 64, N, 8, 16) * e; xw = odd(rng, 64, N, 8, 16) * e
    h = (tb * tr) * tw; top = h.astype(BF).astype(np.float32); h2 = top + (h - top).astype(BF).astype(np.float32)
    tb, tr, tw, xw = choose(np.where(low, h2 * xw > h * xw, h2 * xw < h * xw), tb, tr, tw, xw)
    gm = ((tb * tr) * tw) * xw
    yv = odd(rng, 256, N, 8, 16) * e1; yr = odd(rng, 256, N, 8, 16) * e1; zw = odd(rng, 256, N, 8, 16) * e; b2 = yv
    for k in range(NK): b2 = b2 + gm
    dl = b2 * yr; g2 = (xw * dl) * zw; g3 = dl * (xw * zw); g4 = (b2 * (yr * xw)) * zw
    yv, yr, zw, g2 = choose(np.where(low, (g3 > g2) & (g4 > g2), (g3 < g2) & (g4 < g2)), yv, yr, zw, g2)
    for q in range(N):
        for g in range(8):
            r = rest(rng, d[q, g]); xn[q, g] = r[:2 * U].reshape(2, U); r = r[2 * U:]
            for i in range(2):
                to = goal(q, g, NK + i); a = d[q, g, 8 + i * U:8 + (i + 1) * U]
                b[q, g][:, a] = tb[to][:, None] * sign(rng, 16, U); rec[q, g][:, a] = tr[to][:, None]; w[q, g][:, a] = tw[to][:, None] * sign(rng, 16, U)
            xx = xn[q, g].reshape(-1); b[q, g][:, xx] = 0; w[q, g][:, xx] = xw[q, g][:, None] * sign(rng, 16, 2 * U); shut[q, g, xx] = True
            n = int(need[q, g]); o = rng.permutation(16); gl = g2[q, g] if late[q, g] else gm[q, g]
            t[q, g, :, 0] = gl; t[q, g, o[:n], 0] = np.nextafter(gl[o[:n]], np.float32(0))
            if late[q, g]:
                z[q, g] = r[:3 * L].reshape(3, L); shut[q, g, r[:3 * L]] = True; sb = sign(rng, 16, L); sw = sign(rng, 16, L); sy = sign(rng, 16, L)
                a = d[q, g, K - L:]; b[q, g][:, a] = tb[q, g][:, None] * sb; rec[q, g][:, a] = tr[q, g][:, None]; w[q, g][:, a] = tw[q, g][:, None] * sw
                a = z[q, g, 0]; b[q, g][:, a] = -sb * sw * sy * yv[q, g][:, None]; rec[q, g][:, a] = yr[q, g][:, None]; w[q, g][:, a] = xw[q, g][:, None] * sy
                a = z[q, g, 1]; b[q, g][:, a] = 0; w[q, g][:, a] = zw[q, g][:, None] * sign(rng, 16, L)
                v = zw[q, g][:, None] * sign(rng, 16, L); ab = odd(rng, 16, L) * np.float32(2.0 ** -22) * sign(rng, 16, L); ar = odd(rng, 16, L) * e1; aw = odd(rng, 16, L) * e * sign(rng, 16, L)
                a = d[q, g, K - 2 * L:K - L]; b[q, g][:, a] = ab; rec[q, g][:, a] = ar; w[q, g][:, a] = aw
                a = z[q, g, 2]; w[q, g][:, a] = v; b[q, g][:, a] = (((ab * ar) * aw) * v).astype(BF).astype(np.float32)
                continue
            x[q, g] = r[:NK * M].reshape(NK, M); a = d[q, g, K - M:]
            b[q, g][:, a] = tb[q, g][:, None] * sign(rng, 16, M); rec[q, g][:, a] = tr[q, g][:, None]; w[q, g][:, a] = tw[q, g][:, None] * sign(rng, 16, M)
            xx = x[q, g].reshape(-1); v = np.repeat(xw[q, g][:, None], xx.size, axis=1); u = rng.integers(0, 5, xx.size); b[q, g][:, xx] = 0; shut[q, g, xx] = True
            if n > 0:
                j = np.flatnonzero(u == 1); v[o[rng.integers(0, n, j.size)], j] -= e
            if n < 16:
                j = np.flatnonzero(u == 2); v[o[rng.integers(n, 16, j.size)], j] += e
            j = np.flatnonzero(u == 3); b[q, g][rng.integers(0, 16, j.size), xx[j]] = np.float32(2.0 ** -20) * sign(rng, j.size)
            w[q, g][:, xx] = v * sign(rng, 16, xx.size)
    for q in range(N):
        for g in range(8):
            for i in range(NK + 2):
                y = np.full(K, -1); to = goal(q, g, i); src = np.zeros(0, np.int64); dst = src
                if i >= NK: y[8 + (i - NK) * U:8 + (i - NK + 1) * U] = xn[to][i - NK]
                elif late[q, g]:
                    y[K - L:] = z[q, g, 0]
                    if i == 0: y[K - 2 * L:K - L] = z[q, g, 2]
                    if i < 2: src = z[q, g, 0]; dst = z[q, g, 1 + i]
                else: y[K - M:] = x[q, g, i]
                if i == 0: y[:8] = d[q, g, :8]
                p[q, g, i] = route(rng, d[q, g], y, shut[to], src, dst)
    return pack(b, w, rec, t, p, d)
def setup_inputs_crowd(rng):
    b, w, rec, t, p, d = parts(rng, -1, -1); T = K // (2 * NK); M = K // 4
    x = np.zeros((N, 8, NK, M), np.int64); c = np.zeros((N, 8, T), np.int64); e = np.float32(2.0 ** -9)
    for q in range(N):
        for g in range(8):
            r = rest(rng, d[q, g]); c[q, g] = r[:T]; x[q, g] = r[T:T + NK * M].reshape(NK, M)
            m = d[q, g, :NK * T]; b[q, g][:, m] = sign(rng, 16, NK * T) * (0.75 + 0.5 * unit(rng, 16, NK * T))
            b[q, g][:, c[q, g]] = 2 * sign(rng, 16, T); rec[q, g][:, c[q, g]] = 0.5 + 0.25 * unit(rng, 16, T)
            j = np.arange(2, T, 3); b[q, g][rng.integers(0, 16, j.size), c[q, g, j]] = 0
            a = d[q, g, K - M:]; sb = sign(rng, 16, M); sw = sign(rng, 16, M)
            b[q, g][:, a] = sb * odd(rng, 16, M) * np.float32(2.0 ** -17); w[q, g][:, a] = sw * odd(rng, 16, M) * e; rec[q, g][:, a] = 0.5 + 0.5 * unit(rng, 16, M)
            o = np.argsort(rng.random((NK, 16, M)), axis=0)
            for k in range(NK):
                sx = sign(rng, 16, M); b[q, g][:, x[q, g, k]] = sx
                w[q, g][:, x[q, g, k]] = -sb * sw * sx * (200 + o[k]).astype(np.float32) * e
    for q in range(N):
        for g in range(8):
            for i in range(NK + 2):
                y = np.full(K, -1); shut = np.zeros(W, bool); z = goal(q, g, i); shut[x[z].reshape(-1)] = True; shut[c[z]] = True
                if i < NK:
                    y[i * T:(i + 1) * T] = np.where((np.arange(T) % 3 == 1) & (i == 0), -1, c[q, g]); y[K - M:] = x[q, g, i]
                p[q, g, i] = route(rng, d[q, g], y, shut)
    return pack(b, w, rec, t, p, d)
def setup_inputs_level(rng):
    b, w, rec, t, p, d = parts(rng)
    s = np.where(unit(rng, N, 8, 1, W) < 0.25, sign(rng, N, 8, 16, W), sign(rng, 1, 1, 16, 1) * sign(rng, N, 8, 1, W))
    b = s * np.exp2(rng.integers(-1, 1, (N, 8, 1, W))) * (unit(rng, N, 8, 1, W) >= 0.3)
    w = sign(rng, N, 8, 1, W) * np.exp2(rng.integers(-2, 0, (N, 8, 1, W))) + np.zeros((N, 8, 16, W))
    rec = np.exp2(rng.integers(-1, 1, (N, 8, 1, W))) + np.zeros((N, 8, 16, W))
    e = rng.integers(-6, -2, (N, 8, 1, 1)).astype(np.float64); n = rng.integers(8, 10, (N, 8, 1, 1))
    t = np.where(np.argsort(rng.random((N, 8, 16, 1)), axis=2) < n, np.exp2(e - 1), np.exp2(e))
    return pack(b, w, rec, t, p, d)
def check_ranges(d):
    bad = []
    for k in ("hop", "up", "dn", "wk"):
        if np.min(d[k]) < 0 or np.max(d[k]) > W - 1: bad.append("range of " + k)
    for k in ("hop", "up", "dn"):
        if np.any(np.sort(np.asarray(d[k]).reshape(N, 8, -1, W), axis=-1) != np.arange(W)): bad.append(k + " is no permutation")
    e = np.sort(np.stack([gentries(np.asarray(a)) for a in d["wk"]]), axis=-1)
    if np.any(e[..., 1:] == e[..., :-1]): bad.append("wk names a place twice in a group")
    a = np.abs(np.asarray(d["b0"]).astype(np.float32))
    if not np.all((a == 0) | ((a >= 2.0 ** -20) & (a <= 64))): bad.append("range of b0")
    a = np.abs(np.asarray(d["w"]).astype(np.float32))
    if not np.all((a >= 0.0625) & (a <= 0.5)): bad.append("range of w")
    a = np.asarray(d["rec"]).astype(np.float32)
    if not np.all((a >= 0.0625) & (a <= 1)): bad.append("range of rec")
    a = np.asarray(d["th"]).astype(np.float32)
    if not np.all((a >= 2.0 ** -20) & (a <= 64)): bad.append("range of th")
    return bad
def pick(a, ix):
    return np.take_along_axis(a, ix[:, :, None, :], 3)
def place(a, ix, v):
    np.put_along_axis(a, ix[:, :, None, :], v, 3)
def arrive(b, wf, t, x, h):
    g = h * pick(wf, x); o = pick(b, x)
    new = np.all(o == 0, axis=2, keepdims=True); few = np.sum(np.abs(g) > t, axis=2, keepdims=True) < 9
    place(b, x, np.where(new & few, o, o + g))
def reference(b0, w, rec, th, hop, up, dn, wk):
    b = b0.astype(np.float32).reshape(N, 8, 16, W).copy(); wf = w.astype(np.float32).reshape(N, 8, 16, W); rf = rec.astype(np.float32).reshape(N, 8, 16, W)
    t = th.astype(np.float32).reshape(N, 8, 16, 1); hp = hop.astype(np.int64).reshape(N, 8, NK, W); ul = up.astype(np.int64); dl = dn.astype(np.int64)
    d = np.stack([gentries(a) for a in wk]).astype(np.int64); c = np.zeros((N, 8, 16, W), np.float32)
    for s in range(RO):
        delta = -(pick(b, d) * pick(rf, d))
        place(c, d, pick(c, d) + delta); place(b, d, np.float32(0))
        h = pick(wf, d) * delta
        xs = [np.take_along_axis(hp[:, :, k], d, 2) for k in range(NK)]
        for x in xs: arrive(b, wf, t, x, h)
        x = np.take_along_axis(ul, d, 2); arrive(b, wf, t, np.roll(x, (1, 1), (0, 1)), np.roll(h, (1, 1), (0, 1)))
        x = np.take_along_axis(dl, d, 2); arrive(b, wf, t, np.roll(x, -1, 0), np.roll(h, -1, 0))
        if s == RO - 1: break
        m = np.stack([np.abs(pick(b, x)) for x in xs])
        votes = np.sum(m == np.max(m, axis=0), axis=3)
        ch = np.argmax(votes, axis=0)
        to = np.take_along_axis(np.stack(xs), ch[None], 0)[0]
        held = np.zeros((N, 8, W), bool); np.put_along_axis(held, d, True, 2)
        first = np.full((N, 8, W), NK)
        for k in range(NK - 1, -1, -1):
            qq, gg, jj = np.nonzero(ch == k); first[qq, gg, to[qq, gg, jj]] = k
        go = ~np.take_along_axis(held, to, 2) & (np.take_along_axis(first, to, 2) == ch)
        d = np.where(go, to, d)
    return {"yb": b.reshape(N, 128, W), "yc": c.reshape(N, 128, W)}

def check_inputs(d):
    bad = list(check_ranges(d))
    if not bad:
        for name, y in reference(**d).items():
            for q in range(N):
                v = np.abs(np.asarray(y[q], np.float64)); s = np.sqrt(np.mean(v * v))
                if v.max() > 9 * s or s < 2.0 ** -3: bad.append('%s of rank %d is uneven or too small' % (name, q))
    return bad

@@ -1,0 +1,525 @@
+from concourse.bass import DstId, RemoteDMATransfer
+from concourse.mybir import AluOpType, ActivationFunctionType
+
+W, K, NK, RO = 1024, 256, 4, 3
+PW = K + 16
+HW = K + 32
+ZC = 4 * W
+ORDER = (
+    "0102090004030a0b0h0c0g050f0d060p07080i0y0e0k0v0j0w0m0n0o0q0r0s0t0z0u140l1017111512161318191b1v1s1c221t1w1u231x1y1z2420251l21262728291e1a2j2a1d2c2b2e2k2d2f1m2l1g2h1f2g2m2n2i2o302q2p2r2t2v2s312u1n2w1h1q1o322y332x1p342z353h3i383j0x3k3c36391i373a3l3d1r3b3m3f3e3n3g3o3p413s1j3q3r3u3w3t423v3x433z3y444540461k4748494d4b4a4e4c4g4f4h4i4j4k4s4l4t4m4u4n4v4o4z4p4y504r4x514w525455534q565758595a5c5h5f5e5g5d5k5j5b5l5i5m5o5n5p5q5r5s5w5t5x5y5u605z5v6162646g656q6j6l6h676k6i6r69636m776s666n6t6o786u6p79686v7a6x6w6a7b6y72706z737o717c757d7p747q7e767r6c7s6e7f6b6d7j7h7g7k7i7t7m7l8586877n887u807w7y7x7v89817z6f838a828b848c8d8p8g8e8f8i8k8h8q8j8l8r8n8m8s8t8o8u8v8w8x918z8y92909493959697989g999h9a9i9b9j9c9n9d9l9o9f9k9p9m9r9t9s9q9e9u9v9w9x9ya0a3a4a2a5a1a7a89za9a6aaabacadaeafagakahalamaiaoanajaqaparatb2asb5b8bfaub6baavb9bgb7bwbhbbbcawdxbibdbxbjbebybkbzbmblb3c0bnbrbpbobscdbqc1buc2cebtcfc3bvcgaxchc4c8c6c5c9c7cicbcacucvcwcccxcjckb4clcpcncmcycqcodeczcrcsdfdgd0ctd1d2ayd5d3d4d9d7d6dad8dhdcdbdidjdddkdlazdmdqdodndrb0dpdsdtb1dudvdw")
+CFG = {"order": [int(ORDER[i:i + 2], 36) for i in range(0, len(ORDER), 2)],
+       "mode": "0CCCAC", "src": "ggggwg", "half": 2, "p4": 2, "dense": 0, "spec": 0, "raw": 0, "pm": 0, "pin": 1, "cs": 1, "seeds": (0, 0, 0, 0, 0), "amp": 0.0,
+       "m": {"sc": 3.8, "ga": 1.56, "f": 1.25, "pe": 0.42, "wake": 120.0, "iss": 100.0, "lat": 4500.0}}
+
+SCRATCH = {
+    "b16": ("sbuf", [128, W], "bfloat16"), "w16": ("sbuf", [128, W], "bfloat16"), "r16": ("sbuf", [128, W], "bfloat16"),
+    "thr": ("sbuf", [128, 4], "float32"), "nth": ("sbuf", [128, 4], "float32"), "tb": ("sbuf", [128, W], "int32"), "wki": ("sbuf", [128, 16], "int32"),
+    "bb": ("sbuf", [128, W], "float32"), "cc": ("sbuf", [128, W], "float32"), "ee": ("sbuf", [128, 5 * W + 16], "float32"),
+    "kz": ("sbuf", [128, K], "float32"), "k01": ("sbuf", [128, 2 * K], "float32"),
+    "uu": ("sbuf", [128, 160], "float32"), "u16": ("sbuf", [128, 128], "float32"), "pi": ("sbuf", [128, 8], "int32"),
+    "pf": ("sbuf", [128, 8], "float32"), "pg": ("sbuf", [128, 8], "float32"), "mk0": ("sbuf", [128, 48], "float32"), "mk": ("sbuf", [128, 48], "float32"),
+    "sel": ("sbuf", [128, 160], "bfloat16"), "bd": ("sbuf", [128, 128], "bfloat16"), "idn": ("sbuf", [128, 128], "bfloat16"),
+    "e0": ("sbuf", [128, 160], "float16"), "e1": ("sbuf", [128, 160], "float16"), "sh": ("sbuf", [128, 128], "float32"),
+    "du": ("sbuf", [128, 16 * RO], "uint16"), "dp": ("sbuf", [128, 16], "uint16"), "df": ("sbuf", [128, 16 * RO], "float32"),
+    "xg": ("sbuf", [128, K], "float16"), "yy": ("sbuf", [128, K], "float16"), "xu": ("sbuf", [128, 96], "uint16"),
+    "nr": ("sbuf", [128, K], "float32"), "dl": ("sbuf", [128, K], "float32"),
+    "hb": ("sbuf", [128, RO * HW], "float32"), "lu": ("sbuf", [128, RO * PW], "float32"), "ld": ("sbuf", [128, RO * PW], "float32"),
+    "gg": ("sbuf", [128, 2 * K], "float32"), "ab": ("sbuf", [128, 2 * K], "float32"), "rl": ("sbuf", [128, 2 * K], "bfloat16"),
+    "ov": ("sbuf", [128, 2 * K], "bfloat16"), "idf": ("sbuf", [128, 128], "float32"), "br": ("sbuf", [128, W], "float32"),
+    "hw": ("sbuf", [128, W], "float32"), "wf": ("sbuf", [128, 16], "float32"), "u2": ("sbuf", [128, 48], "float32"), "rw": ("sbuf", [128, 2 * K], "float32"),
+    "mn": ("sbuf", [128, K], "bfloat16"), "nz": ("sbuf", [128, K], "bfloat16"), "n1": ("sbuf", [128, K], "bfloat16"), "ss": ("sbuf", [128, K], "float32"),
+    "ac": ("sbuf", [128, K], "float32"), "wx": ("sbuf", [128, 2 * K], "float32"), "cg": ("sbuf", [128, K], "float32"),
+    "aa": ("sbuf", [128, NK * K], "float32"), "eq": ("sbuf", [128, NK * K], "bfloat16"),
+    "ck": ("sbuf", [128, 64], "float32"), "ky": ("sbuf", [128, 64], "float32"), "k2": ("sbuf", [128, 32], "float32"),
+    "ki": ("sbuf", [128, 48], "int32"), "eu": ("sbuf", [128, 16], "uint16"), "gl": ("sbuf", [128, 48], "uint16"),
+    "xf": ("sbuf", [128, 16], "float32"), "gt": ("sbuf", [128, 3 * K], "bfloat16"), "sc": ("sbuf", [128, 48], "float32"),
+    "uv": ("sbuf", [128, 32], "float32"),
+    "px": ("psum", [128, 512], "float32"), "pc": ("psum", [128, 512], "float32"),
+    "ps0": ("psum", [128, 512], "float32"), "ps1": ("psum", [128, 512], "float32"),
+    "pr0": ("psum", [128, 512], "float32"), "pr1": ("psum", [128, 512], "float32"),
+    "pw0": ("psum", [128, 512], "float32"), "pw1": ("psum", [128, 512], "float32"),
+}
+BANKS = ("px", "pc", "ps0", "ps1", "pr0", "pr1", "pw0", "pw1")
+SEMAPHORES = (["qg", "qv", "qa", "qp", "qs", "l_wk", "l_rec", "l_th", "l_tb", "l_b", "l_w", "st_b", "st_c"]
+              + ["au%d" % s for s in range(RO)] + ["ad%d" % s for s in range(RO)] + ["sent%d" % s for s in range(RO)])
+A = AluOpType
+F = ActivationFunctionType
+
+
+def depends(ops, soft=False):
+    writer, readers, touch, deps = {}, {}, {}, []
+    for i, op in enumerate(ops):
+        d = set(writer[r] for r in op["r"] if r in writer and (soft or r[0] != "~"))
+        for w in op["w"]:
+            if w[0] == "~":
+                continue
+            d.update(readers.get(w, []))
+            if w in writer:
+                d.add(writer[w])
+        for b in set(x.split(".")[0] for x in op["r"] + op["w"]):
+            if b in BANKS:
+                d.update(j for j in touch.setdefault(b, []) if ops[j]["q"] != op["q"])
+                touch[b] = [j for j in touch[b] if ops[j]["q"] == op["q"]] + [i]
+        for r in op["r"]:
+            readers.setdefault(r, []).append(i)
+        for w in op["w"]:
+            writer[w] = i
+            readers[w] = []
+        deps.append(d)
+    return deps
+
+
+def span(op, m):
+    kind, n = op["c"]
+    if kind == "D":
+        return m["iss"], n
+    if kind == "R":
+        return n, n
+    if kind == "L":
+        return 0.0, m["lat"]
+    if kind == "E":
+        t = max(64, n) * 0.83
+    elif kind == "P":
+        t = max(64, n) * m["pe"]
+    elif kind == "I":
+        t = 130 + n * 1.66
+    else:
+        t = (50 if op["q"] == "v" else 65) + n * 0.83 * m["ga" if kind == "G" else "sc"]
+    return t * m["f"], t * m["f"]
+
+
+def arrange(ops, m, seeds, amp):
+    n = len(ops)
+    deps = depends(ops)
+    order_only = [b - a for a, b in zip(deps, depends(ops, True))]
+    prev = {}
+    for i, op in enumerate(ops):
+        if op["q"] in "gs" and op["c"][0] != "L":
+            if op["q"] in prev:
+                order_only[i].add(prev[op["q"]])
+            prev[op["q"]] = i
+    sp = [span(op, m) for op in ops]
+    succ = [[] for _ in ops]
+    left = [0] * n
+    for i in range(n):
+        for j in deps[i] | order_only[i]:
+            succ[j].append(i)
+            left[i] += 1
+    tail = [0.0] * n
+    for i in range(n - 1, -1, -1):
+        tail[i] = max([sp[i][1]] + [(sp[i][1] + m["wake"] if i in deps[k] else sp[i][0]) + tail[k] for k in succ[i]])
+    x = {}
+    for i in range(n):
+        g = ops[i]["seg"]
+        x[g] = (x.get(g, seeds[g] * 7919 + 12345) * 1103515245 + 12345) % 2147483648
+        tail[i] += amp * x[g] / 2147483648.0
+    free, ready, at, out = {}, [i for i in range(n) if left[i] == 0], [0.0] * n, []
+    while ready:
+        st = {i: max(at[i], free.get(ops[i]["q"], 0.0)) if ops[i]["c"][0] != "L" else at[i] for i in ready}
+        i = min(ready, key=lambda k: (st[k] + sp[k][0], k))
+        if ops[i]["c"][0] != "L":
+            q, lim = ops[i]["q"], st[i] + sp[i][0]
+            i = max((k for k in ready if ops[k]["q"] == q and ops[k]["c"][0] != "L" and st[k] <= lim), key=lambda k: (tail[k], -k))
+            free[q] = st[i] + sp[i][0]
+        ready.remove(i)
+        out.append(i)
+        for k in succ[i]:
+            if i in deps[k]:
+                at[k] = max(at[k], st[i] + sp[i][1] + (0.0 if ops[i]["q"] == ops[k]["q"] == "p" else m["wake"]))
+            left[k] -= 1
+            if left[k] == 0:
+                ready.append(k)
+    return [ops[i] for i in out]
+
+
+def emit(g, T, ops):
+    ops = [ops[i] for i in CFG["order"]] if CFG.get("order") else arrange(ops, CFG["m"], CFG["seeds"], CFG["amp"])
+    deps = depends(ops)
+    queue = {"g": g, "v": g.vector, "a": g.scalar, "p": g.tensor, "s": g.sync}
+    clock, pos = {q: {} for q in queue}, {q: 0 for q in queue}
+    for i, op in enumerate(ops):
+        q = op["q"]
+        if op["ev"] is None:
+            pos[q] += 1
+            op["key"], op["pos"] = "q" + q, pos[q]
+        else:
+            op["key"], op["pos"] = op["ev"]
+        op["waits"] = []
+        if op["fn"] is not None or op["end"]:
+            for j in sorted(deps[i], reverse=True):
+                d = ops[j]
+                if q == "p" and d["q"] == "p":
+                    continue
+                if clock[q].get(d["key"], 0) >= d["pos"]:
+                    continue
+                op["waits"].append(j)
+                d["need"] = True
+                for k, v in d["clock"].items():
+                    clock[q][k] = max(clock[q].get(k, 0), v)
+        op["clock"] = dict(clock[q]) if op["fn"] is not None else {}
+        op["clock"][op["key"]] = op["pos"]
+    count = {}
+    for op in ops:
+        if op["ev"] is None and op.get("need"):
+            count[op["key"]] = count.get(op["key"], 0) + 1
+            op["val"] = count[op["key"]]
+        elif op["ev"] is not None:
+            op["val"] = op["pos"]
+    for op in ops:
+        e = queue[op["q"]]
+        for j in op["waits"]:
+            e.wait_ge(T.sem[ops[j]["key"]], ops[j]["val"])
+        if op["fn"] is None:
+            continue
+        ins = op["fn"](e)
+        if op["ev"] is None:
+            if op.get("need"):
+                ins.then_inc(T.sem[op["key"]], 1)
+        elif op["dma"]:
+            ins.then_inc(T.sem[op["key"]], 16)
+
+
+def neighbours(T, topo, rank):
+    n = len(T.cores)
+    src = T.cores[rank]
+    dst = [T.cores[(rank + 1) % n], T.cores[(rank - 1) % n]]
+    return dst, [e for e in topo.engines(src, dst[0]) if e in topo.engines(src, dst[1])]
+
+
+def rank_program(g, core, T, topo):
+    rank = T.rank_of(core)
+    if rank is None:
+        return
+    n = len(T.cores)
+    ops = []
+
+    seg = [0]
+    SM = ("E", 64)
+
+    def op(q, fn, r, w, c=SM, ev=None, dma=False, end=False):
+        ops.append({"q": q, "fn": fn, "r": list(r), "w": list(w), "c": c, "ev": ev, "dma": dma, "end": end, "seg": seg[0]})
+
+    def dma(q, out, in_, r, w, sem, t, val=16):
+        op(q, lambda e: e.dma_start(out, in_), r, w, ("D", t), ev=(sem, val), dma=True)
+
+    def ts(out, in0, s1, s2, op0, op1, r, w, c=SM):
+        if op1 is None:
+            op("v", lambda e: e.tensor_scalar(out, in0, s1, None, op0), r, w, c)
+        else:
+            op("v", lambda e: e.tensor_scalar(out, in0, s1, s2, op0, op1), r, w, c)
+
+    def tt(out, in0, in1, o, r, w, c=SM):
+        op("v", lambda e: e.tensor_tensor(out, in0, in1, o), r, w, c)
+
+    def cp(out, in_, r, w, c=SM):
+        op("v", lambda e: e.tensor_copy(out, in_), r, w, c)
+
+    def act(out, in_, f, r, w, c=SM, **kw):
+        op("a", lambda e: e.activation(out, in_, f, **kw), r, w, c)
+
+    def iota(out, pat, base, cm, w, flt=True):
+        cols = 1
+        for p in pat:
+            cols *= p[1]
+        if flt:
+            op("g", lambda e: e.iota(out, pat, base, cm, allow_small_or_imprecise_dtypes=True), [], w, ("I", cols))
+        else:
+            op("g", lambda e: e.iota(out, pat, base, cm), [], w, ("I", cols))
+
+    def mms(items, r, w, cycles):
+        def fn(e):
+            ins = None
+            for out, lhs, rhs, st, sp in items:
+                ins = e.matmul(out, lhs, rhs, st, sp)
+            return ins
+        op("p", fn, r, w, ("P", cycles))
+
+    def unwrap(out, src, cols, r, w):
+        mms([(out, T.sel[:, 15 - i:143 - i], src[:, i:16 * cols:16], i == 0, i == 15) for i in range(16)], r + ["sel"], w, 1024)
+
+    def two(t, a):
+        return t[:, K * (a % 2):K * (a % 2) + K]
+
+    op("v", lambda e: e.memset(T.tb[:], 0), [], ["tb0"], ("E", W))
+    dma("s", T.wki[:], T.wk[:], [], ["wki"], "l_wk", 2600)
+    dma("a", T.b16[:], T.b0[:], [], ["b16"], "l_b", 2700)
+    dma("s", T.r16[:], T.rec[:], [], ["r16"], "l_rec", 3500)
+    dma("a", T.thr[:, 0:1], T.th[:], [], ["thr"], "l_th", 3500)
+    dma("s", T.tb[0:128:4, :], T.hop[:], ["tb0"], ["tbh"], "l_tb", 2900, 48)
+    dma("s", T.tb[2:128:16, :], T.up[:], ["tb0"], ["tbu"], "l_tb", 2900, 48)
+    dma("s", T.tb[6:128:16, :], T.dn[:], ["tb0"], ["tbd"], "l_tb", 2900, 48)
+    dma("s", T.w16[:], T.w[:], [], ["w16"], "l_w", 3600)
+    iota(T.pi[:, 0:2], [[16, 2]], 0, 1, ["pi0"], flt=False)
+    iota(T.uu[:], [[1, 160]], 0, 0, ["uu"])
+    iota(T.u16[:], [[16, 8], [0, 16]], 0, 0, ["u16"])
+    iota(T.mk0[:], [[0, 16], [1, 3]], 0, 0, ["mk0"])
+    op("v", lambda e: e.memset(T.kz[:], -200.0), [], ["kz"], ("E", K))
+    act(T.ee[:, 5 * W:5 * W + 16], T.kz[:, 0:16], F.Sigmoid, ["kz"], ["eez", "warm"], ("R", 1400))
+    ts(T.pi[:, 2:3], T.pi[:, 0:1], 112, None, A.bitwise_and, None, ["pi0"], ["pi2"])
+    ts(T.pi[:, 3:4], T.pi[:, 0:1], 16, None, A.bitwise_and, None, ["pi0"], ["pi3"])
+    ts(T.pi[:, 4:5], T.pi[:, 1:2], 127, None, A.bitwise_and, None, ["pi0"], ["pi4"])
+    cp(T.pf[:, 0:5], T.pi[:, 0:5], ["pi0", "pi2", "pi3", "pi4"], ["pf"])
+    ts(T.pg[:, 0:1], T.pf[:, 3:4], 0.0625, None, A.mult, None, ["pf"], ["pg0"])
+    ts(T.pg[:, 1:2], T.pf[:, 3:4], -0.0625, 1.0, A.mult, A.add, ["pf"], ["pg1"])
+    ts(T.pg[:, 2:3], T.pf[:, 2:3], 15.0, None, A.add, None, ["pf"], ["pg2"])
+    ts(T.bd[:], T.u16[:], T.pf[:, 2:3], None, A.is_equal, None, ["u16", "pf"], ["bd"], ("E", 128))
+    ts(T.e0[:], T.uu[:], T.pf[:, 1:2], T.pg[:, 1:2], A.is_equal, A.mult, ["uu", "pf", "pg1"], ["e0"], ("E", 160))
+    ts(T.e1[:], T.uu[:], T.pf[:, 1:2], T.pg[:, 0:1], A.is_equal, A.mult, ["uu", "pf", "pg0"], ["e1"], ("E", 160))
+    iota(T.k01[:], [[200, 2], [0, K]], 0, 0, ["k01"])
+    iota(T.cc[:], [[0, W]], 0, 0, ["cc"])
+    cp(T.du[:, 0:16], T.wki[:], ["wki"], ["du0"])
+    cp(T.dp[:, 0:16:2], T.wki[:, 0:8], ["wki"], ["dp0"])
+    cp(T.dp[:, 1:16:2], T.wki[:, 8:16], ["wki"], ["dp1"])
+    cp(T.bb[:], T.b16[:], ["b16"], ["bb"], ("E", W))
+    ts(T.idn[:], T.uu[:, 0:128], T.pf[:, 0:1], None, A.is_equal, None, ["uu", "pf"], ["idn"], ("E", 128))
+    if CFG["dense"]:
+        for j in range(4):
+            c0, c1 = K * j, K * (j % 2)
+            act(T["pr%d" % (j // 2)][:, c1:c1 + K], T.r16[:, c0:c0 + K], F.Copy, ["r16", "warm"], ["pr%d.%d" % (j // 2, j)], ("E", K), scale=-1.0)
+            act(T["pw%d" % (j // 2)][:, c1:c1 + K], T.w16[:, c0:c0 + K], F.Copy, ["w16", "warm"], ["pw%d.%d" % (j // 2, j)], ("E", K))
+    ts(T.sh[:], T.uu[:, 0:128], T.pf[:, 4:5], None, A.is_equal, None, ["uu", "pf"], ["sh"], ("E", 128))
+    ts(T.sel[:], T.uu[:], T.pg[:, 2:3], 4096.0, A.is_equal, A.mult, ["uu", "pg2"], ["sel"], ("E", 160))
+    ts(T.mk[:], T.mk0[:], 1.0, None, A.min, None, ["mk0"], ["mk"])
+    ts(T.df[:, 0:16], T.wki[:], 2048.0, None, A.add, None, ["wki"], ["df0"])
+    ts(T.nth[:, 0:1], T.thr[:, 0:1], -1.0, None, A.mult, None, ["thr"], ["nth"])
+
+    dst, eng = neighbours(T, topo, rank)
+    n_up = len(neighbours(T, topo, (rank - 1) % n)[1])
+    n_dn = len(neighbours(T, topo, (rank + 1) % n)[1])
+    mode, nh, src, dln = CFG["mode"], CFG["half"], CFG["src"], "dl"
+
+    for s in range(RO):
+        last = s == RO - 1
+        seg[0] = 2 * s
+        du, dun = T.du[:, 16 * s:16 * s + 16], "du%d" % s
+        hb0 = HW * s
+        h, hn = T.hb[:, hb0 + 16:hb0 + 16 + K], "h%d" % s
+        lu, ld = T.lu[:, PW * s:PW * s + PW], T.ld[:, PW * s:PW * s + PW]
+
+        def xl(a, i=0, parts=1):
+            c = 16 // parts
+            return T.xu[:, 16 * a + c * i:16 * a + c * i + c]
+
+        def xlist(a):
+            if a < NK:
+                cp(xl(a), T.px[:, 2 * a:256:16], ["px.a"], ["x%d" % a])
+            elif a == NK:
+                cp(xl(a), T.pc[:, K:PW], ["pc.l"], ["x4"])
+            else:
+                cp(xl(a), ld[:, K:PW], ["ld%d" % s], ["x5"])
+
+        def tables():
+            cp(T.xg[:], T.tb[:].indirect(T.dp[:]), ["tb0", "tbh", "tbu", "tbd", "dp0", "dp1"], ["xg"], ("G", K))
+            op("v", lambda e: e.transpose(T.yy[:], T.xg[:]), ["xg"], ["yy"], ("E", 128))
+            mms([(T.px[:, 0:120], T.e0[:, 16:144], T.yy[:, 0:240:2], True, False),
+                 (T.px[:, 0:120], T.e0[:, 0:128], T.yy[:, 16:256:2], False, True),
+                 (T.px[:, 128:248], T.e1[:, 32:160], T.yy[:, 0:240:2], True, False),
+                 (T.px[:, 128:248], T.e1[:, 16:144], T.yy[:, 16:256:2], False, True)], ["yy", "e0", "e1"], ["px.a"], 480)
+
+        tables()
+        if s > 0 and CFG["dense"]:
+            if CFG["dense"] == 2:
+                act(h, T.hw[:].indirect(du), F.Copy, ["hw%d" % j for j in range(4)] + [dun], [hn, "~cg"], ("G", K))
+            else:
+                cp(h, T.hw[:].indirect(du), ["hw%d" % j for j in range(4)] + [dun], [hn], ("G", K))
+            act(T.bb[:].indirect(du), T.kz[:], F.Sigmoid, ["kz", dun, "~cg"], ["bb", "~z"], ("S", K))
+            act(T.dl[:], T.br[:].indirect(du), F.Copy, ["br%d" % j for j in range(4)] + [dun, "~z"], ["dl"], ("G", K))
+            act(T.cg[:], T.cc[:].indirect(du), F.Copy, ["cc", dun, "~z"], ["cg"], ("G", K))
+        else:
+            act(T.nr[:], T.r16[:].indirect(du), F.Copy, ["r16", dun, "warm"], ["nr", "~nr"], ("G", K), scale=-1.0)
+            if s > 0:
+                act(T.cg[:], T.cc[:].indirect(du), F.Copy, ["cc", dun, "~nr"], ["cg", "~cg"], ("G", K))
+            bw, bn = (T.b16, "b16") if s == 0 else (T.bb, "bb")
+            tt(T.dl[:], bw[:].indirect(du), T.nr[:], A.mult, [bn, dun, "nr"], ["dl"], ("G", K))
+            tt(h, T.w16[:].indirect(du), T.dl[:], A.mult, ["w16", dun, "dl"], [hn], ("G", K))
+            act(T.bb[:].indirect(du), T.kz[:], F.Sigmoid, ["kz", dun, "~cg"], ["bb"], ("S", K))
+        if s == 0 or not CFG["spec"]:
+            xlist(0)
+        cp(T.hb[:, hb0:hb0 + 16], T.px[:, 1:256:16], ["px.a"], [hn + "u"])
+        cp(T.hb[:, hb0 + 16 + K:hb0 + HW], T.px[:, 3:256:16], ["px.a"], [hn + "d"])
+        xlist(1)
+
+        def send(i, land, from_, sem, s=s):
+            rid, pid = topo.addr(dst[i], core)
+            return lambda e: e.remote_dma(land, from_, T.sem[sem], T.sem["sent%d" % s], pid, rid, sum(1 << x for x in eng))
+        op("g", send(0, lu, T.hb[:, hb0:hb0 + PW], "au%d" % s), [hn, hn + "u"], ["su%d" % s], ("R", 3000 if s == 0 else 1000), ev=("sent%d" % s, len(eng)))
+        op("g", send(1, ld, T.hb[:, hb0 + 16:hb0 + HW], "ad%d" % s), [hn, hn + "d"], ["sd%d" % s], ("R", 1000), ev=("sent%d" % s, 2 * len(eng)))
+        op("g", None, ["su%d" % s], ["lu%d" % s], ("L", 0), ev=("au%d" % s, n_up))
+        op("g", None, ["sd%d" % s], ["ld%d" % s], ("L", 0), ev=("ad%d" % s, n_dn))
+        if s == 0:
+            for m in (4, 3, 2, 1, 0):
+                iota(T.ee[:, m * W:(m + 1) * W], [[0, W]], 0, 0, ["ee%d" % m])
+
+        def gv(a):
+            return T.gg[:, K * (a % 2):K * (a % 2) + K]
+
+        def part(t, i, parts):
+            return t[:, (K // parts) * i:(K // parts) * (i + 1)]
+
+        def p1(a):
+            if src[a] == "g":
+                tt(gv(a), T.w16[:].indirect(xl(a)), h if a < NK else ld[:, 0:K], A.mult, ["w16", "x%d" % a, hn if a < NK else "ld%d" % s],
+                   ["g%d" % (a % 2)], ("G", K))
+            else:
+                act(two(T.wx, a), T.w16[:].indirect(xl(a)), F.Copy, ["w16", "x%d" % a], ["wx%d" % (a % 2)], ("G", K))
+                tt(gv(a), two(T.wx, a), T.px[:, K:2 * K], A.mult, ["wx%d" % (a % 2), "px.u"], ["g%d" % (a % 2)], ("E", K))
+
+        def p2(a):
+            act(two(T.ab, a), gv(a), F.Abs, ["g%d" % (a % 2)], ["ab%d" % (a % 2)], ("E", K))
+
+        def p3(a):
+            ab, ov, rl = "ab%d" % (a % 2), "ov%d" % (a % 2), "rl%d" % (a % 2)
+            if mode[a] == "A":
+                ts(two(T.ov, a), two(T.ab, a), T.thr[:, 0:1], None, A.is_gt, None, [ab, "thr"], [ov], ("E", K))
+            elif mode[a] == "0":
+                ts(two(T.ov, a), two(T.ab, a), T.thr[:, 0:1], 0.0625, A.is_gt, A.mult, [ab, "thr"], [ov], ("E", K))
+            else:
+                act(two(T.rl, a), two(T.ab, a), F.Relu, [ab, "nth"], [rl], ("E", K), bias=T.nth[:, 0:1])
+                if mode[a] == "C":
+                    act(two(T.ov, a), two(T.rl, a), F.Sign, [rl], [ov], ("E", K))
+                else:
+                    ts(two(T.ov, a), two(T.rl, a), 0.0, None, A.is_gt, None, [rl], [ov], ("E", K // 2))
+
+        def p4(a):
+            mms([(T.pc[:, 0:K], T.bd[:], two(T.ov, a), True, True)], ["bd", "ov%d" % (a % 2)], ["pc.c"], K)
+
+        def p5(a):
+            act(T.mn[:], T.pc[:, 0:K], F.Relu, ["pc.c"], ["mn"], ("E", K), bias=-8.0)
+            for i in range(nh):
+                mms([(T["ps%d" % i][:, 0:K // nh], T.idn[:], part(T.mn, i, nh), True, False)], ["idn", "mn"], ["ps%d" % i], K // nh)
+
+        def c1(a, i):
+            act(part(T.nz, i, nh), T.bb[:].indirect(xl(a, i, nh)), F.Abs, ["bb", "x%d" % a], ["nz%d" % i], ("G", K // nh))
+            mms([(T["ps%d" % i][:, 0:K // nh], T.bd[:], part(T.nz, i, nh), False, True)], ["bd", "nz%d" % i], ["ps%d" % i], K // nh)
+
+        def sm(a):
+            tt(T.ss[:], T.bb[:].indirect(xl(a)), gv(a), A.add, ["bb", "x%d" % a, "g%d" % (a % 2)], ["ss"], ("G", K))
+
+        def c3(a, i):
+            act(part(T.ac, i, nh), T["ps%d" % i][:, 0:K // nh], F.Sign, ["ps%d" % i], ["ac%d" % i], ("E", K // nh))
+
+        def c4(a, i, parts):
+            tt(T.bb[:].indirect(xl(a, i, parts)), part(T.ss, i, parts), part(T.ac, i, parts), A.mult,
+               ["ss", "x%d" % a] + (["ac%d" % i] if parts == nh else ["ac%d" % j for j in range(nh)]), ["bb"], ("S", K // parts))
+
+        def cscat(i=0, parts=1):
+            c = 16 // parts
+            lst = T.du[:, 16 * s + c * i:16 * s + c * i + c]
+            if s == 0:
+                cp(T.cc[:].indirect(lst), part(T.dl, i, parts), [dln, dun, "~eu"], ["cc"], ("S", K // parts))
+            else:
+                tt(T.cc[:].indirect(lst), part(T.cg, i, parts), part(T.dl, i, parts), A.add, ["cg", dln, dun, "~eu"], ["cc"], ("S", K // parts))
+
+        if last:
+            for i in range(4):
+                cscat(i, 4)
+            dma("s", T.yc[:], T.cc[:], ["cc"], ["yc"], "st_c", 3500)
+        xlist(2); xlist(3)
+        if not last:
+            for k in range(NK):
+                ts(T.ck[:, 16 * k:16 * k + 16], T.px[:, 2 * k:256:16], float((NK - 1 - k) * W), None, A.add, None, ["px.a"], ["ck%d" % k])
+        xlist(5)
+
+        p1(0)
+        if CFG["pm"]:
+            ts(T.ov[:, 0:K], gv(0), T.thr[:, 0:1], 0.0625, A.is_gt, A.mult, ["g0", "thr"], ["ov0"], ("E", K))
+            ts(T.ov[:, K:2 * K], gv(0), T.nth[:, 0:1], 0.0625, A.is_lt, A.mult, ["g0", "nth"], ["ov1"], ("E", K))
+        else:
+            p2(0); p3(0)
+        nzs = ["nz%d" % i for i in range(nh)]
+        act(T.nz[:], T.bb[:].indirect(xl(0)), F.Abs, ["bb", "x0"], nzs, ("G", K))
+        act(T.n1[:], T.nz[:], F.Sign, nzs, ["n1"], ("E", K))
+        sm(0)
+        p0 = T.ps1[:, K:2 * K]
+        mms([(p0, T.bd[:], T.ov[:, 0:K], True, False)], ["bd", "ov0"], ["ps1.v"], K)
+        if CFG["pm"]:
+            mms([(p0, T.bd[:], T.ov[:, K:2 * K], False, False)], ["bd", "ov1"], ["ps1.v"], K)
+        mms([(p0, T.bd[:], T.n1[:], False, True)], ["bd", "n1"], ["ps1.v", "ps1"], K)
+        ts(T.ac[:], p0, 0.53125, None, A.is_gt, None, ["ps1.v"], ["ac%d" % i for i in range(nh)], ("E", K))
+        c4(0, 0, 1)
+        for a in range(1, 6):
+            if a == NK:
+                mms([(T.pc[:, K:PW], T.sh[:], lu[:, 0:16], True, True)], ["sh", "lu%d" % s], ["pc.l"], 256)
+                mms([(T.px[:, K:2 * K], T.sh[:], lu[:, 16:PW], True, True)], ["sh", "lu%d" % s], ["px.u"], 4 * K)
+                xlist(4)
+            p1(a); p2(a); p3(a); p4(a); p5(a)
+            for i in range(nh):
+                c1(a, i)
+            sm(a)
+            for i in range(nh):
+                c3(a, i)
+            for i in range(nh):
+                c4(a, i, nh)
+        if last:
+            break
+
+        seg[0] = 2 * s + 1
+        n4 = CFG["p4"]
+        c4w = K // n4
+        for i in range(n4):
+            for k in range(NK):
+                av = T.aa[:, K * k + c4w * i:K * k + c4w * (i + 1)]
+                if k < NK - CFG["raw"]:
+                    act(av, T.bb[:].indirect(xl(k, i, n4)), F.Abs, ["bb", "x%d" % k, "~a"], ["a%d%d" % (k, i), "~a"], ("G", c4w))
+                else:
+                    rw = T.rw[:, K * (k % 2) + c4w * i:K * (k % 2) + c4w * (i + 1)]
+                    cp(rw, T.bb[:].indirect(xl(k, i, n4)), ["bb", "x%d" % k], ["rw%d%d" % (k, i)], ("G", c4w))
+                    act(av, rw, F.Abs, ["rw%d%d" % (k, i)], ["a%d%d" % (k, i)], ("E", c4w))
+        if CFG["dense"]:
+            for j in range(4):
+                c0, c1_ = K * j, K * (j % 2)
+                tt(T.br[:, c0:c0 + K], T.bb[:, c0:c0 + K], T["pr%d" % (j // 2)][:, c1_:c1_ + K], A.mult, ["bb", "pr%d.%d" % (j // 2, j)], ["br%d" % j], ("E", K))
+                tt(T.hw[:, c0:c0 + K], T.br[:, c0:c0 + K], T["pw%d" % (j // 2)][:, c1_:c1_ + K], A.mult, ["br%d" % j, "pw%d.%d" % (j // 2, j)], ["hw%d" % j], ("E", K))
+        kin = T.k01[:, K * s:K * s + K]
+        for m in (4, 3):
+            act(T.ee[:, m * W:(m + 1) * W].indirect(du), kin, F.Sigmoid, ["k01", dun] + (["~a"] if m == 3 or CFG["pin"] else []), ["ee%d" % m], ("S", K))
+        for i in range(n4):
+            av = [T.aa[:, K * k + c4w * i:K * k + c4w * (i + 1)] for k in range(NK)]
+            an = ["a%d%d" % (k, i) for k in range(NK)]
+            pm, pn = T.ps0[:, K + c4w * i:K + c4w * (i + 1)], "ps0.%d" % i
+            tt(pm, av[0], av[1], A.max, an[0:2], [pn], ("E", 2 * c4w))
+            tt(pm, av[2], pm, A.max, [an[2], pn], [pn], ("E", c4w))
+            tt(pm, av[3], pm, A.max, [an[3], pn], [pn], ("E", c4w))
+            for k in range(NK):
+                tt(T.eq[:, K * k + c4w * i:K * k + c4w * (i + 1)], av[k], pm, A.is_equal, [an[k], pn], ["eq%d%d" % (k, i)], ("E", c4w))
+        unwrap(T.ps1[:, K:K + 64], T.eq, 64, ["eq%d%d" % (k, i) for k in range(NK) for i in range(n4)], ["ps1.v"])
+        tt(T.ky[:], T.ck[:], T.ps1[:, K:K + 64], A.add, ["ck%d" % k for k in range(NK)] + ["ps1.v"], ["ky"])
+        tt(T.k2[:], T.ky[:, 0:32], T.ky[:, 32:64], A.max, ["ky"], ["k2"])
+        tt(T.ki[:, 0:16], T.k2[:, 0:16], T.k2[:, 16:32], A.max, ["k2"], ["ki0"])
+        ts(T.ki[:, 16:32], T.ki[:, 0:16], NK * W - 1, None, A.bitwise_and, None, ["ki0"], ["ki1"])
+        ts(T.ki[:, 32:48], T.ki[:, 0:16], W - 1, None, A.bitwise_and, None, ["ki0"], ["ki2"])
+        cp(T.eu[:], T.ki[:, 16:32], ["ki1"], ["eu", "~eu"])
+        for i in range(CFG["cs"]):
+            cscat(i, CFG["cs"])
+        ee03, ee14 = ["ee0", "ee1", "ee2", "ee3"], ["ee1", "ee2", "ee3", "ee4", "eez"]
+        act(T.ee[:, 0:4 * W].indirect(T.eu[:]), kin, F.Sigmoid, ["k01", "eu"], ee03, ("S", K))
+        for m in range(3):
+            ts(T.gl[:, m:48:3], T.ki[:, 16:32], float(m * W), float(ZC), A.add, A.min, ["ki1"], ["gl%d" % m])
+        ts(T.xf[:], T.ki[:, 32:48], 2048.0, None, A.add, None, ["ki2"], ["xf"])
+        if CFG["spec"]:
+            cp(T.dp[:, 0:16:2], T.ki[:, 32:40], ["ki2"], ["dp0"])
+            cp(T.dp[:, 1:16:2], T.ki[:, 40:48], ["ki2"], ["dp1"])
+            tables()
+            ts(T.wf[:], T.px[:, 0:256:16], float(3 * W), None, A.add, None, ["px.a"], ["wf"])
+        win, lev, gls = T.ee[:, W:5 * W + 16], 0.25 + 0.5 * s, ["gl0", "gl1", "gl2"]
+        act(T.gt[:, 0:384], win.indirect(T.gl[:, 0:24]), F.Relu, ee14 + gls, ["gt0"], ("G", 384), bias=-lev)
+        ts(T.gt[:, 384:768], win.indirect(T.gl[:, 24:48]), lev, None, A.is_gt, None, ee14 + gls, ["gt1"], ("G", 384))
+        unwrap(T.ps1[:, K:K + 48], T.gt, 48, ["gt0", "gt1"], ["ps1.v"])
+        op("v", lambda e: e.tensor_tensor_scan(T.sc[:], T.mk[:], T.ps1[:, K:K + 48], 0.0, A.mult, A.add), ["mk", "ps1.v"], ["sc"])
+        if CFG["spec"]:
+            tt(T.u2[:, 0:16], T.wf[:], T.sc[:, 2:48:3], A.subtract, ["wf", "sc"], ["u2"])
+            tt(T.u2[:, 16:32], T.ck[:, 0:16], T.sc[:, 2:48:3], A.min, ["ck0", "sc"], ["v2"])
+            tt(T.u2[:, 32:48], T.u2[:, 0:16], T.u2[:, 16:32], A.max, ["u2", "v2"], ["m2"])
+            ts(xl(0), T.u2[:, 32:48], float(-3 * W), None, A.add, None, ["m2"], ["x0"])
+        df, dfn = T.df[:, 16 * s:16 * s + 16], T.df[:, 16 * s + 16:16 * s + 32]
+        tt(T.uv[:, 0:16], T.xf[:], T.sc[:, 2:48:3], A.subtract, ["xf", "sc"], ["u"])
+        tt(T.uv[:, 16:32], df, T.sc[:, 2:48:3], A.min, ["df%d" % s, "sc"], ["v"])
+        tt(dfn, T.uv[:, 0:16], T.uv[:, 16:32], A.max, ["u", "v"], ["df%d" % (s + 1)])
+        ts(T.du[:, 16 * s + 16:16 * s + 32], dfn, -2048.0, None, A.add, None, ["df%d" % (s + 1)], ["du%d" % (s + 1)])
+        ts(T.dp[:, 0:16:2], T.df[:, 16 * s + 16:16 * s + 24], -2048.0, None, A.add, None, ["df%d" % (s + 1)], ["dp0"])
+        ts(T.dp[:, 1:16:2], T.df[:, 16 * s + 24:16 * s + 32], -2048.0, None, A.add, None, ["df%d" % (s + 1)], ["dp1"])
+
+    dma("s", T.yb[:], T.bb[:], ["bb"], ["yb"], "st_b", 3500)
+    op("s", None, ["yb", "yc"], [], ("R", 0), end=True)
+    op("g", None, ["sd%d" % s for s in range(RO)], [], ("R", 0), end=True)
+    emit(g, T, ops)

@@ -5,54 +5,56 @@ W, K, NK, RO = 1024, 256, 4, 3
 PW = K + 16
 HW = K + 32
 ZC = 4 * W
-ORDER = (
-    "0102090004030a0b0h0c0g050f0d060p07080i0y0e0k0v0j0w0m0n0o0q0r0s0t0z0u140l1017111512161318191b1v1s1c221t1w1u231x1y1z2420251l21262728291e1a2j2a1d2c2b2e2k2d2f1m2l1g2h1f2g2m2n2i2o302q2p2r2t2v2s312u1n2w1h1q1o322y332x1p342z353h3i383j0x3k3c36391i373a3l3d1r3b3m3f3e3n3g3o3p413s1j3q3r3u3w3t423v3x433z3y444540461k4748494d4b4a4e4c4g4f4h4i4j4k4s4l4t4m4u4n4v4o4z4p4y504r4x514w525455534q565758595a5c5h5f5e5g5d5k5j5b5l5i5m5o5n5p5q5r5s5w5t5x5y5u605z5v6162646g656q6j6l6h676k6i6r69636m776s666n6t6o786u6p79686v7a6x6w6a7b6y72706z737o717c757d7p747q7e767r6c7s6e7f6b6d7j7h7g7k7i7t7m7l8586877n887u807w7y7x7v89817z6f838a828b848c8d8p8g8e8f8i8k8h8q8j8l8r8n8m8s8t8o8u8v8w8x918z8y92909493959697989g999h9a9i9b9j9c9n9d9l9o9f9k9p9m9r9t9s9q9e9u9v9w9x9ya0a3a4a2a5a1a7a89za9a6aaabacadaeafagakahalamaiaoanajaqaparatb2asb5b8bfaub6baavb9bgb7bwbhbbbcawdxbibdbxbjbebybkbzbmblb3c0bnbrbpbobscdbqc1buc2cebtcfc3bvcgaxchc4c8c6c5c9c7cicbcacucvcwcccxcjckb4clcpcncmcycqcodeczcrcsdfdgd0ctd1d2ayd5d3d4d9d7d6dad8dhdcdbdidjdddkdlazdmdqdodndrb0dpdsdtb1dudvdw")
-CFG = {"order": [int(ORDER[i:i + 2], 36) for i in range(0, len(ORDER), 2)],
-       "mode": "0CCCAC", "src": "ggggwg", "half": 2, "p4": 2, "dense": 0, "spec": 0, "raw": 0, "pm": 0, "pin": 1, "cs": 1, "seeds": (0, 0, 0, 0, 0), "amp": 0.0,
-       "m": {"sc": 3.8, "ga": 1.56, "f": 1.25, "pe": 0.42, "wake": 120.0, "iss": 100.0, "lat": 4500.0}}
+BIG, TINY = 2.0 ** 99, 2.0 ** -30
+N4 = 4
+NB = 3
+PLAN = ["Z0 g0 g1 L3 B0 B1 R1 L2 O0 S0 Q0 W2 o1 V0 W3 C1 M1 G2 B2 X1 U0 R2",
+        "N1 n1 A1 G3 S1 o2 P1 C2 L4 B3 H4 a1 M2 R3 X2 p1 W4",
+        "o3 N2 n2 G4 S2 C3 A2 L5 B4 P2 H5 a2 M3 X3 W5 R4 p2",
+        "G5 N3 S3 n3 A3 a3 o4 B5 C4 M4 P3 p3 X4",
+        "S4 R5 N4 n4 o5 A4 P4 a4 C5 M5 p4 X5 E0",
+        "E1 N5 S5 n5 E2 A5 P5 a5 p5"]
+CFG = {"cut": 4, "fused": 1, "vb": 384, "cl": ((0, 4), (4, 16)), "plan": [PLAN] * RO}
 
 SCRATCH = {
     "b16": ("sbuf", [128, W], "bfloat16"), "w16": ("sbuf", [128, W], "bfloat16"), "r16": ("sbuf", [128, W], "bfloat16"),
     "thr": ("sbuf", [128, 4], "float32"), "nth": ("sbuf", [128, 4], "float32"), "tb": ("sbuf", [128, W], "int32"), "wki": ("sbuf", [128, 16], "int32"),
     "bb": ("sbuf", [128, W], "float32"), "cc": ("sbuf", [128, W], "float32"), "ee": ("sbuf", [128, 5 * W + 16], "float32"),
-    "kz": ("sbuf", [128, K], "float32"), "k01": ("sbuf", [128, 2 * K], "float32"),
-    "uu": ("sbuf", [128, 160], "float32"), "u16": ("sbuf", [128, 128], "float32"), "pi": ("sbuf", [128, 8], "int32"),
-    "pf": ("sbuf", [128, 8], "float32"), "pg": ("sbuf", [128, 8], "float32"), "mk0": ("sbuf", [128, 48], "float32"), "mk": ("sbuf", [128, 48], "float32"),
-    "sel": ("sbuf", [128, 160], "bfloat16"), "bd": ("sbuf", [128, 128], "bfloat16"), "idn": ("sbuf", [128, 128], "bfloat16"),
-    "e0": ("sbuf", [128, 160], "float16"), "e1": ("sbuf", [128, 160], "float16"), "sh": ("sbuf", [128, 128], "float32"),
-    "du": ("sbuf", [128, 16 * RO], "uint16"), "dp": ("sbuf", [128, 16], "uint16"), "df": ("sbuf", [128, 16 * RO], "float32"),
-    "xg": ("sbuf", [128, K], "float16"), "yy": ("sbuf", [128, K], "float16"), "xu": ("sbuf", [128, 96], "uint16"),
-    "nr": ("sbuf", [128, K], "float32"), "dl": ("sbuf", [128, K], "float32"),
+    "kw": ("sbuf", [128, 16], "float32"), "kz": ("sbuf", [128, K], "float32"), "k01": ("sbuf", [128, 2 * K], "float32"),
+    "uu": ("sbuf", [128, 160], "bfloat16"), "u16": ("sbuf", [128, 128], "bfloat16"), "u4": ("sbuf", [128, 144], "bfloat16"), "pi": ("sbuf", [128, 8], "int32"),
+    "pf": ("sbuf", [128, 8], "float32"), "pg": ("sbuf", [128, 8], "float32"), "mq": ("sbuf", [128, 4], "float32"),
+    "mk0": ("sbuf", [128, 64], "float32"), "mk": ("sbuf", [128, 64], "float32"), "pat": ("sbuf", [128, 64], "bfloat16"), "kc": ("sbuf", [128, 64], "bfloat16"),
+    "sel": ("sbuf", [128, 160], "bfloat16"), "sl2": ("sbuf", [128, 160], "bfloat16"), "bd": ("sbuf", [128, 128], "bfloat16"), "idn": ("sbuf", [128, 128], "bfloat16"),
+    "cz": ("sbuf", [128, 144], "bfloat16"), "ex": ("sbuf", [128, 512], "bfloat16"),
+    "e0": ("sbuf", [128, 160], "float16"), "e1": ("sbuf", [128, 160], "float16"), "sh": ("sbuf", [128, 128], "float32"), "idf": ("sbuf", [128, 128], "float32"),
+    "du": ("sbuf", [128, 16 * RO], "uint16"), "df": ("sbuf", [128, 16], "float32"),
+    "xg": ("sbuf", [128, K], "float16"), "yy": ("sbuf", [128, 8, 32], "float16"), "xu": ("sbuf", [128, 96], "uint16"), "xm": ("sbuf", [128, N4, 64 // N4], "uint16"),
+    "bo": ("sbuf", [128, K], "float32"), "dl": ("sbuf", [128, K], "float32"),
     "hb": ("sbuf", [128, RO * HW], "float32"), "lu": ("sbuf", [128, RO * PW], "float32"), "ld": ("sbuf", [128, RO * PW], "float32"),
-    "gg": ("sbuf", [128, 2 * K], "float32"), "ab": ("sbuf", [128, 2 * K], "float32"), "rl": ("sbuf", [128, 2 * K], "bfloat16"),
-    "ov": ("sbuf", [128, 2 * K], "bfloat16"), "idf": ("sbuf", [128, 128], "float32"), "br": ("sbuf", [128, W], "float32"),
-    "hw": ("sbuf", [128, W], "float32"), "wf": ("sbuf", [128, 16], "float32"), "u2": ("sbuf", [128, 48], "float32"), "rw": ("sbuf", [128, 2 * K], "float32"),
-    "mn": ("sbuf", [128, K], "bfloat16"), "nz": ("sbuf", [128, K], "bfloat16"), "n1": ("sbuf", [128, K], "bfloat16"), "ss": ("sbuf", [128, K], "float32"),
-    "ac": ("sbuf", [128, K], "float32"), "wx": ("sbuf", [128, 2 * K], "float32"), "cg": ("sbuf", [128, K], "float32"),
-    "aa": ("sbuf", [128, NK * K], "float32"), "eq": ("sbuf", [128, NK * K], "bfloat16"),
-    "ck": ("sbuf", [128, 64], "float32"), "ky": ("sbuf", [128, 64], "float32"), "k2": ("sbuf", [128, 32], "float32"),
-    "ki": ("sbuf", [128, 48], "int32"), "eu": ("sbuf", [128, 16], "uint16"), "gl": ("sbuf", [128, 48], "uint16"),
-    "xf": ("sbuf", [128, 16], "float32"), "gt": ("sbuf", [128, 3 * K], "bfloat16"), "sc": ("sbuf", [128, 48], "float32"),
-    "uv": ("sbuf", [128, 32], "float32"),
-    "px": ("psum", [128, 512], "float32"), "pc": ("psum", [128, 512], "float32"),
+    "gg": ("sbuf", [128, NB * K], "float32"), "ab": ("sbuf", [128, NB * K], "float32"), "rl": ("sbuf", [128, NB * K], "bfloat16"),
+    "ov": ("sbuf", [128, NB * K], "bfloat16"), "wx": ("sbuf", [128, NB * K], "float32"),
+    "mn": ("sbuf", [128, 64], "bfloat16"), "nz": ("sbuf", [128, K], "bfloat16"), "ss": ("sbuf", [128, K], "float32"),
+    "ac": ("sbuf", [128, K], "float32"), "cg": ("sbuf", [128, K], "float32"),
+    "aa": ("sbuf", [128, N4, NK * K // N4], "float32"), "eq": ("sbuf", [128, K, NK], "bfloat16"), "ck": ("sbuf", [128, 64], "float32"),
+    "ky": ("sbuf", [128, 64], "int32"), "ki": ("sbuf", [128, 32], "int32"), "eu": ("sbuf", [128, 16], "uint16"), "gl": ("sbuf", [128, 48], "uint16"),
+    "gt": ("sbuf", [128, K, 4], "bfloat16"), "d1": ("sbuf", [128, 64], "float32"), "sc": ("sbuf", [128, 64], "float32"),
+    "px": ("psum", [128, 32, 16], "float32"), "pc": ("psum", [128, 512], "float32"),
     "ps0": ("psum", [128, 512], "float32"), "ps1": ("psum", [128, 512], "float32"),
-    "pr0": ("psum", [128, 512], "float32"), "pr1": ("psum", [128, 512], "float32"),
-    "pw0": ("psum", [128, 512], "float32"), "pw1": ("psum", [128, 512], "float32"),
+    "ph": ("psum", [128, 512], "float32"), "pu": ("psum", [128, 32, 16], "float32"),
+    "pd": ("psum", [128, 512], "float32"), "pk": ("psum", [128, 512], "float32"),
 }
-BANKS = ("px", "pc", "ps0", "ps1", "pr0", "pr1", "pw0", "pw1")
+BANKS = ("px", "pc", "ps0", "ps1", "ph", "pu", "pd", "pk")
 SEMAPHORES = (["qg", "qv", "qa", "qp", "qs", "l_wk", "l_rec", "l_th", "l_tb", "l_b", "l_w", "st_b", "st_c"]
               + ["au%d" % s for s in range(RO)] + ["ad%d" % s for s in range(RO)] + ["sent%d" % s for s in range(RO)])
 A = AluOpType
 F = ActivationFunctionType
 
 
-def depends(ops, soft=False):
+def depends(ops):
     writer, readers, touch, deps = {}, {}, {}, []
     for i, op in enumerate(ops):
-        d = set(writer[r] for r in op["r"] if r in writer and (soft or r[0] != "~"))
+        d = set(writer[r] for r in op["r"] if r in writer)
         for w in op["w"]:
-            if w[0] == "~":
-                continue
             d.update(readers.get(w, []))
             if w in writer:
                 d.add(writer[w])
@@ -69,71 +71,7 @@ def depends(ops, soft=False):
     return deps
 
 
-def span(op, m):
-    kind, n = op["c"]
-    if kind == "D":
-        return m["iss"], n
-    if kind == "R":
-        return n, n
-    if kind == "L":
-        return 0.0, m["lat"]
-    if kind == "E":
-        t = max(64, n) * 0.83
-    elif kind == "P":
-        t = max(64, n) * m["pe"]
-    elif kind == "I":
-        t = 130 + n * 1.66
-    else:
-        t = (50 if op["q"] == "v" else 65) + n * 0.83 * m["ga" if kind == "G" else "sc"]
-    return t * m["f"], t * m["f"]
-
-
-def arrange(ops, m, seeds, amp):
-    n = len(ops)
-    deps = depends(ops)
-    order_only = [b - a for a, b in zip(deps, depends(ops, True))]
-    prev = {}
-    for i, op in enumerate(ops):
-        if op["q"] in "gs" and op["c"][0] != "L":
-            if op["q"] in prev:
-                order_only[i].add(prev[op["q"]])
-            prev[op["q"]] = i
-    sp = [span(op, m) for op in ops]
-    succ = [[] for _ in ops]
-    left = [0] * n
-    for i in range(n):
-        for j in deps[i] | order_only[i]:
-            succ[j].append(i)
-            left[i] += 1
-    tail = [0.0] * n
-    for i in range(n - 1, -1, -1):
-        tail[i] = max([sp[i][1]] + [(sp[i][1] + m["wake"] if i in deps[k] else sp[i][0]) + tail[k] for k in succ[i]])
-    x = {}
-    for i in range(n):
-        g = ops[i]["seg"]
-        x[g] = (x.get(g, seeds[g] * 7919 + 12345) * 1103515245 + 12345) % 2147483648
-        tail[i] += amp * x[g] / 2147483648.0
-    free, ready, at, out = {}, [i for i in range(n) if left[i] == 0], [0.0] * n, []
-    while ready:
-        st = {i: max(at[i], free.get(ops[i]["q"], 0.0)) if ops[i]["c"][0] != "L" else at[i] for i in ready}
-        i = min(ready, key=lambda k: (st[k] + sp[k][0], k))
-        if ops[i]["c"][0] != "L":
-            q, lim = ops[i]["q"], st[i] + sp[i][0]
-            i = max((k for k in ready if ops[k]["q"] == q and ops[k]["c"][0] != "L" and st[k] <= lim), key=lambda k: (tail[k], -k))
-            free[q] = st[i] + sp[i][0]
-        ready.remove(i)
-        out.append(i)
-        for k in succ[i]:
-            if i in deps[k]:
-                at[k] = max(at[k], st[i] + sp[i][1] + (0.0 if ops[i]["q"] == ops[k]["q"] == "p" else m["wake"]))
-            left[k] -= 1
-            if left[k] == 0:
-                ready.append(k)
-    return [ops[i] for i in out]
-
-
 def emit(g, T, ops):
-    ops = [ops[i] for i in CFG["order"]] if CFG.get("order") else arrange(ops, CFG["m"], CFG["seeds"], CFG["amp"])
     deps = depends(ops)
     queue = {"g": g, "v": g.vector, "a": g.scalar, "p": g.tensor, "s": g.sync}
     clock, pos = {q: {} for q in queue}, {q: 0 for q in queue}
@@ -183,7 +121,16 @@ def neighbours(T, topo, rank):
     n = len(T.cores)
     src = T.cores[rank]
     dst = [T.cores[(rank + 1) % n], T.cores[(rank - 1) % n]]
-    return dst, [e for e in topo.engines(src, dst[0]) if e in topo.engines(src, dst[1])]
+    may = [topo.engines(src, d) for d in dst]
+    if not CFG["fused"]:
+        both = [e for e in may[0] if e in may[1]]
+        return dst, [both, both]
+    size = min(len(may[0]), len(may[1]), len(set(may[0]) | set(may[1])) // 2)
+    i = 0 if len(may[0]) <= len(may[1]) else 1
+    eng = [None, None]
+    eng[i] = may[i][:size]
+    eng[1 - i] = [e for e in may[1 - i] if e not in eng[i]][:size]
+    return dst, eng
 
 
 def rank_program(g, core, T, topo):
@@ -191,335 +138,338 @@ def rank_program(g, core, T, topo):
     if rank is None:
         return
     n = len(T.cores)
-    ops = []
+    ops, tag = [], ["start"]
 
-    seg = [0]
-    SM = ("E", 64)
+    def op(q, fn, r, w, ev=None, dma=False, end=False):
+        ops.append({"tag": tag[0], "q": q, "fn": fn, "r": list(r), "w": list(w), "ev": ev, "dma": dma, "end": end})
 
-    def op(q, fn, r, w, c=SM, ev=None, dma=False, end=False):
-        ops.append({"q": q, "fn": fn, "r": list(r), "w": list(w), "c": c, "ev": ev, "dma": dma, "end": end, "seg": seg[0]})
+    def dma(q, out, in_, r, w, sem, val=16):
+        op(q, lambda e: e.dma_start(out, in_), r, w, ev=(sem, val), dma=True)
 
-    def dma(q, out, in_, r, w, sem, t, val=16):
-        op(q, lambda e: e.dma_start(out, in_), r, w, ("D", t), ev=(sem, val), dma=True)
-
-    def ts(out, in0, s1, s2, op0, op1, r, w, c=SM):
+    def ts(out, in0, s1, s2, op0, op1, r, w):
         if op1 is None:
-            op("v", lambda e: e.tensor_scalar(out, in0, s1, None, op0), r, w, c)
+            op("v", lambda e: e.tensor_scalar(out, in0, s1, None, op0), r, w)
         else:
-            op("v", lambda e: e.tensor_scalar(out, in0, s1, s2, op0, op1), r, w, c)
+            op("v", lambda e: e.tensor_scalar(out, in0, s1, s2, op0, op1), r, w)
 
-    def tt(out, in0, in1, o, r, w, c=SM):
-        op("v", lambda e: e.tensor_tensor(out, in0, in1, o), r, w, c)
+    def tt(out, in0, in1, o, r, w):
+        op("v", lambda e: e.tensor_tensor(out, in0, in1, o), r, w)
 
-    def cp(out, in_, r, w, c=SM):
-        op("v", lambda e: e.tensor_copy(out, in_), r, w, c)
+    def cp(out, in_, r, w):
+        op("v", lambda e: e.tensor_copy(out, in_), r, w)
 
-    def act(out, in_, f, r, w, c=SM, **kw):
-        op("a", lambda e: e.activation(out, in_, f, **kw), r, w, c)
+    def fill(out, v, w):
+        op("v", lambda e: e.memset(out, v), [], w)
+
+    def scan(out, d0, d1, o1, r, w):
+        op("v", lambda e: e.tensor_tensor_scan(out, d0, d1, 0.0, A.mult, o1), r, w)
+
+    def act(out, in_, f, r, w, **kw):
+        op("a", lambda e: e.activation(out, in_, f, **kw), r, w)
 
     def iota(out, pat, base, cm, w, flt=True):
-        cols = 1
-        for p in pat:
-            cols *= p[1]
         if flt:
-            op("g", lambda e: e.iota(out, pat, base, cm, allow_small_or_imprecise_dtypes=True), [], w, ("I", cols))
+            op("g", lambda e: e.iota(out, pat, base, cm, allow_small_or_imprecise_dtypes=True), [], w)
         else:
-            op("g", lambda e: e.iota(out, pat, base, cm), [], w, ("I", cols))
+            op("g", lambda e: e.iota(out, pat, base, cm), [], w)
 
-    def mms(items, r, w, cycles):
+    def mms(items, r, w):
         def fn(e):
             ins = None
             for out, lhs, rhs, st, sp in items:
                 ins = e.matmul(out, lhs, rhs, st, sp)
             return ins
-        op("p", fn, r, w, ("P", cycles))
+        op("p", fn, r, w)
 
-    def unwrap(out, src, cols, r, w):
-        mms([(out, T.sel[:, 15 - i:143 - i], src[:, i:16 * cols:16], i == 0, i == 15) for i in range(16)], r + ["sel"], w, 1024)
-
-    def two(t, a):
-        return t[:, K * (a % 2):K * (a % 2) + K]
-
-    op("v", lambda e: e.memset(T.tb[:], 0), [], ["tb0"], ("E", W))
-    dma("s", T.wki[:], T.wk[:], [], ["wki"], "l_wk", 2600)
-    dma("a", T.b16[:], T.b0[:], [], ["b16"], "l_b", 2700)
-    dma("s", T.r16[:], T.rec[:], [], ["r16"], "l_rec", 3500)
-    dma("a", T.thr[:, 0:1], T.th[:], [], ["thr"], "l_th", 3500)
-    dma("s", T.tb[0:128:4, :], T.hop[:], ["tb0"], ["tbh"], "l_tb", 2900, 48)
-    dma("s", T.tb[2:128:16, :], T.up[:], ["tb0"], ["tbu"], "l_tb", 2900, 48)
-    dma("s", T.tb[6:128:16, :], T.dn[:], ["tb0"], ["tbd"], "l_tb", 2900, 48)
-    dma("s", T.w16[:], T.w[:], [], ["w16"], "l_w", 3600)
+    vb = CFG["vb"]
+    fill(T.kw[:], -200.0, ["kw"])
+    fill(T.tb[:], 0, ["tb0"])
+    dma("s", T.wki[:], T.wk[:], [], ["wki"], "l_wk")
+    dma("a", T.b16[:], T.b0[:], [], ["b16"], "l_b")
+    dma("s", T.r16[:], T.rec[:], [], ["r16"], "l_rec")
+    dma("a", T.thr[:, 0:1], T.th[:], [], ["thr"], "l_th")
+    dma("s", T.tb[0:128:4, :], T.hop[:], ["tb0"], ["tbh"], "l_tb", 48)
+    dma("s", T.tb[2:128:16, :], T.up[:], ["tb0"], ["tbu"], "l_tb", 48)
+    dma("s", T.tb[6:128:16, :], T.dn[:], ["tb0"], ["tbd"], "l_tb", 48)
+    dma("s", T.w16[:], T.w[:], [], ["w16"], "l_w")
     iota(T.pi[:, 0:2], [[16, 2]], 0, 1, ["pi0"], flt=False)
     iota(T.uu[:], [[1, 160]], 0, 0, ["uu"])
     iota(T.u16[:], [[16, 8], [0, 16]], 0, 0, ["u16"])
-    iota(T.mk0[:], [[0, 16], [1, 3]], 0, 0, ["mk0"])
-    op("v", lambda e: e.memset(T.kz[:], -200.0), [], ["kz"], ("E", K))
-    act(T.ee[:, 5 * W:5 * W + 16], T.kz[:, 0:16], F.Sigmoid, ["kz"], ["eez", "warm"], ("R", 1400))
+    iota(T.u4[:], [[4, 36], [0, 4]], 0, 0, ["u4"])
+    iota(T.mk0[:], [[0, 16], [1, 4]], 0, 0, ["mk0"])
+    iota(T.kz[:], [[0, K]], -200, 0, ["kz"])
+    iota(T.kc[:], [[0, 16], [-W, NK]], (NK - 1) * W, 0, ["kc"])
+    iota(T.d1[:], [[0, 64]], 0, 0, ["d1a", "d1b"])
+    act(T.ee[:, 5 * W:5 * W + 16], T.kw[:], F.Sigmoid, ["kw"], ["eez"])
     ts(T.pi[:, 2:3], T.pi[:, 0:1], 112, None, A.bitwise_and, None, ["pi0"], ["pi2"])
     ts(T.pi[:, 3:4], T.pi[:, 0:1], 16, None, A.bitwise_and, None, ["pi0"], ["pi3"])
     ts(T.pi[:, 4:5], T.pi[:, 1:2], 127, None, A.bitwise_and, None, ["pi0"], ["pi4"])
-    cp(T.pf[:, 0:5], T.pi[:, 0:5], ["pi0", "pi2", "pi3", "pi4"], ["pf"])
+    ts(T.pi[:, 5:6], T.pi[:, 0:1], 12, None, A.bitwise_and, None, ["pi0"], ["pi5"])
+    cp(T.pf[:, 0:6], T.pi[:, 0:6], ["pi0", "pi2", "pi3", "pi4", "pi5"], ["pf"])
     ts(T.pg[:, 0:1], T.pf[:, 3:4], 0.0625, None, A.mult, None, ["pf"], ["pg0"])
     ts(T.pg[:, 1:2], T.pf[:, 3:4], -0.0625, 1.0, A.mult, A.add, ["pf"], ["pg1"])
     ts(T.pg[:, 2:3], T.pf[:, 2:3], 15.0, None, A.add, None, ["pf"], ["pg2"])
-    ts(T.bd[:], T.u16[:], T.pf[:, 2:3], None, A.is_equal, None, ["u16", "pf"], ["bd"], ("E", 128))
-    ts(T.e0[:], T.uu[:], T.pf[:, 1:2], T.pg[:, 1:2], A.is_equal, A.mult, ["uu", "pf", "pg1"], ["e0"], ("E", 160))
-    ts(T.e1[:], T.uu[:], T.pf[:, 1:2], T.pg[:, 0:1], A.is_equal, A.mult, ["uu", "pf", "pg0"], ["e1"], ("E", 160))
-    iota(T.k01[:], [[200, 2], [0, K]], 0, 0, ["k01"])
-    iota(T.cc[:], [[0, W]], 0, 0, ["cc"])
+    ts(T.pg[:, 3:4], T.pf[:, 2:3], 12.0, None, A.add, None, ["pf"], ["pg3"])
+    ts(T.bd[:], T.u16[:], T.pf[:, 2:3], None, A.is_equal, None, ["u16", "pf"], ["bd"])
+    ts(T.mq[:], T.u4[:, 0:16:4], T.pf[:, 5:6], None, A.is_equal, None, ["u4", "pf"], ["mq"])
+    ts(T.e0[:], T.uu[:], T.pf[:, 1:2], T.pg[:, 1:2], A.is_equal, A.mult, ["uu", "pf", "pg1"], ["e0"])
+    ts(T.e1[:], T.uu[:], T.pf[:, 1:2], T.pg[:, 0:1], A.is_equal, A.mult, ["uu", "pf", "pg0"], ["e1"])
+    ts(T.idf[:], T.uu[:, 0:128], T.pf[:, 0:1], None, A.is_equal, None, ["uu", "pf"], ["idf"])
+    ts(T.cz[:], T.u4[:], T.pg[:, 3:4], None, A.is_equal, None, ["u4", "pg3"], ["cz"])
     cp(T.du[:, 0:16], T.wki[:], ["wki"], ["du0"])
-    cp(T.dp[:, 0:16:2], T.wki[:, 0:8], ["wki"], ["dp0"])
-    cp(T.dp[:, 1:16:2], T.wki[:, 8:16], ["wki"], ["dp1"])
-    cp(T.bb[:], T.b16[:], ["b16"], ["bb"], ("E", W))
-    ts(T.idn[:], T.uu[:, 0:128], T.pf[:, 0:1], None, A.is_equal, None, ["uu", "pf"], ["idn"], ("E", 128))
-    if CFG["dense"]:
-        for j in range(4):
-            c0, c1 = K * j, K * (j % 2)
-            act(T["pr%d" % (j // 2)][:, c1:c1 + K], T.r16[:, c0:c0 + K], F.Copy, ["r16", "warm"], ["pr%d.%d" % (j // 2, j)], ("E", K), scale=-1.0)
-            act(T["pw%d" % (j // 2)][:, c1:c1 + K], T.w16[:, c0:c0 + K], F.Copy, ["w16", "warm"], ["pw%d.%d" % (j // 2, j)], ("E", K))
-    ts(T.sh[:], T.uu[:, 0:128], T.pf[:, 4:5], None, A.is_equal, None, ["uu", "pf"], ["sh"], ("E", 128))
-    ts(T.sel[:], T.uu[:], T.pg[:, 2:3], 4096.0, A.is_equal, A.mult, ["uu", "pg2"], ["sel"], ("E", 160))
-    ts(T.mk[:], T.mk0[:], 1.0, None, A.min, None, ["mk0"], ["mk"])
-    ts(T.df[:, 0:16], T.wki[:], 2048.0, None, A.add, None, ["wki"], ["df0"])
+    for q in range(4):
+        ts(T.ex[:, 128 * q:128 * q + 128], T.u16[:], T.pf[:, 2:3], T.mq[:, q:q + 1], A.is_equal, A.mult, ["u16", "pf", "mq"], ["ex%d" % q])
+    ts(T.sh[:], T.uu[:, 0:128], T.pf[:, 4:5], None, A.is_equal, None, ["uu", "pf"], ["sh"])
     ts(T.nth[:, 0:1], T.thr[:, 0:1], -1.0, None, A.mult, None, ["thr"], ["nth"])
+    if vb:
+        cp(T.bb[:, 0:vb], T.b16[:, 0:vb], ["b16"], ["bbv"])
+
+    def late():
+        ts(T.idn[:], T.uu[:, 0:128], T.pf[:, 0:1], None, A.is_equal, None, ["uu", "pf"], ["idn"])
+        ts(T.sel[:], T.uu[:], T.pg[:, 2:3], 4096.0, A.is_equal, A.mult, ["uu", "pg2"], ["sel"])
+        ts(T.sl2[:], T.uu[:], T.pg[:, 2:3], -0.03125, A.is_equal, A.mult, ["uu", "pg2"], ["sl2"])
+        fill(T.gt[:, :, 0], 0.0, ["gtz"])
+        ts(T.mk[:], T.mk0[:], 1.0, None, A.min, None, ["mk0"], ["mk"])
+        for k, (cols, v) in enumerate(((T.pat[:, 0:64:4], 0.0), (T.pat[:, 1:64:4], 1.0), (T.pat[:, 2:32:4], 1.0), (T.pat[:, 34:64:4], 0.5), (T.pat[:, 3:64:4], 0.5))):
+            fill(cols, v, ["pat%d" % k])
 
     dst, eng = neighbours(T, topo, rank)
-    n_up = len(neighbours(T, topo, (rank - 1) % n)[1])
-    n_dn = len(neighbours(T, topo, (rank + 1) % n)[1])
-    mode, nh, src, dln = CFG["mode"], CFG["half"], CFG["src"], "dl"
+    n_up = len(neighbours(T, topo, (rank - 1) % n)[1][0])
+    n_dn = len(neighbours(T, topo, (rank + 1) % n)[1][1])
+    UP, DN = NK, NK + 1
+    PARTS = [(0, CFG["cut"]), (CFG["cut"], 16)]
 
     for s in range(RO):
         last = s == RO - 1
-        seg[0] = 2 * s
         du, dun = T.du[:, 16 * s:16 * s + 16], "du%d" % s
         hb0 = HW * s
         h, hn = T.hb[:, hb0 + 16:hb0 + 16 + K], "h%d" % s
         lu, ld = T.lu[:, PW * s:PW * s + PW], T.ld[:, PW * s:PW * s + PW]
 
-        def xl(a, i=0, parts=1):
-            c = 16 // parts
-            return T.xu[:, 16 * a + c * i:16 * a + c * i + c]
+        def two(t, a):
+            return t[:, K * (a % NB):K * (a % NB) + K]
+
+        def xl(a, c0=0, c1=16):
+            return T.xu[:, 16 * a + c0:16 * a + c1]
 
         def xlist(a):
             if a < NK:
-                cp(xl(a), T.px[:, 2 * a:256:16], ["px.a"], ["x%d" % a])
-            elif a == NK:
-                cp(xl(a), T.pc[:, K:PW], ["pc.l"], ["x4"])
+                cp(xl(a), T.px[:, 0:16, 2 * a], ["px.a"], ["x%d" % a])
+            elif a == UP:
+                mms([(T.px[:, 16, :], T.sh[:], lu[:, 0:16], True, True)], ["sh", "lu%d" % s], ["px.l"])
+                cp(xl(a), T.px[:, 16, :], ["px.l"], ["x4"])
             else:
                 cp(xl(a), ld[:, K:PW], ["ld%d" % s], ["x5"])
 
-        def tables():
-            cp(T.xg[:], T.tb[:].indirect(T.dp[:]), ["tb0", "tbh", "tbu", "tbd", "dp0", "dp1"], ["xg"], ("G", K))
-            op("v", lambda e: e.transpose(T.yy[:], T.xg[:]), ["xg"], ["yy"], ("E", 128))
-            mms([(T.px[:, 0:120], T.e0[:, 16:144], T.yy[:, 0:240:2], True, False),
-                 (T.px[:, 0:120], T.e0[:, 0:128], T.yy[:, 16:256:2], False, True),
-                 (T.px[:, 128:248], T.e1[:, 32:160], T.yy[:, 0:240:2], True, False),
-                 (T.px[:, 128:248], T.e1[:, 16:144], T.yy[:, 16:256:2], False, True)], ["yy", "e0", "e1"], ["px.a"], 480)
-
-        tables()
-        if s > 0 and CFG["dense"]:
-            if CFG["dense"] == 2:
-                act(h, T.hw[:].indirect(du), F.Copy, ["hw%d" % j for j in range(4)] + [dun], [hn, "~cg"], ("G", K))
+        def h_psum(a):
+            if a < NK:
+                mms([(T.ph[:, 0:K], T.idf[:], h, True, True)], ["idf", hn], ["ph"])
+            elif a == UP:
+                mms([(T.pu[:, 0:16, :], T.sh[:], lu[:, 16:PW], True, True)], ["sh", "lu%d" % s], ["pu.h"])
             else:
-                cp(h, T.hw[:].indirect(du), ["hw%d" % j for j in range(4)] + [dun], [hn], ("G", K))
-            act(T.bb[:].indirect(du), T.kz[:], F.Sigmoid, ["kz", dun, "~cg"], ["bb", "~z"], ("S", K))
-            act(T.dl[:], T.br[:].indirect(du), F.Copy, ["br%d" % j for j in range(4)] + [dun, "~z"], ["dl"], ("G", K))
-            act(T.cg[:], T.cc[:].indirect(du), F.Copy, ["cc", dun, "~z"], ["cg"], ("G", K))
-        else:
-            act(T.nr[:], T.r16[:].indirect(du), F.Copy, ["r16", dun, "warm"], ["nr", "~nr"], ("G", K), scale=-1.0)
-            if s > 0:
-                act(T.cg[:], T.cc[:].indirect(du), F.Copy, ["cc", dun, "~nr"], ["cg", "~cg"], ("G", K))
-            bw, bn = (T.b16, "b16") if s == 0 else (T.bb, "bb")
-            tt(T.dl[:], bw[:].indirect(du), T.nr[:], A.mult, [bn, dun, "nr"], ["dl"], ("G", K))
-            tt(h, T.w16[:].indirect(du), T.dl[:], A.mult, ["w16", dun, "dl"], [hn], ("G", K))
-            act(T.bb[:].indirect(du), T.kz[:], F.Sigmoid, ["kz", dun, "~cg"], ["bb"], ("S", K))
-        if s == 0 or not CFG["spec"]:
-            xlist(0)
-        cp(T.hb[:, hb0:hb0 + 16], T.px[:, 1:256:16], ["px.a"], [hn + "u"])
-        cp(T.hb[:, hb0 + 16 + K:hb0 + HW], T.px[:, 3:256:16], ["px.a"], [hn + "d"])
-        xlist(1)
+                mms([(T.pd[:, 0:K], T.idf[:], ld[:, 0:K], True, True)], ["idf", "ld%d" % s], ["pd"])
 
-        def send(i, land, from_, sem, s=s):
-            rid, pid = topo.addr(dst[i], core)
-            return lambda e: e.remote_dma(land, from_, T.sem[sem], T.sem["sent%d" % s], pid, rid, sum(1 << x for x in eng))
-        op("g", send(0, lu, T.hb[:, hb0:hb0 + PW], "au%d" % s), [hn, hn + "u"], ["su%d" % s], ("R", 3000 if s == 0 else 1000), ev=("sent%d" % s, len(eng)))
-        op("g", send(1, ld, T.hb[:, hb0 + 16:hb0 + HW], "ad%d" % s), [hn, hn + "d"], ["sd%d" % s], ("R", 1000), ev=("sent%d" % s, 2 * len(eng)))
-        op("g", None, ["su%d" % s], ["lu%d" % s], ("L", 0), ev=("au%d" % s, n_up))
-        op("g", None, ["sd%d" % s], ["ld%d" % s], ("L", 0), ev=("ad%d" % s, n_dn))
+        def weights(a):
+            act(two(T.wx, a), T.w16[:].indirect(xl(a)), F.Copy, ["w16", "x%d" % a], ["wx%d" % (a % NB)])
+
+        def grad(a):
+            hp, hpn = (T.ph[:, 0:K], "ph") if a < NK else (T.pu[:, 0:16, :], "pu.h") if a == UP else (T.pd[:, 0:K], "pd")
+            tt(two(T.gg, a), two(T.wx, a), hp, A.mult, ["wx%d" % (a % NB), hpn], ["g%d" % (a % NB)])
+
+        def grad_gather(a):
+            tt(two(T.gg, a), T.w16[:].indirect(xl(a)), h if a < NK else ld[:, 0:K], A.mult, ["w16", "x%d" % a, hn if a < NK else "ld%d" % s], ["g%d" % (a % NB)])
+
+        def size(a):
+            act(two(T.ab, a), two(T.gg, a), F.Abs, ["g%d" % (a % NB)], ["ab%d" % (a % NB)])
+
+        def excess(a):
+            act(two(T.rl, a), two(T.ab, a), F.Relu, ["ab%d" % (a % NB), "nth"], ["rl%d" % (a % NB)], bias=T.nth[:, 0:1])
+
+        def over(a):
+            ts(two(T.ov, a), two(T.ab, a), T.thr[:, 0:1], 1.0 if a else TINY, A.is_gt, A.mult, ["ab%d" % (a % NB), "thr"], ["ov%d" % (a % NB)])
+
+        def over_excess(a):
+            ts(two(T.ov, a), two(T.rl, a), 0.0, None, A.is_gt, None, ["rl%d" % (a % NB)], ["ov%d" % (a % NB)])
+
+        def sign_excess(a):
+            act(two(T.ov, a), two(T.rl, a), F.Sign, ["rl%d" % (a % NB)], ["ov%d" % (a % NB)])
+
+        def count(a):
+            mms([(T.pc[:, 0:64], T.cz[:, 12 - 4 * q:140 - 4 * q], two(T.ov, a)[:, 64 * q:64 * q + 64], q == 0, q == 3) for q in range(4)],
+                ["cz", "ov%d" % (a % NB)], ["pc.c"])
+
+        def strong(a):
+            act(T.mn[:], T.pc[:, 0:64], F.Relu, ["pc.c"], ["mn"], bias=-8.0)
+
+        def spread(a):
+            for i, (c0, c1) in enumerate(PARTS):
+                ps, items = T["ps%d" % i], []
+                for q in range(4):
+                    lo, hi = max(16 * c0, 64 * q), min(16 * c1, 64 * q + 64)
+                    if lo < hi:
+                        items.append((ps[:, lo - 16 * c0:hi - 16 * c0], T.ex[:, 128 * q:128 * q + 128], T.mn[:, lo - 64 * q:hi - 64 * q], not items, False))
+                if items:
+                    mms(items, ["mn"] + ["ex%d" % q for q in range(4)], ["ps%d" % i])
+
+        def held(a, i):
+            c0, c1 = PARTS[i]
+            if c0 < c1:
+                act(T.nz[:, 16 * c0:16 * c1], T.bb[:].indirect(xl(a, c0, c1)), F.Abs, ["bb", "x%d" % a], ["nz%d" % i])
+                mms([(T["ps%d" % i][:, 0:16 * (c1 - c0)], T.bd[:], T.nz[:, 16 * c0:16 * c1], False, True)], ["bd", "nz%d" % i], ["ps%d" % i])
+
+        def total(a):
+            tt(T.ss[:], T.bb[:].indirect(xl(a)), two(T.gg, a), A.add, ["bb", "x%d" % a, "g%d" % (a % NB)], ["ss"])
+
+        def accept(i):
+            c0, c1 = PARTS[i]
+            if c0 < c1:
+                act(T.ac[:, 16 * c0:16 * c1], T["ps%d" % i][:, 0:16 * (c1 - c0)], F.Sign, ["ps%d" % i], ["ac%d" % i])
+
+        def put(a, i):
+            c0, c1 = PARTS[i]
+            if c0 < c1:
+                tt(T.bb[:].indirect(xl(a, c0, c1)), T.ss[:, 16 * c0:16 * c1], T.ac[:, 16 * c0:16 * c1], A.mult, ["ss", "x%d" % a, "ac%d" % i], ["bb"])
+
+        def held_first(a):
+            act(T.nz[:], T.bb[:].indirect(xl(a)), F.Abs, ["bb", "x%d" % a], ["nz0", "nz1"], scale=BIG)
+            mms([(T.ps0[:, 0:K], T.bd[:], T.nz[:], True, False)], ["bd", "nz0", "nz1"], ["ps0"])
+
+        def sum_first(a):
+            mms([(T.ps0[:, 0:K], T.bd[:], two(T.ov, a), False, True)], ["bd", "ov%d" % (a % NB)], ["ps0"])
+
+        def accept_first(a):
+            ts(T.ac[:], T.ps0[:, 0:K], 8.5 * TINY, None, A.is_gt, None, ["ps0"], ["ac0", "ac1"])
+
+        def put_first(a):
+            tt(T.bb[:].indirect(xl(a)), T.ss[:], T.ac[:], A.mult, ["ss", "x%d" % a, "ac0", "ac1"], ["bb"])
+
+        def cscat(c0, c1):
+            lst, dl = T.du[:, 16 * s + c0:16 * s + c1], T.dl[:, 16 * c0:16 * c1]
+            if s == 0:
+                cp(T.cc[:].indirect(lst), dl, ["dl", dun], ["cc"])
+            else:
+                tt(T.cc[:].indirect(lst), T.cg[:, 16 * c0:16 * c1], dl, A.add, ["cg", "dl", dun], ["cc"])
+
+        def send():
+            sides = [(lu, T.hb[:, hb0:hb0 + PW], "au%d" % s), (ld, T.hb[:, hb0 + 16:hb0 + HW], "ad%d" % s)]
+            sent = T.sem["sent%d" % s]
+            if CFG["fused"]:
+                tr = []
+                for i, (land, from_, sem) in enumerate(sides):
+                    rid, pid = topo.addr(dst[i], core)
+                    tr.append(RemoteDMATransfer(dst_ids=[DstId(rid=rid, pnc=pid)], dma_engine_mask=sum(1 << x for x in eng[i]),
+                                                remote_sem=T.sem[sem], src=from_, dst=land))
+                op("g", lambda e: e.remote_dma_fused(tr, local_sem=sent), [hn, hn + "u", hn + "d"], ["su%d" % s, "sd%d" % s],
+                   ev=("sent%d" % s, len(eng[0]) + len(eng[1])))
+            else:
+                def one(i):
+                    rid, pid = topo.addr(dst[i], core)
+                    return lambda e: e.remote_dma(sides[i][0], sides[i][1], T.sem[sides[i][2]], sent, pid, rid, sum(1 << x for x in eng[i]))
+                op("g", one(0), [hn, hn + "u"], ["su%d" % s], ev=("sent%d" % s, len(eng[0])))
+                op("g", one(1), [hn, hn + "d"], ["sd%d" % s], ev=("sent%d" % s, 2 * len(eng[0])))
+            op("g", None, ["su%d" % s], ["lu%d" % s], ev=("au%d" % s, n_up))
+            op("g", None, ["sd%d" % s], ["ld%d" % s], ev=("ad%d" % s, n_dn))
+
+        bw, bn = (T.b16, "b16") if s == 0 else (T.bb, "bb")
+        act(T.bo[:], bw[:].indirect(du), F.Copy, [bn, dun], ["bo"], scale=-1.0)
         if s == 0:
+            act(T.bb[:, vb:W], T.b16[:, vb:W], F.Copy, ["b16"], ["bb"])
+        act(T.bb[:].indirect(du), T.kz[:], F.Sigmoid, ["kz", dun, "bbv"], ["bb"])
+        cp(T.xg[:], T.tb[:].indirect(du), ["tb0", "tbh", "tbu", "tbd", dun], ["xg"])
+        tt(T.dl[:], T.r16[:].indirect(du), T.bo[:], A.mult, ["r16", dun, "bo"], ["dl"])
+        op("v", lambda e: e.transpose(T.yy[:], T.xg[:]), ["xg"], ["yy"])
+        mms([(T.px[:, 0:16:2, 0:8], T.e0[:, 16:144], T.yy[:, :, 0:16:2], True, False),
+             (T.px[:, 0:16:2, 0:8], T.e0[:, 0:128], T.yy[:, :, 16:32:2], False, True),
+             (T.px[:, 1:16:2, 0:8], T.e1[:, 32:160], T.yy[:, :, 0:16:2], True, False),
+             (T.px[:, 1:16:2, 0:8], T.e1[:, 16:144], T.yy[:, :, 16:32:2], False, True)], ["yy", "e0", "e1"], ["px.a"])
+        tt(h, T.w16[:].indirect(du), T.dl[:], A.mult, ["w16", dun, "dl"], [hn])
+        h_psum(1)
+        xlist(0)
+        xlist(1)
+        act(T.hb[:, hb0:hb0 + 16], T.px[:, 0:16, 1], F.Copy, ["px.a"], [hn + "u"])
+        act(T.hb[:, hb0 + 16 + K:hb0 + HW], T.px[:, 0:16, 3], F.Copy, ["px.a"], [hn + "d"])
+        if not last:
+            act(T.ck[:], T.px[:, 0:16, 0:8:2], F.Copy, ["px.a"], ["ck"])
+        send()
+        if s == 0:
+            iota(T.cc[:], [[0, W]], 0, 0, ["cc"])
+            iota(T.k01[:], [[200, 2], [0, K]], 0, 0, ["k01"])
             for m in (4, 3, 2, 1, 0):
                 iota(T.ee[:, m * W:(m + 1) * W], [[0, W]], 0, 0, ["ee%d" % m])
 
-        def gv(a):
-            return T.gg[:, K * (a % 2):K * (a % 2) + K]
+        def spare(i):
+            if i == 0 and s > 0:
+                act(T.cg[:], T.cc[:].indirect(du), F.Copy, ["cc", dun], ["cg"])
+            elif i == 1 and not last:
+                for k in range(NK):
+                    cp(T.xm[:, :, 16 // N4 * k:16 // N4 * (k + 1)], xl(k), ["x%d" % k], ["xm%d" % k])
+            elif i > 0 and last:
+                cscat(*CFG["cl"][i - 1])
+                if i == len(CFG["cl"]):
+                    dma("s", T.yc[:], T.cc[:], ["cc"], ["yc"], "st_c")
 
-        def part(t, i, parts):
-            return t[:, (K // parts) * i:(K // parts) * (i + 1)]
-
-        def p1(a):
-            if src[a] == "g":
-                tt(gv(a), T.w16[:].indirect(xl(a)), h if a < NK else ld[:, 0:K], A.mult, ["w16", "x%d" % a, hn if a < NK else "ld%d" % s],
-                   ["g%d" % (a % 2)], ("G", K))
-            else:
-                act(two(T.wx, a), T.w16[:].indirect(xl(a)), F.Copy, ["w16", "x%d" % a], ["wx%d" % (a % 2)], ("G", K))
-                tt(gv(a), two(T.wx, a), T.px[:, K:2 * K], A.mult, ["wx%d" % (a % 2), "px.u"], ["g%d" % (a % 2)], ("E", K))
-
-        def p2(a):
-            act(two(T.ab, a), gv(a), F.Abs, ["g%d" % (a % 2)], ["ab%d" % (a % 2)], ("E", K))
-
-        def p3(a):
-            ab, ov, rl = "ab%d" % (a % 2), "ov%d" % (a % 2), "rl%d" % (a % 2)
-            if mode[a] == "A":
-                ts(two(T.ov, a), two(T.ab, a), T.thr[:, 0:1], None, A.is_gt, None, [ab, "thr"], [ov], ("E", K))
-            elif mode[a] == "0":
-                ts(two(T.ov, a), two(T.ab, a), T.thr[:, 0:1], 0.0625, A.is_gt, A.mult, [ab, "thr"], [ov], ("E", K))
-            else:
-                act(two(T.rl, a), two(T.ab, a), F.Relu, [ab, "nth"], [rl], ("E", K), bias=T.nth[:, 0:1])
-                if mode[a] == "C":
-                    act(two(T.ov, a), two(T.rl, a), F.Sign, [rl], [ov], ("E", K))
-                else:
-                    ts(two(T.ov, a), two(T.rl, a), 0.0, None, A.is_gt, None, [rl], [ov], ("E", K // 2))
-
-        def p4(a):
-            mms([(T.pc[:, 0:K], T.bd[:], two(T.ov, a), True, True)], ["bd", "ov%d" % (a % 2)], ["pc.c"], K)
-
-        def p5(a):
-            act(T.mn[:], T.pc[:, 0:K], F.Relu, ["pc.c"], ["mn"], ("E", K), bias=-8.0)
-            for i in range(nh):
-                mms([(T["ps%d" % i][:, 0:K // nh], T.idn[:], part(T.mn, i, nh), True, False)], ["idn", "mn"], ["ps%d" % i], K // nh)
-
-        def c1(a, i):
-            act(part(T.nz, i, nh), T.bb[:].indirect(xl(a, i, nh)), F.Abs, ["bb", "x%d" % a], ["nz%d" % i], ("G", K // nh))
-            mms([(T["ps%d" % i][:, 0:K // nh], T.bd[:], part(T.nz, i, nh), False, True)], ["bd", "nz%d" % i], ["ps%d" % i], K // nh)
-
-        def sm(a):
-            tt(T.ss[:], T.bb[:].indirect(xl(a)), gv(a), A.add, ["bb", "x%d" % a, "g%d" % (a % 2)], ["ss"], ("G", K))
-
-        def c3(a, i):
-            act(part(T.ac, i, nh), T["ps%d" % i][:, 0:K // nh], F.Sign, ["ps%d" % i], ["ac%d" % i], ("E", K // nh))
-
-        def c4(a, i, parts):
-            tt(T.bb[:].indirect(xl(a, i, parts)), part(T.ss, i, parts), part(T.ac, i, parts), A.mult,
-               ["ss", "x%d" % a] + (["ac%d" % i] if parts == nh else ["ac%d" % j for j in range(nh)]), ["bb"], ("S", K // parts))
-
-        def cscat(i=0, parts=1):
-            c = 16 // parts
-            lst = T.du[:, 16 * s + c * i:16 * s + c * i + c]
-            if s == 0:
-                cp(T.cc[:].indirect(lst), part(T.dl, i, parts), [dln, dun, "~eu"], ["cc"], ("S", K // parts))
-            else:
-                tt(T.cc[:].indirect(lst), part(T.cg, i, parts), part(T.dl, i, parts), A.add, ["cg", dln, dun, "~eu"], ["cc"], ("S", K // parts))
-
-        if last:
-            for i in range(4):
-                cscat(i, 4)
-            dma("s", T.yc[:], T.cc[:], ["cc"], ["yc"], "st_c", 3500)
-        xlist(2); xlist(3)
-        if not last:
-            for k in range(NK):
-                ts(T.ck[:, 16 * k:16 * k + 16], T.px[:, 2 * k:256:16], float((NK - 1 - k) * W), None, A.add, None, ["px.a"], ["ck%d" % k])
-        xlist(5)
-
-        p1(0)
-        if CFG["pm"]:
-            ts(T.ov[:, 0:K], gv(0), T.thr[:, 0:1], 0.0625, A.is_gt, A.mult, ["g0", "thr"], ["ov0"], ("E", K))
-            ts(T.ov[:, K:2 * K], gv(0), T.nth[:, 0:1], 0.0625, A.is_lt, A.mult, ["g0", "nth"], ["ov1"], ("E", K))
-        else:
-            p2(0); p3(0)
-        nzs = ["nz%d" % i for i in range(nh)]
-        act(T.nz[:], T.bb[:].indirect(xl(0)), F.Abs, ["bb", "x0"], nzs, ("G", K))
-        act(T.n1[:], T.nz[:], F.Sign, nzs, ["n1"], ("E", K))
-        sm(0)
-        p0 = T.ps1[:, K:2 * K]
-        mms([(p0, T.bd[:], T.ov[:, 0:K], True, False)], ["bd", "ov0"], ["ps1.v"], K)
-        if CFG["pm"]:
-            mms([(p0, T.bd[:], T.ov[:, K:2 * K], False, False)], ["bd", "ov1"], ["ps1.v"], K)
-        mms([(p0, T.bd[:], T.n1[:], False, True)], ["bd", "n1"], ["ps1.v", "ps1"], K)
-        ts(T.ac[:], p0, 0.53125, None, A.is_gt, None, ["ps1.v"], ["ac%d" % i for i in range(nh)], ("E", K))
-        c4(0, 0, 1)
-        for a in range(1, 6):
-            if a == NK:
-                mms([(T.pc[:, K:PW], T.sh[:], lu[:, 0:16], True, True)], ["sh", "lu%d" % s], ["pc.l"], 256)
-                mms([(T.px[:, K:2 * K], T.sh[:], lu[:, 16:PW], True, True)], ["sh", "lu%d" % s], ["px.u"], 4 * K)
-                xlist(4)
-            p1(a); p2(a); p3(a); p4(a); p5(a)
-            for i in range(nh):
-                c1(a, i)
-            sm(a)
-            for i in range(nh):
-                c3(a, i)
-            for i in range(nh):
-                c4(a, i, nh)
+        stage = {"L": xlist, "H": h_psum, "W": weights, "G": grad, "g": grad_gather, "B": size, "R": excess, "O": over, "o": over_excess, "s": sign_excess,
+                 "C": count, "M": strong, "X": spread, "N": lambda a: held(a, 0), "n": lambda a: held(a, 1), "S": total,
+                 "A": lambda a: accept(0), "a": lambda a: accept(1), "P": lambda a: put(a, 0), "p": lambda a: put(a, 1),
+                 "Z": held_first, "Q": sum_first, "V": accept_first, "U": put_first, "E": spare}
+        for t in " ".join(CFG["plan"][s]).split():
+            tag[0] = ("plan", s, t)
+            stage[t[0]](int(t[1]))
+        tag[0] = "r%d" % s
         if last:
             break
 
-        seg[0] = 2 * s + 1
-        n4 = CFG["p4"]
-        c4w = K // n4
+        n4, c4, j4 = N4, 16 // N4, K // N4
+        pk = T.pk[:, 0:64]
+        if s == 0:
+            late()
+        mms([(pk, T.idf[:], T.ck[:], True, False), (pk, T.idn[:], T.kc[:], False, False)], ["idf", "idn", "ck", "kc"], ["pk"])
+        mms([(T.pc[:, 0:64], T.idn[:], T.pat[:], True, False)], ["idn"] + ["pat%d" % k for k in range(5)], ["pc.c"])
         for i in range(n4):
-            for k in range(NK):
-                av = T.aa[:, K * k + c4w * i:K * k + c4w * (i + 1)]
-                if k < NK - CFG["raw"]:
-                    act(av, T.bb[:].indirect(xl(k, i, n4)), F.Abs, ["bb", "x%d" % k, "~a"], ["a%d%d" % (k, i), "~a"], ("G", c4w))
-                else:
-                    rw = T.rw[:, K * (k % 2) + c4w * i:K * (k % 2) + c4w * (i + 1)]
-                    cp(rw, T.bb[:].indirect(xl(k, i, n4)), ["bb", "x%d" % k], ["rw%d%d" % (k, i)], ("G", c4w))
-                    act(av, rw, F.Abs, ["rw%d%d" % (k, i)], ["a%d%d" % (k, i)], ("E", c4w))
-        if CFG["dense"]:
-            for j in range(4):
-                c0, c1_ = K * j, K * (j % 2)
-                tt(T.br[:, c0:c0 + K], T.bb[:, c0:c0 + K], T["pr%d" % (j // 2)][:, c1_:c1_ + K], A.mult, ["bb", "pr%d.%d" % (j // 2, j)], ["br%d" % j], ("E", K))
-                tt(T.hw[:, c0:c0 + K], T.br[:, c0:c0 + K], T["pw%d" % (j // 2)][:, c1_:c1_ + K], A.mult, ["br%d" % j, "pw%d.%d" % (j // 2, j)], ["hw%d" % j], ("E", K))
+            act(T.aa[:, i, :], T.bb[:].indirect(T.xm[:, i, :]), F.Abs, ["bb"] + ["xm%d" % k for k in range(NK)], ["a%d" % i])
         kin = T.k01[:, K * s:K * s + K]
         for m in (4, 3):
-            act(T.ee[:, m * W:(m + 1) * W].indirect(du), kin, F.Sigmoid, ["k01", dun] + (["~a"] if m == 3 or CFG["pin"] else []), ["ee%d" % m], ("S", K))
-        for i in range(n4):
-            av = [T.aa[:, K * k + c4w * i:K * k + c4w * (i + 1)] for k in range(NK)]
-            an = ["a%d%d" % (k, i) for k in range(NK)]
-            pm, pn = T.ps0[:, K + c4w * i:K + c4w * (i + 1)], "ps0.%d" % i
-            tt(pm, av[0], av[1], A.max, an[0:2], [pn], ("E", 2 * c4w))
-            tt(pm, av[2], pm, A.max, [an[2], pn], [pn], ("E", c4w))
-            tt(pm, av[3], pm, A.max, [an[3], pn], [pn], ("E", c4w))
-            for k in range(NK):
-                tt(T.eq[:, K * k + c4w * i:K * k + c4w * (i + 1)], av[k], pm, A.is_equal, [an[k], pn], ["eq%d%d" % (k, i)], ("E", c4w))
-        unwrap(T.ps1[:, K:K + 64], T.eq, 64, ["eq%d%d" % (k, i) for k in range(NK) for i in range(n4)], ["ps1.v"])
-        tt(T.ky[:], T.ck[:], T.ps1[:, K:K + 64], A.add, ["ck%d" % k for k in range(NK)] + ["ps1.v"], ["ky"])
-        tt(T.k2[:], T.ky[:, 0:32], T.ky[:, 32:64], A.max, ["ky"], ["k2"])
-        tt(T.ki[:, 0:16], T.k2[:, 0:16], T.k2[:, 16:32], A.max, ["k2"], ["ki0"])
-        ts(T.ki[:, 16:32], T.ki[:, 0:16], NK * W - 1, None, A.bitwise_and, None, ["ki0"], ["ki1"])
-        ts(T.ki[:, 32:48], T.ki[:, 0:16], W - 1, None, A.bitwise_and, None, ["ki0"], ["ki2"])
-        cp(T.eu[:], T.ki[:, 16:32], ["ki1"], ["eu", "~eu"])
-        for i in range(CFG["cs"]):
-            cscat(i, CFG["cs"])
-        ee03, ee14 = ["ee0", "ee1", "ee2", "ee3"], ["ee1", "ee2", "ee3", "ee4", "eez"]
-        act(T.ee[:, 0:4 * W].indirect(T.eu[:]), kin, F.Sigmoid, ["k01", "eu"], ee03, ("S", K))
-        for m in range(3):
-            ts(T.gl[:, m:48:3], T.ki[:, 16:32], float(m * W), float(ZC), A.add, A.min, ["ki1"], ["gl%d" % m])
-        ts(T.xf[:], T.ki[:, 32:48], 2048.0, None, A.add, None, ["ki2"], ["xf"])
-        if CFG["spec"]:
-            cp(T.dp[:, 0:16:2], T.ki[:, 32:40], ["ki2"], ["dp0"])
-            cp(T.dp[:, 1:16:2], T.ki[:, 40:48], ["ki2"], ["dp1"])
-            tables()
-            ts(T.wf[:], T.px[:, 0:256:16], float(3 * W), None, A.add, None, ["px.a"], ["wf"])
-        win, lev, gls = T.ee[:, W:5 * W + 16], 0.25 + 0.5 * s, ["gl0", "gl1", "gl2"]
-        act(T.gt[:, 0:384], win.indirect(T.gl[:, 0:24]), F.Relu, ee14 + gls, ["gt0"], ("G", 384), bias=-lev)
-        ts(T.gt[:, 384:768], win.indirect(T.gl[:, 24:48]), lev, None, A.is_gt, None, ee14 + gls, ["gt1"], ("G", 384))
-        unwrap(T.ps1[:, K:K + 48], T.gt, 48, ["gt0", "gt1"], ["ps1.v"])
-        op("v", lambda e: e.tensor_tensor_scan(T.sc[:], T.mk[:], T.ps1[:, K:K + 48], 0.0, A.mult, A.add), ["mk", "ps1.v"], ["sc"])
-        if CFG["spec"]:
-            tt(T.u2[:, 0:16], T.wf[:], T.sc[:, 2:48:3], A.subtract, ["wf", "sc"], ["u2"])
-            tt(T.u2[:, 16:32], T.ck[:, 0:16], T.sc[:, 2:48:3], A.min, ["ck0", "sc"], ["v2"])
-            tt(T.u2[:, 32:48], T.u2[:, 0:16], T.u2[:, 16:32], A.max, ["u2", "v2"], ["m2"])
-            ts(xl(0), T.u2[:, 32:48], float(-3 * W), None, A.add, None, ["m2"], ["x0"])
-        df, dfn = T.df[:, 16 * s:16 * s + 16], T.df[:, 16 * s + 16:16 * s + 32]
-        tt(T.uv[:, 0:16], T.xf[:], T.sc[:, 2:48:3], A.subtract, ["xf", "sc"], ["u"])
-        tt(T.uv[:, 16:32], df, T.sc[:, 2:48:3], A.min, ["df%d" % s, "sc"], ["v"])
-        tt(dfn, T.uv[:, 0:16], T.uv[:, 16:32], A.max, ["u", "v"], ["df%d" % (s + 1)])
-        ts(T.du[:, 16 * s + 16:16 * s + 32], dfn, -2048.0, None, A.add, None, ["df%d" % (s + 1)], ["du%d" % (s + 1)])
-        ts(T.dp[:, 0:16:2], T.df[:, 16 * s + 16:16 * s + 24], -2048.0, None, A.add, None, ["df%d" % (s + 1)], ["dp0"])
-        ts(T.dp[:, 1:16:2], T.df[:, 16 * s + 24:16 * s + 32], -2048.0, None, A.add, None, ["df%d" % (s + 1)], ["dp1"])
+            act(T.ee[:, m * W:(m + 1) * W].indirect(du), kin, F.Sigmoid, ["k01", dun], ["ee%d" % m])
 
-    dma("s", T.yb[:], T.bb[:], ["bb"], ["yb"], "st_b", 3500)
-    op("s", None, ["yb", "yc"], [], ("R", 0), end=True)
-    op("g", None, ["sd%d" % s for s in range(RO)], [], ("R", 0), end=True)
+        def vote(i, ks):
+            for k in ks if i >= 0 else ():
+                tt(T.eq[:, j4 * i:j4 * i + j4, k], T.aa[:, i, j4 * k:j4 * k + j4], T.pu[:, 16 + c4 * i:16 + c4 * (i + 1), :], A.is_equal,
+                   ["a%d" % i, "pu.%d" % i], ["eq%d%d" % (k, i)])
+        was, wn = (T.wki[:], "wki") if s == 0 else (T.sc[:, 3:64:4], "sc")
+        cp(T.df[:], was, [wn], ["df"])
+        cp(T.d1[:, 3:64:4], was, [wn], ["d1b"])
+        for i in range(n4):
+            av = [T.aa[:, i, j4 * k:j4 * k + j4] for k in range(NK)]
+            pm, pn = T.pu[:, 16 + c4 * i:16 + c4 * (i + 1), :], "pu.%d" % i
+            tt(pm, av[0], av[1], A.max, ["a%d" % i], [pn])
+            vote(i - 1, (0, 1))
+            tt(pm, av[2], pm, A.max, ["a%d" % i, pn], [pn])
+            vote(i - 1, (2, 3))
+            tt(pm, av[3], pm, A.max, ["a%d" % i, pn], [pn])
+        vote(n4 - 1, range(NK))
+        mms([(pk, T.sel[:, 15 - i:143 - i], T.eq[:, i:K:16, :], False, i == 15) for i in range(16)],
+            ["sel"] + ["eq%d%d" % (k, i) for k in range(NK) for i in range(n4)], ["pk"])
+        cscat(0, 8)
+        scan(T.ky[:], T.mk[:], pk, A.max, ["mk", "pk"], ["ky"])
+        ts(T.ki[:, 0:16], T.ky[:, 3:64:4], NK * W - 1, None, A.bitwise_and, None, ["ky"], ["ki1"])
+        ts(T.ki[:, 16:32], T.ky[:, 3:64:4], W - 1, None, A.bitwise_and, None, ["ky"], ["ki2"])
+        cp(T.eu[:], T.ki[:, 0:16], ["ki1"], ["eu"])
+        ee03, ee14 = ["ee0", "ee1", "ee2", "ee3"], ["ee1", "ee2", "ee3", "ee4", "eez"]
+        act(T.ee[:, 0:4 * W].indirect(T.eu[:]), kin, F.Sigmoid, ["k01", "eu"], ee03)
+        for m in range(3):
+            ts(T.gl[:, 16 * m:16 * m + 16], T.ki[:, 0:16], float(m * W), float(ZC), A.add, A.min, ["ki1"], ["gl%d" % m])
+        tt(T.d1[:, 0:64:4], T.ki[:, 16:32], T.df[:], A.subtract, ["ki2", "df"], ["d1a"])
+        cscat(8, 16)
+        win, lev, gls = T.ee[:, W:5 * W + 16], 0.25 + 0.5 * s, ["gl0", "gl1", "gl2"]
+        ts(T.gt[:, :, 1], win.indirect(T.gl[:, 0:16]), lev, 2.0, A.is_gt, A.mult, ee14 + gls, ["gt0"])
+        ts(T.gt[:, 0:128, 2], win.indirect(T.gl[:, 16:24]), lev, 2.0, A.is_gt, A.mult, ee14 + gls, ["gt1"])
+        act(T.gt[:, 128:K, 2], win.indirect(T.gl[:, 24:32]), F.Sign, ee14 + gls, ["gt2"], bias=-lev)
+        act(T.gt[:, :, 3], win.indirect(T.gl[:, 32:48]), F.Sign, ee14 + gls, ["gt3"], bias=-lev)
+        mms([(T.pc[:, 0:64], T.sl2[:, 15 - i:143 - i], T.gt[:, i:K:16, :], False, i == 15) for i in range(16)], ["sl2", "gtz", "gt0", "gt1", "gt2", "gt3"], ["pc.c"])
+        scan(T.sc[:], T.pc[:, 0:64], T.d1[:], A.add, ["pc.c", "d1a", "d1b"], ["sc"])
+        cp(T.du[:, 16 * s + 16:16 * s + 32], T.sc[:, 3:64:4], ["sc"], ["du%d" % (s + 1)])
+
+    dma("s", T.yb[:], T.bb[:], ["bb"], ["yb"], "st_b")
+    op("s", None, ["yb", "yc"], [], end=True)
+    op("g", None, ["sd%d" % s for s in range(RO)], [], end=True)
     emit(g, T, ops)

@@ -2,48 +2,58 @@ from concourse.bass import DstId, RemoteDMATransfer
 from concourse.mybir import AluOpType, ActivationFunctionType
 
 W, K, NK, RO = 1024, 256, 4, 3
-PW = K + 16
-HW = K + 32
+LW = 64
+PW = K + LW
+HW = K + 2 * LW
 ZC = 4 * W
+COL = (0, 2, 4, 6, 1, 3)
 BIG, TINY = 2.0 ** 99, 2.0 ** -30
-N4 = 4
 NB = 3
-PLAN = ["Z0 g0 g1 L3 B0 B1 R1 L2 O0 S0 Q0 W2 o1 V0 W3 C1 M1 G2 B2 X1 U0 R2",
-        "N1 n1 A1 G3 S1 o2 P1 C2 L4 B3 H4 a1 M2 R3 X2 p1 W4",
+FIRST = ["bo cv zs xg dl yy h H1 L0 L1 L2 L3 hl tx"]
+NEXT = ["zs h tx dl H1 cg"]
+HOP0 = ["g0 Z0 g1 B0 B1 R1 T0 S0 Q0 W2 o1 V0 W3 C1 M1 G2 B2 X1 U0 R2"]
+HOP1 = HOP0
+HOPS = ["N1 n1 A1 G3 S1 o2 P1 C2 L4 B3 H4 a1 M2 R3 X2 p1 W4",
         "o3 N2 n2 G4 S2 C3 A2 L5 B4 P2 H5 a2 M3 X3 W5 R4 p2",
         "G5 N3 S3 n3 A3 a3 o4 B5 C4 M4 P3 p3 X4",
-        "S4 R5 N4 n4 o5 A4 P4 a4 C5 M5 p4 X5 E0",
-        "E1 N5 S5 n5 E2 A5 P5 a5 p5"]
-CFG = {"cut": 4, "fused": 1, "vb": 384, "cl": ((0, 4), (4, 16)), "plan": [PLAN] * RO}
+        "S4 R5 N4 n4 o5 c0 A4 P4 a4 C5 M5 df0 df1 df2 xh il c1 p4 X5",
+        "xi N5 S5 n5 c2 A5 P5 a5 c3 p5"]
+MOVE = ["pk va0 va1 va2 va3 em4 em3 dr0 dr1 vm0 vm1 ve0 ve1 vm2 vm3 ve2 ve3 un dr2 dr3 dh0 el pt a1x a2x eu mk wu gl sx dd sy gv0 gv1 gs0 gs1 uc "
+        "dx1 dx2 dx3 dx4 dx5 dx6 dh1 dh2 dh3 ch0 ch1 ch5 ch6 ch2 cd ch3 ch4 cx"]
+LATE = ["kidn kpr kpw kq kz0 kz1 kz2 kz3 ksel ksl2 kgt kmk kpat kh0 kh1"]
+P1 = "h g0 g1 D0 zs dl H1 Z0 q0 S0 W2 B1 W3 G2 V0 R1 B2 o1 C1 cg R2 U0 tx G3 M1 o2 X1 N1 C2 n1 A1 B3 S1 a1 P1 R3 L4 W4 p1 M2 H4 o3 X2 N2 G4 n2 S2 A2 B4 C3 a2 L5 M3 P2 W5 H5 p2 R4 X3 N3 S3 n3 o4 A3 G5 a3 B5 C4 P3 p3 df0 M4 df1 R5 S4 X4 o5 c0 N4 n4 A4 P4 df2 a4 xh C5 M5 c1 il X5 p4 N5 c2 S5 n5 A5 c3 P5 a5 xi p5 dr1 va0 va1 dr0 va2 vm0 pk vm1 va3 ve0 ve1 vm2 vm3 ve2 ve3 dh0 dr2 em4 un dr3 el a1x a2x eu wu em3 mk dd sx gl gs0 sy gs1 gv0 pt gv1 dx1 dx4 uc dx5 dh1 dh3 dh2 dx6 dx2 ch0 ch1 dx3 ch4 ch3 ch2 cd ch6 ch5 cx"
+P0 = "bo xg dl cv zs yy hl h L0 g0 L1 Z0 L3 L2 B0 W2 g1 T0 H1 Q0 B1 S0 R1 kidn W3 V0 o1 G2 tx C1 M1 B2 U0 R2 X1 G3 N1 n1 S1 o2 A1 C2 kh0 P1 B3 kq a1 R3 L4 p1 H4 W4 M2 o3 X2 N2 L5 kmk G4 S2 C3 n2 H5 kpw A2 P2 ksl2 B4 a2 M3 X3 W5 p2 R4 df2 N3 G5 n3 o4 A3 B5 S3 kpat C4 P3 a3 kz3 R5 df0 kz0 M4 p3 kz1 kpr X4 kz2 S4 df1 o5 N4 c0 n4 A4 kh1 C5 a4 P4 M5 xh p4 c1 S5 il ksel xi X5 N5 c2 n5 A5 a5 P5 c3 p5 kgt em3 dr1 va0 va1 dr0 va2 vm0 vm1 ve0 ve1 va3 vm2 vm3 ve2 ve3 pk dr3 em4 dr2 dh0 un el a1x a2x eu wu gl sx dd sy mk gs1 gv0 gv1 gs0 dx5 dx1 dx2 dx3 pt dh2 dh3 dh1 uc dx4 ch1 ch0 ch2 ch4 ch3 cd dx6 ch5 ch6 cx"
+CFG = {"cut": 4, "vb": 384, "ch": ((0, 4), (4, 8), (8, 12), (12, 16)), "plan": [[P0], [P1], [P1]]}
 
 SCRATCH = {
     "b16": ("sbuf", [128, W], "bfloat16"), "w16": ("sbuf", [128, W], "bfloat16"), "r16": ("sbuf", [128, W], "bfloat16"),
     "thr": ("sbuf", [128, 4], "float32"), "nth": ("sbuf", [128, 4], "float32"), "tb": ("sbuf", [128, W], "int32"), "wki": ("sbuf", [128, 16], "int32"),
     "bb": ("sbuf", [128, W], "float32"), "cc": ("sbuf", [128, W], "float32"), "ee": ("sbuf", [128, 5 * W + 16], "float32"),
+    "br": ("sbuf", [128, W], "float32"), "hw": ("sbuf", [128, W], "float32"),
     "kw": ("sbuf", [128, 16], "float32"), "kz": ("sbuf", [128, K], "float32"), "k01": ("sbuf", [128, 2 * K], "float32"),
     "uu": ("sbuf", [128, 160], "bfloat16"), "u16": ("sbuf", [128, 128], "bfloat16"), "u4": ("sbuf", [128, 144], "bfloat16"), "pi": ("sbuf", [128, 8], "int32"),
-    "pf": ("sbuf", [128, 8], "float32"), "pg": ("sbuf", [128, 8], "float32"), "mq": ("sbuf", [128, 4], "float32"),
-    "mk0": ("sbuf", [128, 64], "float32"), "mk": ("sbuf", [128, 64], "float32"), "pat": ("sbuf", [128, 64], "bfloat16"), "kc": ("sbuf", [128, 64], "bfloat16"),
+    "pf": ("sbuf", [128, 8], "float32"), "pg": ("sbuf", [128, 8], "float32"), "mq": ("sbuf", [128, 8], "float32"),
+    "mk0": ("sbuf", [128, 64], "float32"), "mk": ("sbuf", [128, 64], "float32"), "mv": ("sbuf", [128, 2 * K], "float32"),
+    "pat": ("sbuf", [128, 64], "bfloat16"), "kc": ("sbuf", [128, 64], "bfloat16"),
     "sel": ("sbuf", [128, 160], "bfloat16"), "sl2": ("sbuf", [128, 160], "bfloat16"), "bd": ("sbuf", [128, 128], "bfloat16"), "idn": ("sbuf", [128, 128], "bfloat16"),
-    "cz": ("sbuf", [128, 144], "bfloat16"), "ex": ("sbuf", [128, 512], "bfloat16"),
+    "cz": ("sbuf", [128, 144], "bfloat16"), "ex": ("sbuf", [128, 512], "bfloat16"), "zq": ("sbuf", [128, 4, 144], "float16"),
     "e0": ("sbuf", [128, 160], "float16"), "e1": ("sbuf", [128, 160], "float16"), "sh": ("sbuf", [128, 128], "float32"), "idf": ("sbuf", [128, 128], "float32"),
-    "du": ("sbuf", [128, 16 * RO], "uint16"), "df": ("sbuf", [128, 16], "float32"),
-    "xg": ("sbuf", [128, K], "float16"), "yy": ("sbuf", [128, 8, 32], "float16"), "xu": ("sbuf", [128, 96], "uint16"), "xm": ("sbuf", [128, N4, 64 // N4], "uint16"),
+    "wu": ("sbuf", [128, 16], "uint16"),
+    "xg": ("sbuf", [128, K], "float16"), "yy": ("sbuf", [128, 8, 32], "float16"), "xu": ("sbuf", [128, 112], "uint16"),
+    "xh": ("sbuf", [128, 96], "float16"), "xi": ("sbuf", [128, 64], "uint16"),
     "bo": ("sbuf", [128, K], "float32"), "dl": ("sbuf", [128, K], "float32"),
     "hb": ("sbuf", [128, RO * HW], "float32"), "lu": ("sbuf", [128, RO * PW], "float32"), "ld": ("sbuf", [128, RO * PW], "float32"),
     "gg": ("sbuf", [128, NB * K], "float32"), "ab": ("sbuf", [128, NB * K], "float32"), "rl": ("sbuf", [128, NB * K], "bfloat16"),
     "ov": ("sbuf", [128, NB * K], "bfloat16"), "wx": ("sbuf", [128, NB * K], "float32"),
     "mn": ("sbuf", [128, 64], "bfloat16"), "nz": ("sbuf", [128, K], "bfloat16"), "ss": ("sbuf", [128, K], "float32"),
     "ac": ("sbuf", [128, K], "float32"), "cg": ("sbuf", [128, K], "float32"),
-    "aa": ("sbuf", [128, N4, NK * K // N4], "float32"), "eq": ("sbuf", [128, K, NK], "bfloat16"), "ck": ("sbuf", [128, 64], "float32"),
+    "aa": ("sbuf", [128, NK * K], "float32"), "eq": ("sbuf", [128, 16, 64], "bfloat16"), "idh": ("sbuf", [128, 2, 128], "float16"),
     "ky": ("sbuf", [128, 64], "int32"), "ki": ("sbuf", [128, 32], "int32"), "eu": ("sbuf", [128, 16], "uint16"), "gl": ("sbuf", [128, 48], "uint16"),
-    "gt": ("sbuf", [128, K, 4], "bfloat16"), "d1": ("sbuf", [128, 64], "float32"), "sc": ("sbuf", [128, 64], "float32"),
-    "px": ("psum", [128, 32, 16], "float32"), "pc": ("psum", [128, 512], "float32"),
-    "ps0": ("psum", [128, 512], "float32"), "ps1": ("psum", [128, 512], "float32"),
-    "ph": ("psum", [128, 512], "float32"), "pu": ("psum", [128, 32, 16], "float32"),
-    "pd": ("psum", [128, 512], "float32"), "pk": ("psum", [128, 512], "float32"),
+    "gt": ("sbuf", [128, K, 4], "bfloat16"), "d1": ("sbuf", [128, 7, 64], "float32"), "sc": ("sbuf", [128, 5, 64], "float32"),
+    "px": ("psum", [128, 32, 16], "float32"), "ps0": ("psum", [128, 512], "float32"), "ps1": ("psum", [128, 512], "float32"), "ph": ("psum", [128, 512], "float32"),
+    "pr0": ("psum", [128, 512], "float32"), "pr1": ("psum", [128, 512], "float32"), "pw0": ("psum", [128, 512], "float32"), "pw1": ("psum", [128, 512], "float32"),
 }
-BANKS = ("px", "pc", "ps0", "ps1", "ph", "pu", "pd", "pk")
+BANKS = ("px", "ps0", "ps1", "ph", "pr0", "pr1", "pw0", "pw1")
 SEMAPHORES = (["qg", "qv", "qa", "qp", "qs", "l_wk", "l_rec", "l_th", "l_tb", "l_b", "l_w", "st_b", "st_c"]
               + ["au%d" % s for s in range(RO)] + ["ad%d" % s for s in range(RO)] + ["sent%d" % s for s in range(RO)])
 A = AluOpType
@@ -122,9 +132,6 @@ def neighbours(T, topo, rank):
     src = T.cores[rank]
     dst = [T.cores[(rank + 1) % n], T.cores[(rank - 1) % n]]
     may = [topo.engines(src, d) for d in dst]
-    if not CFG["fused"]:
-        both = [e for e in may[0] if e in may[1]]
-        return dst, [both, both]
     size = min(len(may[0]), len(may[1]), len(set(may[0]) | set(may[1])) // 2)
     i = 0 if len(may[0]) <= len(may[1]) else 1
     eng = [None, None]
@@ -161,8 +168,8 @@ def rank_program(g, core, T, topo):
     def fill(out, v, w):
         op("v", lambda e: e.memset(out, v), [], w)
 
-    def scan(out, d0, d1, o1, r, w):
-        op("v", lambda e: e.tensor_tensor_scan(out, d0, d1, 0.0, A.mult, o1), r, w)
+    def scan(out, d0, d1, o0, o1, r, w):
+        op("v", lambda e: e.tensor_tensor_scan(out, d0, d1, 0.0, o0, o1), r, w)
 
     def act(out, in_, f, r, w, **kw):
         op("a", lambda e: e.activation(out, in_, f, **kw), r, w)
@@ -196,27 +203,26 @@ def rank_program(g, core, T, topo):
     iota(T.uu[:], [[1, 160]], 0, 0, ["uu"])
     iota(T.u16[:], [[16, 8], [0, 16]], 0, 0, ["u16"])
     iota(T.u4[:], [[4, 36], [0, 4]], 0, 0, ["u4"])
-    iota(T.mk0[:], [[0, 16], [1, 4]], 0, 0, ["mk0"])
     iota(T.kz[:], [[0, K]], -200, 0, ["kz"])
-    iota(T.kc[:], [[0, 16], [-W, NK]], (NK - 1) * W, 0, ["kc"])
-    iota(T.d1[:], [[0, 64]], 0, 0, ["d1a", "d1b"])
+    iota(T.hb[:, 0:HW], [[0, HW]], 0, 0, ["hb", "h0"])
     act(T.ee[:, 5 * W:5 * W + 16], T.kw[:], F.Sigmoid, ["kw"], ["eez"])
     ts(T.pi[:, 2:3], T.pi[:, 0:1], 112, None, A.bitwise_and, None, ["pi0"], ["pi2"])
     ts(T.pi[:, 3:4], T.pi[:, 0:1], 16, None, A.bitwise_and, None, ["pi0"], ["pi3"])
     ts(T.pi[:, 4:5], T.pi[:, 1:2], 127, None, A.bitwise_and, None, ["pi0"], ["pi4"])
     ts(T.pi[:, 5:6], T.pi[:, 0:1], 12, None, A.bitwise_and, None, ["pi0"], ["pi5"])
-    cp(T.pf[:, 0:6], T.pi[:, 0:6], ["pi0", "pi2", "pi3", "pi4", "pi5"], ["pf"])
+    ts(T.pi[:, 6:7], T.pi[:, 0:1], 3, None, A.bitwise_and, None, ["pi0"], ["pi6"])
+    cp(T.pf[:, 0:7], T.pi[:, 0:7], ["pi0", "pi2", "pi3", "pi4", "pi5", "pi6"], ["pf"])
     ts(T.pg[:, 0:1], T.pf[:, 3:4], 0.0625, None, A.mult, None, ["pf"], ["pg0"])
     ts(T.pg[:, 1:2], T.pf[:, 3:4], -0.0625, 1.0, A.mult, A.add, ["pf"], ["pg1"])
     ts(T.pg[:, 2:3], T.pf[:, 2:3], 15.0, None, A.add, None, ["pf"], ["pg2"])
     ts(T.pg[:, 3:4], T.pf[:, 2:3], 12.0, None, A.add, None, ["pf"], ["pg3"])
     ts(T.bd[:], T.u16[:], T.pf[:, 2:3], None, A.is_equal, None, ["u16", "pf"], ["bd"])
-    ts(T.mq[:], T.u4[:, 0:16:4], T.pf[:, 5:6], None, A.is_equal, None, ["u4", "pf"], ["mq"])
+    ts(T.mq[:, 0:4], T.u4[:, 0:16:4], T.pf[:, 5:6], None, A.is_equal, None, ["u4", "pf"], ["mq"])
     ts(T.e0[:], T.uu[:], T.pf[:, 1:2], T.pg[:, 1:2], A.is_equal, A.mult, ["uu", "pf", "pg1"], ["e0"])
     ts(T.e1[:], T.uu[:], T.pf[:, 1:2], T.pg[:, 0:1], A.is_equal, A.mult, ["uu", "pf", "pg0"], ["e1"])
     ts(T.idf[:], T.uu[:, 0:128], T.pf[:, 0:1], None, A.is_equal, None, ["uu", "pf"], ["idf"])
     ts(T.cz[:], T.u4[:], T.pg[:, 3:4], None, A.is_equal, None, ["u4", "pg3"], ["cz"])
-    cp(T.du[:, 0:16], T.wki[:], ["wki"], ["du0"])
+    cp(T.xu[:, 0:16], T.wki[:], ["wki"], ["du"])
     for q in range(4):
         ts(T.ex[:, 128 * q:128 * q + 128], T.u16[:], T.pf[:, 2:3], T.mq[:, q:q + 1], A.is_equal, A.mult, ["u16", "pf", "mq"], ["ex%d" % q])
     ts(T.sh[:], T.uu[:, 0:128], T.pf[:, 4:5], None, A.is_equal, None, ["uu", "pf"], ["sh"])
@@ -224,82 +230,158 @@ def rank_program(g, core, T, topo):
     if vb:
         cp(T.bb[:, 0:vb], T.b16[:, 0:vb], ["b16"], ["bbv"])
 
-    def late():
-        ts(T.idn[:], T.uu[:, 0:128], T.pf[:, 0:1], None, A.is_equal, None, ["uu", "pf"], ["idn"])
-        ts(T.sel[:], T.uu[:], T.pg[:, 2:3], 4096.0, A.is_equal, A.mult, ["uu", "pg2"], ["sel"])
-        ts(T.sl2[:], T.uu[:], T.pg[:, 2:3], -0.03125, A.is_equal, A.mult, ["uu", "pg2"], ["sl2"])
-        fill(T.gt[:, :, 0], 0.0, ["gtz"])
-        ts(T.mk[:], T.mk0[:], 1.0, None, A.min, None, ["mk0"], ["mk"])
+    def quarters():
+        ts(T.mq[:, 4:8], T.uu[:, 0:4], T.pf[:, 6:7], None, A.is_equal, None, ["uu", "pf"], ["mr"])
+        ts(T.pg[:, 4:5], T.pf[:, 0:1], 3.0, None, A.add, None, ["pf"], ["pg4"])
+
+    def pattern():
         for k, (cols, v) in enumerate(((T.pat[:, 0:64:4], 0.0), (T.pat[:, 1:64:4], 1.0), (T.pat[:, 2:32:4], 1.0), (T.pat[:, 34:64:4], 0.5), (T.pat[:, 3:64:4], 0.5))):
             fill(cols, v, ["pat%d" % k])
+
+    def widen(name, src, sn):
+        for j in range(2):
+            mms([(T["%s%d" % (name, j)][:], T.idn[:], src[:, 512 * j:512 * j + 512], True, True)], ["idn", sn], ["%s%d" % (name, j)])
+
+    late = {
+        "kidn": lambda: ts(T.idn[:], T.uu[:, 0:128], T.pf[:, 0:1], None, A.is_equal, None, ["uu", "pf"], ["idn"]),
+        "kh": lambda i: ts(T.idh[:, i, :], T.uu[:, 0:128], T.pf[:, 0:1], 1.0 - 2 * i, A.is_equal, A.mult, ["uu", "pf"], ["idh%d" % i]),
+        "kpr": lambda: widen("pr", T.r16, "r16"), "kpw": lambda: widen("pw", T.w16, "w16"), "kq": quarters,
+        "kz": lambda r: ts(T.zq[:, r, :], T.uu[:, 0:144], T.pg[:, 4:5], T.mq[:, 4 + r:5 + r], A.is_equal, A.mult, ["uu", "pg4", "mr"], ["zq%d" % r]),
+        "ksel": lambda: ts(T.sel[:], T.uu[:], T.pg[:, 2:3], 4096.0, A.is_equal, A.mult, ["uu", "pg2"], ["sel"]),
+        "ksl": lambda _: ts(T.sl2[:], T.uu[:], T.pg[:, 2:3], -0.03125, A.is_equal, A.mult, ["uu", "pg2"], ["sl2"]),
+        "kgt": lambda: fill(T.gt[:, :, 0], 0.0, ["gtz"]),
+        "kmk": lambda: ts(T.mk[:], T.mk0[:], 1.0, None, A.min, None, ["mk0"], ["mk"]), "kpat": pattern}
 
     dst, eng = neighbours(T, topo, rank)
     n_up = len(neighbours(T, topo, (rank - 1) % n)[1][0])
     n_dn = len(neighbours(T, topo, (rank + 1) % n)[1][1])
     UP, DN = NK, NK + 1
     PARTS = [(0, CFG["cut"]), (CFG["cut"], 16)]
+    CH = CFG["ch"]
 
     for s in range(RO):
         last = s == RO - 1
-        du, dun = T.du[:, 16 * s:16 * s + 16], "du%d" % s
+        du, dun = T.xu[:, 0:16], "du"
         hb0 = HW * s
-        h, hn = T.hb[:, hb0 + 16:hb0 + 16 + K], "h%d" % s
+        h, hn = T.hb[:, hb0 + LW:hb0 + LW + K], "h%d" % s
         lu, ld = T.lu[:, PW * s:PW * s + PW], T.ld[:, PW * s:PW * s + PW]
+        brs, hws = ["br%d" % j for j in range(4)], ["hw%d" % j for j in range(4)]
 
-        def two(t, a):
+        def buf(t, a):
             return t[:, K * (a % NB):K * (a % NB) + K]
 
         def xl(a, c0=0, c1=16):
-            return T.xu[:, 16 * a + c0:16 * a + c1]
+            return T.xu[:, 16 + 16 * a + c0:16 + 16 * a + c1]
+
+        def old_b():
+            act(T.bo[:], T.b16[:].indirect(du), F.Copy, ["b16", dun], ["bo"], scale=-1.0)
+
+        def delta():
+            if s == 0:
+                tt(T.dl[:], T.r16[:].indirect(du), T.bo[:], A.mult, ["r16", dun, "bo"], ["dl"])
+            else:
+                act(T.dl[:], T.br[:].indirect(du), F.Copy, brs + [dun], ["dl"], scale=-1.0)
+
+        def make_h():
+            if s == 0:
+                tt(h, T.w16[:].indirect(du), T.dl[:], A.mult, ["w16", dun, "dl"], [hn])
+            else:
+                ts(h, T.hw[:].indirect(du), -1.0, None, A.mult, None, hws + [dun], [hn])
+
+        def tables(lst, ln):
+            cp(T.xg[:], T.tb[:].indirect(lst), ["tb0", "tbh", "tbu", "tbd", ln], ["xg"])
+
+        def to_lists(less=False):
+            if less:
+                mms([(T.px[:, 0:16, c], T.idh[:, 1, :], T.xh[:, 16 * (t % 6):16 * (t % 6) + 16], t == 0, False) for t, c in enumerate(COL + (5,))],
+                    ["idh1", "xh"], ["px.a"])
+            op("v", lambda e: e.transpose(T.yy[:], T.xg[:]), ["xg"], ["yy"])
+            mms([(T.px[:, 0:16:2, 0:7], T.e0[:, 16:144], T.yy[:, :, 0:14:2], not less, False),
+                 (T.px[:, 0:16:2, 0:7], T.e0[:, 0:128], T.yy[:, :, 16:30:2], False, False),
+                 (T.px[:, 1:16:2, 0:7], T.e1[:, 32:160], T.yy[:, :, 0:14:2], False, False),
+                 (T.px[:, 1:16:2, 0:7], T.e1[:, 16:144], T.yy[:, :, 16:30:2], False, True)], ["yy", "e0", "e1"], ["px.a"])
+
+        def payload_lists():
+            act(T.hb[:, hb0 + 3:hb0 + LW:4], T.px[:, 0:16, COL[UP]], F.Copy, ["px.a", "hb"], [hn + "u"])
+            act(T.hb[:, hb0 + LW + K + 3:hb0 + HW:4], T.px[:, 0:16, COL[DN]], F.Copy, ["px.a", "hb"], [hn + "d"])
+
+        def send():
+            tr = []
+            for i, (land, from_, sem) in enumerate([(lu, T.hb[:, hb0:hb0 + PW], "au%d" % s), (ld, T.hb[:, hb0 + LW:hb0 + HW], "ad%d" % s)]):
+                rid, pid = topo.addr(dst[i], core)
+                tr.append(RemoteDMATransfer(dst_ids=[DstId(rid=rid, pnc=pid)], dma_engine_mask=sum(1 << x for x in eng[i]),
+                                            remote_sem=T.sem[sem], src=from_, dst=land))
+            sent = T.sem["sent%d" % s]
+            op("g", lambda e: e.remote_dma_fused(tr, local_sem=sent), [hn, hn + "u", hn + "d"], ["sd%d" % s], ev=("sent%d" % s, len(eng[0]) + len(eng[1])))
+            op("g", None, ["sd%d" % s], ["lu%d" % s], ev=("au%d" % s, n_up))
+            op("g", None, ["sd%d" % s], ["ld%d" % s], ev=("ad%d" % s, n_dn))
+            if s == 0:
+                iota(T.cc[:], [[0, W]], 0, 0, ["cc"])
+                iota(T.mk0[:], [[0, 16], [1, 4]], 0, 0, ["mk0"])
+                iota(T.kc[:], [[0, 16], [-W, NK]], (NK - 1) * W, 0, ["kc"])
+                iota(T.d1[:], [[0, 7], [0, 64]], 0, 0, ["d1"])
+                iota(T.mv[:], [[0, 128], [4096, 4]], 0, 0, ["mv"])
+                iota(T.k01[:], [[200, 2], [0, K]], 0, 0, ["k01"])
+                for m in (4, 3, 2, 1, 0):
+                    iota(T.ee[:, m * W:(m + 1) * W], [[0, W]], 0, 0, ["ee%d" % m])
+
+        def cscat(i):
+            lst, dl = T.xu[:, 4 * i:4 * i + 4], T.dl[:, 64 * i:64 * i + 64]
+            if s == 0:
+                cp(T.cc[:].indirect(lst), dl, ["dl", dun], ["cc"])
+            else:
+                tt(T.cc[:].indirect(lst), T.cg[:, 64 * i:64 * i + 64], dl, A.add, ["cg", "dl", dun], ["cc"])
+            if last and i == 3:
+                dma("s", T.yc[:], T.cc[:], ["cc"], ["yc"], "st_c")
 
         def xlist(a):
             if a < NK:
                 cp(xl(a), T.px[:, 0:16, 2 * a], ["px.a"], ["x%d" % a])
             elif a == UP:
-                mms([(T.px[:, 16, :], T.sh[:], lu[:, 0:16], True, True)], ["sh", "lu%d" % s], ["px.l"])
+                mms([(T.px[:, 16, :], T.sh[:], lu[:, 3:LW:4], True, True)], ["sh", "lu%d" % s], ["px.l"])
                 cp(xl(a), T.px[:, 16, :], ["px.l"], ["x4"])
             else:
-                cp(xl(a), ld[:, K:PW], ["ld%d" % s], ["x5"])
+                cp(xl(a), ld[:, K + 3:PW:4], ["ld%d" % s], ["x5"])
 
         def h_psum(a):
             if a < NK:
-                mms([(T.ph[:, 0:K], T.idf[:], h, True, True)], ["idf", hn], ["ph"])
+                mms([(T.ph[:, 0:K], T.idf[:], h, True, True)], ["idf", hn], ["ph.0"])
             elif a == UP:
-                mms([(T.pu[:, 0:16, :], T.sh[:], lu[:, 16:PW], True, True)], ["sh", "lu%d" % s], ["pu.h"])
+                mms([(T.ph[:, K:2 * K], T.sh[:], lu[:, LW:PW], True, True)], ["sh", "lu%d" % s], ["ph.1"])
             else:
-                mms([(T.pd[:, 0:K], T.idf[:], ld[:, 0:K], True, True)], ["idf", "ld%d" % s], ["pd"])
+                mms([(T.ph[:, 0:K], T.idf[:], ld[:, 0:K], True, True)], ["idf", "ld%d" % s], ["ph.0"])
 
         def weights(a):
-            act(two(T.wx, a), T.w16[:].indirect(xl(a)), F.Copy, ["w16", "x%d" % a], ["wx%d" % (a % NB)])
+            act(buf(T.wx, a), T.w16[:].indirect(xl(a)), F.Copy, ["w16", "x%d" % a], ["wx%d" % (a % NB)])
 
         def grad(a):
-            hp, hpn = (T.ph[:, 0:K], "ph") if a < NK else (T.pu[:, 0:16, :], "pu.h") if a == UP else (T.pd[:, 0:K], "pd")
-            tt(two(T.gg, a), two(T.wx, a), hp, A.mult, ["wx%d" % (a % NB), hpn], ["g%d" % (a % NB)])
+            i = int(a == UP)
+            tt(buf(T.gg, a), buf(T.wx, a), T.ph[:, K * i:K * i + K], A.mult, ["wx%d" % (a % NB), "ph.%d" % i], ["g%d" % (a % NB)])
 
         def grad_gather(a):
-            tt(two(T.gg, a), T.w16[:].indirect(xl(a)), h if a < NK else ld[:, 0:K], A.mult, ["w16", "x%d" % a, hn if a < NK else "ld%d" % s], ["g%d" % (a % NB)])
+            tt(buf(T.gg, a), T.w16[:].indirect(xl(a)), h if a < NK else ld[:, 0:K], A.mult, ["w16", "x%d" % a, hn if a < NK else "ld%d" % s], ["g%d" % (a % NB)])
 
         def size(a):
-            act(two(T.ab, a), two(T.gg, a), F.Abs, ["g%d" % (a % NB)], ["ab%d" % (a % NB)])
+            act(buf(T.ab, a), buf(T.gg, a), F.Abs, ["g%d" % (a % NB)], ["ab%d" % (a % NB)])
 
         def excess(a):
-            act(two(T.rl, a), two(T.ab, a), F.Relu, ["ab%d" % (a % NB), "nth"], ["rl%d" % (a % NB)], bias=T.nth[:, 0:1])
+            act(buf(T.rl, a), buf(T.ab, a), F.Relu, ["ab%d" % (a % NB), "nth"], ["rl%d" % (a % NB)], bias=T.nth[:, 0:1])
 
         def over(a):
-            ts(two(T.ov, a), two(T.ab, a), T.thr[:, 0:1], 1.0 if a else TINY, A.is_gt, A.mult, ["ab%d" % (a % NB), "thr"], ["ov%d" % (a % NB)])
+            ts(buf(T.ov, a), buf(T.ab, a), T.thr[:, 0:1], None, A.is_gt, None, ["ab%d" % (a % NB), "thr"], ["ov%d" % (a % NB)])
 
         def over_excess(a):
-            ts(two(T.ov, a), two(T.rl, a), 0.0, None, A.is_gt, None, ["rl%d" % (a % NB)], ["ov%d" % (a % NB)])
+            ts(buf(T.ov, a), buf(T.rl, a), 0.0, None, A.is_gt, None, ["rl%d" % (a % NB)], ["ov%d" % (a % NB)])
 
         def sign_excess(a):
-            act(two(T.ov, a), two(T.rl, a), F.Sign, ["rl%d" % (a % NB)], ["ov%d" % (a % NB)])
+            act(buf(T.ov, a), buf(T.rl, a), F.Sign, ["rl%d" % (a % NB)], ["ov%d" % (a % NB)])
 
         def count(a):
-            mms([(T.pc[:, 0:64], T.cz[:, 12 - 4 * q:140 - 4 * q], two(T.ov, a)[:, 64 * q:64 * q + 64], q == 0, q == 3) for q in range(4)],
-                ["cz", "ov%d" % (a % NB)], ["pc.c"])
+            mms([(T.px[:, 17:21, :], T.cz[:, 12 - 4 * q:140 - 4 * q], buf(T.ov, a)[:, 64 * q:64 * q + 64], q == 0, q == 3) for q in range(4)],
+                ["cz", "ov%d" % (a % NB)], ["px.c"])
 
         def strong(a):
-            act(T.mn[:], T.pc[:, 0:64], F.Relu, ["pc.c"], ["mn"], bias=-8.0)
+            act(T.mn[:], T.px[:, 17:21, :], F.Relu, ["px.c"], ["mn"], bias=-8.0)
 
         def spread(a):
             for i, (c0, c1) in enumerate(PARTS):
@@ -308,166 +390,148 @@ def rank_program(g, core, T, topo):
                     lo, hi = max(16 * c0, 64 * q), min(16 * c1, 64 * q + 64)
                     if lo < hi:
                         items.append((ps[:, lo - 16 * c0:hi - 16 * c0], T.ex[:, 128 * q:128 * q + 128], T.mn[:, lo - 64 * q:hi - 64 * q], not items, False))
-                if items:
-                    mms(items, ["mn"] + ["ex%d" % q for q in range(4)], ["ps%d" % i])
+                mms(items, ["mn"] + ["ex%d" % q for q in range(4)], ["ps%d" % i])
 
         def held(a, i):
             c0, c1 = PARTS[i]
-            if c0 < c1:
-                act(T.nz[:, 16 * c0:16 * c1], T.bb[:].indirect(xl(a, c0, c1)), F.Abs, ["bb", "x%d" % a], ["nz%d" % i])
-                mms([(T["ps%d" % i][:, 0:16 * (c1 - c0)], T.bd[:], T.nz[:, 16 * c0:16 * c1], False, True)], ["bd", "nz%d" % i], ["ps%d" % i])
+            act(T.nz[:, 16 * c0:16 * c1], T.bb[:].indirect(xl(a, c0, c1)), F.Abs, ["bb", "x%d" % a], ["nz%d" % i])
+            mms([(T["ps%d" % i][:, 0:16 * (c1 - c0)], T.bd[:], T.nz[:, 16 * c0:16 * c1], False, True)], ["bd", "nz%d" % i], ["ps%d" % i])
 
         def total(a):
-            tt(T.ss[:], T.bb[:].indirect(xl(a)), two(T.gg, a), A.add, ["bb", "x%d" % a, "g%d" % (a % NB)], ["ss"])
+            tt(T.ss[:], T.bb[:].indirect(xl(a)), buf(T.gg, a), A.add, ["bb", "x%d" % a, "g%d" % (a % NB)], ["ss"])
 
         def accept(i):
             c0, c1 = PARTS[i]
-            if c0 < c1:
-                act(T.ac[:, 16 * c0:16 * c1], T["ps%d" % i][:, 0:16 * (c1 - c0)], F.Sign, ["ps%d" % i], ["ac%d" % i])
+            act(T.ac[:, 16 * c0:16 * c1], T["ps%d" % i][:, 0:16 * (c1 - c0)], F.Sign, ["ps%d" % i], ["ac%d" % i])
 
         def put(a, i):
             c0, c1 = PARTS[i]
-            if c0 < c1:
-                tt(T.bb[:].indirect(xl(a, c0, c1)), T.ss[:, 16 * c0:16 * c1], T.ac[:, 16 * c0:16 * c1], A.mult, ["ss", "x%d" % a, "ac%d" % i], ["bb"])
+            tt(T.bb[:].indirect(xl(a, c0, c1)), T.ss[:, 16 * c0:16 * c1], T.ac[:, 16 * c0:16 * c1], A.mult, ["ss", "x%d" % a, "ac%d" % i], ["bb"])
 
         def held_first(a):
             act(T.nz[:], T.bb[:].indirect(xl(a)), F.Abs, ["bb", "x%d" % a], ["nz0", "nz1"], scale=BIG)
-            mms([(T.ps0[:, 0:K], T.bd[:], T.nz[:], True, False)], ["bd", "nz0", "nz1"], ["ps0"])
+            mms([(T["ps%d" % a][:, 0:K], T.bd[:], T.nz[:], a == 0, a != 0)], ["bd", "nz0", "nz1"], ["ps%d" % a])
 
         def sum_first(a):
-            mms([(T.ps0[:, 0:K], T.bd[:], two(T.ov, a), False, True)], ["bd", "ov%d" % (a % NB)], ["ps0"])
+            mms([(T["ps%d" % a][:, 0:K], T.bd[:], buf(T.ov, a), a != 0, a == 0)], ["bd", "ov%d" % (a % NB)], ["ps%d" % a])
+
+        def over_first(a):
+            ts(buf(T.ov, a), buf(T.ab, a), T.thr[:, 0:1], TINY, A.is_gt, A.mult, ["ab%d" % (a % NB), "thr"], ["ov%d" % (a % NB)])
+
+        def excess_first(a):
+            ts(buf(T.ov, a), buf(T.rl, a), 0.0, TINY, A.is_gt, A.mult, ["rl%d" % (a % NB)], ["ov%d" % (a % NB)])
+
+        def both_sides(a):
+            ts(buf(T.ov, a), buf(T.gg, a), T.thr[:, 0:1], TINY, A.is_gt, A.mult, ["g%d" % (a % NB), "thr"], ["ov%d" % (a % NB)])
+            ts(buf(T.rl, a), buf(T.gg, a), T.nth[:, 0:1], TINY, A.is_lt, A.mult, ["g%d" % (a % NB), "nth"], ["rl%d" % (a % NB)])
+
+        def sum_both(a):
+            mms([(T.ps0[:, 0:K], T.bd[:], buf(T.ov, a), False, False)], ["bd", "ov%d" % (a % NB)], ["ps0"])
+            mms([(T.ps0[:, 0:K], T.bd[:], buf(T.rl, a), False, True)], ["bd", "rl%d" % (a % NB)], ["ps0"])
 
         def accept_first(a):
-            ts(T.ac[:], T.ps0[:, 0:K], 8.5 * TINY, None, A.is_gt, None, ["ps0"], ["ac0", "ac1"])
+            ts(T.ac[:], T["ps%d" % a][:, 0:K], 8.5 * TINY, None, A.is_gt, None, ["ps%d" % a], ["ac0", "ac1"])
 
         def put_first(a):
             tt(T.bb[:].indirect(xl(a)), T.ss[:], T.ac[:], A.mult, ["ss", "x%d" % a, "ac0", "ac1"], ["bb"])
 
-        def cscat(c0, c1):
-            lst, dl = T.du[:, 16 * s + c0:16 * s + c1], T.dl[:, 16 * c0:16 * c1]
-            if s == 0:
-                cp(T.cc[:].indirect(lst), dl, ["dl", dun], ["cc"])
+        pk, pt = T.ps1[:, K:K + 64], T.ps1[:, K + 64:K + 128]
+        kin = T.k01[:, K * s:K * s + K] if not last else None
+        ee03, ee14 = ["ee0", "ee1", "ee2", "ee3"], ["ee1", "ee2", "ee3", "ee4", "eez"]
+        win, lev = T.ee[:, W:5 * W + 16], 0.25 + 0.5 * s
+
+        def interleave():
+            for r in range(4):
+                mms([(T.px[:, 21:25, r:16:4], T.zq[:, r, 3 + r - k:131 + r - k], T.xh[:, 16 * k:16 * k + 16], k == 0, k == 3) for k in range(NK)],
+                    ["xh", "zq%d" % r], ["px.i"])
+
+        def top(i):
+            c0, c1 = CH[i]
+            return (T.ph, T.ps0)[i % 2][:, 0:64 * (c1 - c0)], ("ph.0", "ps0")[i % 2]
+
+        def largest(i):
+            c0, c1 = CH[i]
+            pm, pn = top(i)
+            scan(pm, T.mv[:, 0:64 * (c1 - c0)], T.aa[:, 64 * c0:64 * c1], A.min, A.max, ["mv", "a%d" % i], [pn] + ["ph.1"] * (i % 2 == 0))
+
+        def vote(i):
+            c0, c1 = CH[i]
+            pm, pn = top(i)
+            for k in range(NK):
+                tt(T.eq[:, c0:c1, k:64:4], T.aa[:, 64 * c0 + k:64 * c1:4], pm[:, 3:64 * (c1 - c0):4], A.is_equal, ["a%d" % i, pn], ["eq%d%d" % (k, i)])
+
+        def count_votes():
+            mms([(pk, T.sel[:, 15 - i:143 - i], T.eq[:, :, 16 * (i % 4) + 4 * (i // 4):16 * (i % 4) + 4 * (i // 4) + 4], False, i == 15) for i in range(16)],
+                ["sel"] + ["eq%d%d" % (k, i) for k in range(NK) for i in range(len(CH))], ["ps1"])
+
+        def stay(i):
+            if i == 0:
+                cp(T.d1[:, 0:5, 3:64:4], T.xu[:, 0:80], ["du", "x0", "x1", "x2", "x3", "d1"], ["old0"])
             else:
-                tt(T.cc[:].indirect(lst), T.cg[:, 16 * c0:16 * c1], dl, A.add, ["cg", "dl", dun], ["cc"])
+                c0 = hb0 + (i - 1) * (LW + K)
+                act(T.d1[:, 4 + i, 3:64:4], T.hb[:, c0 + 3:c0 + LW:4], F.Copy, [hn + "ud"[i - 1], "d1"], ["old%d" % i])
 
-        def send():
-            sides = [(lu, T.hb[:, hb0:hb0 + PW], "au%d" % s), (ld, T.hb[:, hb0 + 16:hb0 + HW], "ad%d" % s)]
-            sent = T.sem["sent%d" % s]
-            if CFG["fused"]:
-                tr = []
-                for i, (land, from_, sem) in enumerate(sides):
-                    rid, pid = topo.addr(dst[i], core)
-                    tr.append(RemoteDMATransfer(dst_ids=[DstId(rid=rid, pnc=pid)], dma_engine_mask=sum(1 << x for x in eng[i]),
-                                                remote_sem=T.sem[sem], src=from_, dst=land))
-                op("g", lambda e: e.remote_dma_fused(tr, local_sem=sent), [hn, hn + "u", hn + "d"], ["su%d" % s, "sd%d" % s],
-                   ev=("sent%d" % s, len(eng[0]) + len(eng[1])))
-            else:
-                def one(i):
-                    rid, pid = topo.addr(dst[i], core)
-                    return lambda e: e.remote_dma(sides[i][0], sides[i][1], T.sem[sides[i][2]], sent, pid, rid, sum(1 << x for x in eng[i]))
-                op("g", one(0), [hn, hn + "u"], ["su%d" % s], ev=("sent%d" % s, len(eng[0])))
-                op("g", one(1), [hn, hn + "d"], ["sd%d" % s], ev=("sent%d" % s, 2 * len(eng[0])))
-            op("g", None, ["su%d" % s], ["lu%d" % s], ev=("au%d" % s, n_up))
-            op("g", None, ["sd%d" % s], ["ld%d" % s], ev=("ad%d" % s, n_dn))
+        def choose(t):
+            c0 = hb0 + HW + (t - 5) * (LW + K)
+            out, on = (T.sc[:, t, :], "sc%d" % t) if t < 5 else (T.hb[:, c0:c0 + LW], "h%d%s" % (s + 1, "ud"[t - 5]))
+            scan(out, pt, T.d1[:, t, :], A.mult, A.add, ["ps1", "dif%d" % t, "old%d" % max(0, t - 4)], [on])
 
-        bw, bn = (T.b16, "b16") if s == 0 else (T.bb, "bb")
-        act(T.bo[:], bw[:].indirect(du), F.Copy, [bn, dun], ["bo"], scale=-1.0)
-        if s == 0:
-            act(T.bb[:, vb:W], T.b16[:, vb:W], F.Copy, ["b16"], ["bb"])
-        act(T.bb[:].indirect(du), T.kz[:], F.Sigmoid, ["kz", dun, "bbv"], ["bb"])
-        cp(T.xg[:], T.tb[:].indirect(du), ["tb0", "tbh", "tbu", "tbd", dun], ["xg"])
-        tt(T.dl[:], T.r16[:].indirect(du), T.bo[:], A.mult, ["r16", dun, "bo"], ["dl"])
-        op("v", lambda e: e.transpose(T.yy[:], T.xg[:]), ["xg"], ["yy"])
-        mms([(T.px[:, 0:16:2, 0:8], T.e0[:, 16:144], T.yy[:, :, 0:16:2], True, False),
-             (T.px[:, 0:16:2, 0:8], T.e0[:, 0:128], T.yy[:, :, 16:32:2], False, True),
-             (T.px[:, 1:16:2, 0:8], T.e1[:, 32:160], T.yy[:, :, 0:16:2], True, False),
-             (T.px[:, 1:16:2, 0:8], T.e1[:, 16:144], T.yy[:, :, 16:32:2], False, True)], ["yy", "e0", "e1"], ["px.a"])
-        tt(h, T.w16[:].indirect(du), T.dl[:], A.mult, ["w16", dun, "dl"], [hn])
-        h_psum(1)
-        xlist(0)
-        xlist(1)
-        act(T.hb[:, hb0:hb0 + 16], T.px[:, 0:16, 1], F.Copy, ["px.a"], [hn + "u"])
-        act(T.hb[:, hb0 + 16 + K:hb0 + HW], T.px[:, 0:16, 3], F.Copy, ["px.a"], [hn + "d"])
-        if not last:
-            act(T.ck[:], T.px[:, 0:16, 0:8:2], F.Copy, ["px.a"], ["ck"])
-        send()
-        if s == 0:
-            iota(T.cc[:], [[0, W]], 0, 0, ["cc"])
-            iota(T.k01[:], [[200, 2], [0, K]], 0, 0, ["k01"])
-            for m in (4, 3, 2, 1, 0):
-                iota(T.ee[:, m * W:(m + 1) * W], [[0, W]], 0, 0, ["ee%d" % m])
+        def dense(j, out, on, in0, in0n, ps):
+            tt(out[:, K * j:K * j + K], in0[:, K * j:K * j + K], T["%s%d" % (ps, j // 2)][:, K * (j % 2):K * (j % 2) + K], A.mult,
+               [in0n, "%s%d" % (ps, j // 2)], ["%s%d" % (on, j)])
 
-        def spare(i):
-            if i == 0 and s > 0:
-                act(T.cg[:], T.cc[:].indirect(du), F.Copy, ["cc", dun], ["cg"])
-            elif i == 1 and not last:
-                for k in range(NK):
-                    cp(T.xm[:, :, 16 // N4 * k:16 // N4 * (k + 1)], xl(k), ["x%d" % k], ["xm%d" % k])
-            elif i > 0 and last:
-                cscat(*CFG["cl"][i - 1])
-                if i == len(CFG["cl"]):
-                    dma("s", T.yc[:], T.cc[:], ["cc"], ["yc"], "st_c")
+        def lookups():
+            for m in range(3):
+                ts(T.gl[:, 16 * m:16 * m + 16], T.ki[:, 0:16], float(m * W), float(ZC), A.add, A.min, ["ki1"], ["gl%d" % m])
 
-        stage = {"L": xlist, "H": h_psum, "W": weights, "G": grad, "g": grad_gather, "B": size, "R": excess, "O": over, "o": over_excess, "s": sign_excess,
-                 "C": count, "M": strong, "X": spread, "N": lambda a: held(a, 0), "n": lambda a: held(a, 1), "S": total,
-                 "A": lambda a: accept(0), "a": lambda a: accept(1), "P": lambda a: put(a, 0), "p": lambda a: put(a, 1),
-                 "Z": held_first, "Q": sum_first, "V": accept_first, "U": put_first, "E": spare}
+        def look_v(i):
+            out, lst = ((T.gt[:, :, 1], T.gl[:, 0:16]), (T.gt[:, 0:128, 2], T.gl[:, 16:24]))[i]
+            ts(out, win.indirect(lst), lev, 2.0, A.is_gt, A.mult, ee14 + ["gl%d" % i], ["gt%d" % i])
+
+        def look_s(i):
+            out, lst = ((T.gt[:, 128:K, 2], T.gl[:, 24:32]), (T.gt[:, :, 3], T.gl[:, 32:48]))[i]
+            act(out, win.indirect(lst), F.Sign, ee14 + ["gl%d" % (i + 1)], ["gt%d" % (i + 2)], bias=-lev)
+
+        stage = {
+            "bo": old_b, "cv": lambda: act(T.bb[:, vb:W], T.b16[:, vb:W], F.Copy, ["b16"], ["bb"]),
+            "zs": lambda: act(T.bb[:].indirect(du), T.kz[:], F.Sigmoid, ["kz", dun, "bbv"], ["bb"]),
+            "xg": lambda: tables(du, dun), "yy": to_lists, "dl": delta, "h": make_h, "hl": payload_lists, "tx": send,
+            "cg": lambda: act(T.cg[:], T.cc[:].indirect(du), F.Copy, ["cc", dun], ["cg"]), "c": cscat,
+            "L": xlist, "H": h_psum, "W": weights, "G": grad, "g": grad_gather, "B": size, "R": excess, "O": over, "o": over_excess, "s": sign_excess,
+            "C": count, "M": strong, "X": spread, "N": lambda a: held(a, 0), "n": lambda a: held(a, 1), "S": total,
+            "A": lambda a: accept(0), "a": lambda a: accept(1), "P": lambda a: put(a, 0), "p": lambda a: put(a, 1),
+            "Z": held_first, "Q": sum_first, "T": over_first, "t": excess_first, "D": both_sides, "q": sum_both, "V": accept_first, "U": put_first}
+        move = {
+            "xh": lambda: cp(T.xh[:], T.d1[:, 1:7, 3:64:4], ["old0", "old1", "old2"], ["xh"]), "il": interleave,
+            "xi": lambda: cp(T.xi[:], T.px[:, 21:25, :], ["px.i"], ["xi"]),
+            "pk": lambda: mms([(pk, T.idn[:], T.kc[:], True, False)] + [(pk[:, k:64:4], T.idh[:, 0, :], T.xh[:, 16 * k:16 * k + 16], False, False) for k in range(NK)],
+                              ["idh0", "idn", "xh", "kc"], ["ps1"]),
+            "va": lambda i: act(T.aa[:, 64 * CH[i][0]:64 * CH[i][1]], T.bb[:].indirect(T.xi[:, 4 * CH[i][0]:4 * CH[i][1]]), F.Abs, ["bb", "xi"], ["a%d" % i]),
+            "em": lambda m: act(T.ee[:, m * W:(m + 1) * W].indirect(du), kin, F.Sigmoid, ["k01", dun], ["ee%d" % m]),
+            "df": stay, "vm": largest, "ve": vote, "un": count_votes,
+            "dr": lambda j: dense(j, T.br, "br", T.bb, "bb", "pr"), "dh": lambda j: dense(j, T.hw, "hw", T.br, "br%d" % j, "pw"),
+            "el": lambda: scan(T.ky[:], T.mk[:], pk, A.mult, A.max, ["mk", "ps1"], ["ky"]),
+            "pt": lambda: mms([(pt, T.idn[:], T.pat[:], True, False)], ["idn"] + ["pat%d" % k for k in range(5)], ["ps1"]),
+            "a1x": lambda: ts(T.ki[:, 0:16], T.ky[:, 3:64:4], NK * W - 1, None, A.bitwise_and, None, ["ky"], ["ki1"]),
+            "a2x": lambda: ts(T.ki[:, 16:32], T.ky[:, 3:64:4], W - 1, None, A.bitwise_and, None, ["ky"], ["ki2"]),
+            "eu": lambda: cp(T.eu[:], T.ki[:, 0:16], ["ki1"], ["eu"]), "wu": lambda: cp(T.wu[:], T.ki[:, 16:32], ["ki2"], ["wu"]),
+            "mk": lambda: act(T.ee[:, 0:4 * W].indirect(T.eu[:]), kin, F.Sigmoid, ["k01", "eu"], ee03),
+            "gl": lookups, "sx": lambda: tables(T.wu[:], "wu"), "sy": lambda: to_lists(True),
+            "dd": lambda: tt(T.d1[:, 0, 0:64:4], T.ki[:, 16:32], T.d1[:, 0, 3:64:4], A.subtract, ["ki2", "old0"], ["dif0"]),
+            "dx": lambda t: act(T.d1[:, t, 0:64:4], T.px[:, 0:16, COL[t - 1]], F.Copy, ["px.a"], ["dif%d" % t]),
+            "gv": look_v, "gs": look_s,
+            "uc": lambda: mms([(pt, T.sl2[:, 15 - i:143 - i], T.gt[:, i:K:16, :], False, i == 15) for i in range(16)],
+                              ["sl2", "gtz", "gt0", "gt1", "gt2", "gt3"], ["ps1"]),
+            "ch": choose,
+            "cd": lambda: cp(T.xu[:, 0:32], T.sc[:, 0:2, 3:64:4], ["sc0", "sc1"], ["du", "x0"]),
+            "cx": lambda: cp(T.xu[:, 32:80], T.sc[:, 2:5, 3:64:4], ["sc2", "sc3", "sc4"], ["x1", "x2", "x3"])}
         for t in " ".join(CFG["plan"][s]).split():
             tag[0] = ("plan", s, t)
-            stage[t[0]](int(t[1]))
+            name = t.rstrip("0123456789")
+            if not (last and name in move):
+                fn = late.get(name) or move.get(name) or stage[name]
+                fn(int(t[len(name):])) if name != t else fn()
         tag[0] = "r%d" % s
-        if last:
-            break
-
-        n4, c4, j4 = N4, 16 // N4, K // N4
-        pk = T.pk[:, 0:64]
-        if s == 0:
-            late()
-        mms([(pk, T.idf[:], T.ck[:], True, False), (pk, T.idn[:], T.kc[:], False, False)], ["idf", "idn", "ck", "kc"], ["pk"])
-        mms([(T.pc[:, 0:64], T.idn[:], T.pat[:], True, False)], ["idn"] + ["pat%d" % k for k in range(5)], ["pc.c"])
-        for i in range(n4):
-            act(T.aa[:, i, :], T.bb[:].indirect(T.xm[:, i, :]), F.Abs, ["bb"] + ["xm%d" % k for k in range(NK)], ["a%d" % i])
-        kin = T.k01[:, K * s:K * s + K]
-        for m in (4, 3):
-            act(T.ee[:, m * W:(m + 1) * W].indirect(du), kin, F.Sigmoid, ["k01", dun], ["ee%d" % m])
-
-        def vote(i, ks):
-            for k in ks if i >= 0 else ():
-                tt(T.eq[:, j4 * i:j4 * i + j4, k], T.aa[:, i, j4 * k:j4 * k + j4], T.pu[:, 16 + c4 * i:16 + c4 * (i + 1), :], A.is_equal,
-                   ["a%d" % i, "pu.%d" % i], ["eq%d%d" % (k, i)])
-        was, wn = (T.wki[:], "wki") if s == 0 else (T.sc[:, 3:64:4], "sc")
-        cp(T.df[:], was, [wn], ["df"])
-        cp(T.d1[:, 3:64:4], was, [wn], ["d1b"])
-        for i in range(n4):
-            av = [T.aa[:, i, j4 * k:j4 * k + j4] for k in range(NK)]
-            pm, pn = T.pu[:, 16 + c4 * i:16 + c4 * (i + 1), :], "pu.%d" % i
-            tt(pm, av[0], av[1], A.max, ["a%d" % i], [pn])
-            vote(i - 1, (0, 1))
-            tt(pm, av[2], pm, A.max, ["a%d" % i, pn], [pn])
-            vote(i - 1, (2, 3))
-            tt(pm, av[3], pm, A.max, ["a%d" % i, pn], [pn])
-        vote(n4 - 1, range(NK))
-        mms([(pk, T.sel[:, 15 - i:143 - i], T.eq[:, i:K:16, :], False, i == 15) for i in range(16)],
-            ["sel"] + ["eq%d%d" % (k, i) for k in range(NK) for i in range(n4)], ["pk"])
-        cscat(0, 8)
-        scan(T.ky[:], T.mk[:], pk, A.max, ["mk", "pk"], ["ky"])
-        ts(T.ki[:, 0:16], T.ky[:, 3:64:4], NK * W - 1, None, A.bitwise_and, None, ["ky"], ["ki1"])
-        ts(T.ki[:, 16:32], T.ky[:, 3:64:4], W - 1, None, A.bitwise_and, None, ["ky"], ["ki2"])
-        cp(T.eu[:], T.ki[:, 0:16], ["ki1"], ["eu"])
-        ee03, ee14 = ["ee0", "ee1", "ee2", "ee3"], ["ee1", "ee2", "ee3", "ee4", "eez"]
-        act(T.ee[:, 0:4 * W].indirect(T.eu[:]), kin, F.Sigmoid, ["k01", "eu"], ee03)
-        for m in range(3):
-            ts(T.gl[:, 16 * m:16 * m + 16], T.ki[:, 0:16], float(m * W), float(ZC), A.add, A.min, ["ki1"], ["gl%d" % m])
-        tt(T.d1[:, 0:64:4], T.ki[:, 16:32], T.df[:], A.subtract, ["ki2", "df"], ["d1a"])
-        cscat(8, 16)
-        win, lev, gls = T.ee[:, W:5 * W + 16], 0.25 + 0.5 * s, ["gl0", "gl1", "gl2"]
-        ts(T.gt[:, :, 1], win.indirect(T.gl[:, 0:16]), lev, 2.0, A.is_gt, A.mult, ee14 + gls, ["gt0"])
-        ts(T.gt[:, 0:128, 2], win.indirect(T.gl[:, 16:24]), lev, 2.0, A.is_gt, A.mult, ee14 + gls, ["gt1"])
-        act(T.gt[:, 128:K, 2], win.indirect(T.gl[:, 24:32]), F.Sign, ee14 + gls, ["gt2"], bias=-lev)
-        act(T.gt[:, :, 3], win.indirect(T.gl[:, 32:48]), F.Sign, ee14 + gls, ["gt3"], bias=-lev)
-        mms([(T.pc[:, 0:64], T.sl2[:, 15 - i:143 - i], T.gt[:, i:K:16, :], False, i == 15) for i in range(16)], ["sl2", "gtz", "gt0", "gt1", "gt2", "gt3"], ["pc.c"])
-        scan(T.sc[:], T.pc[:, 0:64], T.d1[:], A.add, ["pc.c", "d1a", "d1b"], ["sc"])
-        cp(T.du[:, 16 * s + 16:16 * s + 32], T.sc[:, 3:64:4], ["sc"], ["du%d" % (s + 1)])
 
     dma("s", T.yb[:], T.bb[:], ["bb"], ["yb"], "st_b")
     op("s", None, ["yb", "yc"], [], end=True)

@@ -2,28 +2,40 @@ from concourse.bass import DstId, RemoteDMATransfer
 from concourse.mybir import AluOpType, ActivationFunctionType
 
 W, K, NK, RO = 1024, 256, 4, 3
+UP, DN = NK, NK + 1
+KS = K // 2
 LW = 64
 PW = K + LW
 HW = K + 2 * LW
 ZC = 4 * W
+VB = 384
+TV = 768
+NB = 3
 COL = (0, 2, 4, 6, 1, 3)
 BIG, TINY = 2.0 ** 99, 2.0 ** -30
-NB = 3
-FIRST = ["bo cv zs xg dl yy h H1 L0 L1 L2 L3 hl tx"]
-NEXT = ["zs h tx dl H1 cg"]
-HOP0 = ["g0 Z0 g1 B0 B1 R1 T0 S0 Q0 W2 o1 V0 W3 C1 M1 G2 B2 X1 U0 R2"]
-HOP1 = HOP0
-HOPS = ["N1 n1 A1 G3 S1 o2 P1 C2 L4 B3 H4 a1 M2 R3 X2 p1 W4",
-        "o3 N2 n2 G4 S2 C3 A2 L5 B4 P2 H5 a2 M3 X3 W5 R4 p2",
-        "G5 N3 S3 n3 A3 a3 o4 B5 C4 M4 P3 p3 X4",
-        "S4 R5 N4 n4 o5 c0 A4 P4 a4 C5 M5 df0 df1 df2 xh il c1 p4 X5",
-        "xi N5 S5 n5 c2 A5 P5 a5 c3 p5"]
-MOVE = ["pk va0 va1 va2 va3 em4 em3 dr0 dr1 vm0 vm1 ve0 ve1 vm2 vm3 ve2 ve3 un dr2 dr3 dh0 el pt a1x a2x eu mk wu gl sx dd sy gv0 gv1 gs0 gs1 uc "
-        "dx1 dx2 dx3 dx4 dx5 dx6 dh1 dh2 dh3 ch0 ch1 ch5 ch6 ch2 cd ch3 ch4 cx"]
-LATE = ["kidn kpr kpw kq kz0 kz1 kz2 kz3 ksel ksl2 kgt kmk kpat kh0 kh1"]
-P1 = "h g0 g1 D0 zs dl H1 Z0 q0 S0 W2 B1 W3 G2 V0 R1 B2 o1 C1 cg R2 U0 tx G3 M1 o2 X1 N1 C2 n1 A1 B3 S1 a1 P1 R3 L4 W4 p1 M2 H4 o3 X2 N2 G4 n2 S2 A2 B4 C3 a2 L5 M3 P2 W5 H5 p2 R4 X3 N3 S3 n3 o4 A3 G5 a3 B5 C4 P3 p3 df0 M4 df1 R5 S4 X4 o5 c0 N4 n4 A4 P4 df2 a4 xh C5 M5 c1 il X5 p4 N5 c2 S5 n5 A5 c3 P5 a5 xi p5 dr1 va0 va1 dr0 va2 vm0 pk vm1 va3 ve0 ve1 vm2 vm3 ve2 ve3 dh0 dr2 em4 un dr3 el a1x a2x eu wu em3 mk dd sx gl gs0 sy gs1 gv0 pt gv1 dx1 dx4 uc dx5 dh1 dh3 dh2 dx6 dx2 ch0 ch1 dx3 ch4 ch3 ch2 cd ch6 ch5 cx"
-P0 = "bo xg dl cv zs yy hl h L0 g0 L1 Z0 L3 L2 B0 W2 g1 T0 H1 Q0 B1 S0 R1 kidn W3 V0 o1 G2 tx C1 M1 B2 U0 R2 X1 G3 N1 n1 S1 o2 A1 C2 kh0 P1 B3 kq a1 R3 L4 p1 H4 W4 M2 o3 X2 N2 L5 kmk G4 S2 C3 n2 H5 kpw A2 P2 ksl2 B4 a2 M3 X3 W5 p2 R4 df2 N3 G5 n3 o4 A3 B5 S3 kpat C4 P3 a3 kz3 R5 df0 kz0 M4 p3 kz1 kpr X4 kz2 S4 df1 o5 N4 c0 n4 A4 kh1 C5 a4 P4 M5 xh p4 c1 S5 il ksel xi X5 N5 c2 n5 A5 a5 P5 c3 p5 kgt em3 dr1 va0 va1 dr0 va2 vm0 vm1 ve0 ve1 va3 vm2 vm3 ve2 ve3 pk dr3 em4 dr2 dh0 un el a1x a2x eu wu gl sx dd sy mk gs1 gv0 gv1 gs0 dx5 dx1 dx2 dx3 pt dh2 dh3 dh1 uc dx4 ch1 ch0 ch2 ch4 ch3 cd dx6 ch5 ch6 cx"
-CFG = {"cut": 4, "vb": 384, "ch": ((0, 4), (4, 8), (8, 12), (12, 16)), "plan": [[P0], [P1], [P1]]}
+
+FIRST = ("ds1 widev ds3 bd oldb tables ds0 widen ds4 lists idf delta payload h send list0 list1 zero list2 hps1 nth "
+         "gath0 gath1 ex1 size0 both0 counts0 abs1 list3 wx2 exc1 sum0 ok0 grad2 cz ex0 over1 sh count1 rest1 abs2 strong1 spread1 put0")
+HEAD = "h send gath0 hps1 gath1 both0 zero size0 wx2 sum0 abs1 exc1 counts0 grad2 ok0 over1 abs2 count1 rest1 strong1 put0 spread1"
+ARRIVAL = ("exc2 nzs1 nzv1 wx3 oks1 sum1 over2 count2 _ okv1 _ grad3 put1 rest2 abs3 strong2 spread2 "
+           "nzv2 nzs2 sum2 okv2 exc3 _ list4 oks2 hps4 over3 put2 list5 _ _ count3 wx4 strong3 rest3 hps5 spread3 "
+           "nzv3 nzs3 sum3 wx5 oks3 grad4 okv3 abs4 grad5 abs5 put3 _ "
+           "tiny4 partv4 sum4 parts4 exc5 over5 _ rest5 ok4 _ _ put4 _ count5 strong5 spread5 "
+           "nzv5 nzs5 sum5 okv5 _ oks5 put5 _")
+SPARE = ("zbr stay0", "", "", "grow", "stay2 stay1 half", "weave", "", "woven held3", "", "", "", "held4")
+SPARE0 = ("ds2 stay0 zq2 idn", "sel", "c0 zq1 stay2 stay1", "", "half zq3 zq0", "weave less", "wp recp sl", "woven", "held4 gtz", "c1", "c2 mask", "pat c3 held3")
+MOVE = ("look0 keys look1 br0 br1 top0 look2 top1 vote0 vote1 top2 tally0 look3 top3 vote2 tally1 tally2 vote3 hw1 br2 tally3 elect free claim wish claimu wishu "
+        "br3 neg0 mark ahead sections sees0 sees1 neg2 aheadl diff1 seev0 diff4 seev1 step diff3 hw2 blocked hw3 neg1 hw0 diff2 diff5 diff6 "
+        "choose0 choose1 neg3 choose4 choose3 choose2 new0 choose6 choose5 new1")
+
+
+def plan(s):
+    out = (HEAD if s else FIRST).split()
+    spare = list(SPARE if s else SPARE0)
+    for t in ARRIVAL.split():
+        out += spare.pop(0).split() if t == "_" else [t]
+    return out + MOVE.split()
+
 
 SCRATCH = {
     "b16": ("sbuf", [128, W], "bfloat16"), "w16": ("sbuf", [128, W], "bfloat16"), "r16": ("sbuf", [128, W], "bfloat16"),
@@ -31,30 +43,29 @@ SCRATCH = {
     "bb": ("sbuf", [128, W], "float32"), "cc": ("sbuf", [128, W], "float32"), "ee": ("sbuf", [128, 5 * W + 16], "float32"),
     "br": ("sbuf", [128, W], "float32"), "hw": ("sbuf", [128, W], "float32"),
     "kw": ("sbuf", [128, 16], "float32"), "kz": ("sbuf", [128, K], "float32"), "k01": ("sbuf", [128, 2 * K], "float32"),
-    "uu": ("sbuf", [128, 160], "bfloat16"), "u16": ("sbuf", [128, 128], "bfloat16"), "u4": ("sbuf", [128, 144], "bfloat16"), "pi": ("sbuf", [128, 8], "int32"),
+    "uu": ("sbuf", [128, 176], "bfloat16"), "u16": ("sbuf", [128, 128], "bfloat16"), "u4": ("sbuf", [128, 144], "bfloat16"), "pi": ("sbuf", [128, 8], "int32"),
     "pf": ("sbuf", [128, 8], "float32"), "pg": ("sbuf", [128, 8], "float32"), "mq": ("sbuf", [128, 8], "float32"),
-    "mk0": ("sbuf", [128, 64], "float32"), "mk": ("sbuf", [128, 64], "float32"), "mv": ("sbuf", [128, 2 * K], "float32"),
+    "mk0": ("sbuf", [128, 64], "float32"), "mk": ("sbuf", [128, 64], "float32"), "mv": ("sbuf", [128, K], "float32"),
     "pat": ("sbuf", [128, 64], "bfloat16"), "kc": ("sbuf", [128, 64], "bfloat16"),
-    "sel": ("sbuf", [128, 160], "bfloat16"), "sl2": ("sbuf", [128, 160], "bfloat16"), "bd": ("sbuf", [128, 128], "bfloat16"), "idn": ("sbuf", [128, 128], "bfloat16"),
-    "cz": ("sbuf", [128, 144], "bfloat16"), "ex": ("sbuf", [128, 512], "bfloat16"), "zq": ("sbuf", [128, 4, 144], "float16"),
+    "sel": ("sbuf", [128, 160], "bfloat16"), "sl": ("sbuf", [128, 160], "bfloat16"), "bd": ("sbuf", [128, 128], "bfloat16"), "idn": ("sbuf", [128, 128], "bfloat16"),
+    "cz": ("sbuf", [128, 144], "bfloat16"), "ex": ("sbuf", [128, 2, 128], "bfloat16"), "zq": ("sbuf", [128, 4, 144], "bfloat16"), "ndn": ("sbuf", [128, 128], "bfloat16"),
+    "ds": ("sbuf", [128, 5, 176], "bfloat16"),
     "e0": ("sbuf", [128, 160], "float16"), "e1": ("sbuf", [128, 160], "float16"), "sh": ("sbuf", [128, 128], "float32"), "idf": ("sbuf", [128, 128], "float32"),
-    "wu": ("sbuf", [128, 16], "uint16"),
     "xg": ("sbuf", [128, K], "float16"), "yy": ("sbuf", [128, 8, 32], "float16"), "xu": ("sbuf", [128, 112], "uint16"),
-    "xh": ("sbuf", [128, 96], "float16"), "xi": ("sbuf", [128, 64], "uint16"),
-    "bo": ("sbuf", [128, K], "float32"), "dl": ("sbuf", [128, K], "float32"),
+    "xh": ("sbuf", [128, 96], "float16"), "xi": ("sbuf", [128, 64], "uint16"), "wu": ("sbuf", [128, 16], "uint16"),
+    "bo": ("sbuf", [128, K], "float32"), "dl": ("sbuf", [128, K], "float32"), "nb": ("sbuf", [128, W], "float32"),
     "hb": ("sbuf", [128, RO * HW], "float32"), "lu": ("sbuf", [128, RO * PW], "float32"), "ld": ("sbuf", [128, RO * PW], "float32"),
-    "gg": ("sbuf", [128, NB * K], "float32"), "ab": ("sbuf", [128, NB * K], "float32"), "rl": ("sbuf", [128, NB * K], "bfloat16"),
-    "ov": ("sbuf", [128, NB * K], "bfloat16"), "wx": ("sbuf", [128, NB * K], "float32"),
-    "mn": ("sbuf", [128, 64], "bfloat16"), "nz": ("sbuf", [128, K], "bfloat16"), "ss": ("sbuf", [128, K], "float32"),
-    "ac": ("sbuf", [128, K], "float32"), "cg": ("sbuf", [128, K], "float32"),
-    "aa": ("sbuf", [128, NK * K], "float32"), "eq": ("sbuf", [128, 16, 64], "bfloat16"), "idh": ("sbuf", [128, 2, 128], "float16"),
+    "gg": ("sbuf", [128, NB, K], "float32"), "ab": ("sbuf", [128, NB, K], "float32"), "rl": ("sbuf", [128, NB, K], "bfloat16"),
+    "ov": ("sbuf", [128, NB, K], "bfloat16"), "wx": ("sbuf", [128, NB, K], "float32"),
+    "mn": ("sbuf", [128, 64], "bfloat16"), "nz": ("sbuf", [128, K], "bfloat16"), "ss": ("sbuf", [128, K], "float32"), "ac": ("sbuf", [128, K], "float32"),
+    "aa": ("sbuf", [128, NK * K], "float32"), "eq": ("sbuf", [128, 64, 16], "bfloat16"),
     "ky": ("sbuf", [128, 64], "int32"), "ki": ("sbuf", [128, 32], "int32"), "eu": ("sbuf", [128, 16], "uint16"), "gl": ("sbuf", [128, 48], "uint16"),
     "gt": ("sbuf", [128, K, 4], "bfloat16"), "d1": ("sbuf", [128, 7, 64], "float32"), "sc": ("sbuf", [128, 5, 64], "float32"),
     "px": ("psum", [128, 32, 16], "float32"), "ps0": ("psum", [128, 512], "float32"), "ps1": ("psum", [128, 512], "float32"), "ph": ("psum", [128, 512], "float32"),
     "pr0": ("psum", [128, 512], "float32"), "pr1": ("psum", [128, 512], "float32"), "pw0": ("psum", [128, 512], "float32"), "pw1": ("psum", [128, 512], "float32"),
 }
 BANKS = ("px", "ps0", "ps1", "ph", "pr0", "pr1", "pw0", "pw1")
-SEMAPHORES = (["qg", "qv", "qa", "qp", "qs", "l_wk", "l_rec", "l_th", "l_tb", "l_b", "l_w", "st_b", "st_c"]
+SEMAPHORES = (["qg", "qv", "qa", "qp", "qs", "l_wk", "l_rec", "l_th", "l_tb", "l_b", "l_w", "st_b", "st_c", "add0", "add1", "add2", "add3"]
               + ["au%d" % s for s in range(RO)] + ["ad%d" % s for s in range(RO)] + ["sent%d" % s for s in range(RO)])
 A = AluOpType
 F = ActivationFunctionType
@@ -145,10 +156,10 @@ def rank_program(g, core, T, topo):
     if rank is None:
         return
     n = len(T.cores)
-    ops, tag = [], ["start"]
+    ops, at = [], ["start"]
 
     def op(q, fn, r, w, ev=None, dma=False, end=False):
-        ops.append({"tag": tag[0], "q": q, "fn": fn, "r": list(r), "w": list(w), "ev": ev, "dma": dma, "end": end})
+        ops.append({"stage": at[0], "q": q, "fn": fn, "r": list(r), "w": list(w), "ev": ev, "dma": dma, "end": end})
 
     def dma(q, out, in_, r, w, sem, val=16):
         op(q, lambda e: e.dma_start(out, in_), r, w, ev=(sem, val), dma=True)
@@ -188,21 +199,21 @@ def rank_program(g, core, T, topo):
             return ins
         op("p", fn, r, w)
 
-    vb = CFG["vb"]
     fill(T.kw[:], -200.0, ["kw"])
-    fill(T.tb[:], 0, ["tb0"])
+    fill(T.tb[:, 0:TV], 0, ["tb0"])
+    iota(T.pi[:, 0:2], [[16, 2]], 0, 1, ["pi0"], flt=False)
+    iota(T.tb[:, TV:W], [[0, W - TV]], 0, 0, ["tb1"], flt=False)
     dma("s", T.wki[:], T.wk[:], [], ["wki"], "l_wk")
     dma("a", T.b16[:], T.b0[:], [], ["b16"], "l_b")
     dma("s", T.r16[:], T.rec[:], [], ["r16"], "l_rec")
     dma("a", T.thr[:, 0:1], T.th[:], [], ["thr"], "l_th")
-    dma("s", T.tb[0:128:4, :], T.hop[:], ["tb0"], ["tbh"], "l_tb", 48)
-    dma("s", T.tb[2:128:16, :], T.up[:], ["tb0"], ["tbu"], "l_tb", 48)
-    dma("s", T.tb[6:128:16, :], T.dn[:], ["tb0"], ["tbd"], "l_tb", 48)
+    dma("s", T.tb[0:128:4, :], T.hop[:], ["tb0", "tb1"], ["tbh"], "l_tb", 48)
+    dma("s", T.tb[2:128:16, :], T.up[:], ["tb0", "tb1"], ["tbu"], "l_tb", 48)
+    dma("s", T.tb[6:128:16, :], T.dn[:], ["tb0", "tb1"], ["tbd"], "l_tb", 48)
     dma("s", T.w16[:], T.w[:], [], ["w16"], "l_w")
-    iota(T.pi[:, 0:2], [[16, 2]], 0, 1, ["pi0"], flt=False)
-    iota(T.uu[:], [[1, 160]], 0, 0, ["uu"])
+    iota(T.uu[:], [[1, 176]], -16, 0, ["uu"])
     iota(T.u16[:], [[16, 8], [0, 16]], 0, 0, ["u16"])
-    iota(T.u4[:], [[4, 36], [0, 4]], 0, 0, ["u4"])
+    iota(T.u4[:], [[4, 36], [0, 4]], -12, 0, ["u4"])
     iota(T.kz[:], [[0, K]], -200, 0, ["kz"])
     iota(T.hb[:, 0:HW], [[0, HW]], 0, 0, ["hb", "h0"])
     act(T.ee[:, 5 * W:5 * W + 16], T.kw[:], F.Sigmoid, ["kw"], ["eez"])
@@ -214,94 +225,77 @@ def rank_program(g, core, T, topo):
     cp(T.pf[:, 0:7], T.pi[:, 0:7], ["pi0", "pi2", "pi3", "pi4", "pi5", "pi6"], ["pf"])
     ts(T.pg[:, 0:1], T.pf[:, 3:4], 0.0625, None, A.mult, None, ["pf"], ["pg0"])
     ts(T.pg[:, 1:2], T.pf[:, 3:4], -0.0625, 1.0, A.mult, A.add, ["pf"], ["pg1"])
-    ts(T.pg[:, 2:3], T.pf[:, 2:3], 15.0, None, A.add, None, ["pf"], ["pg2"])
-    ts(T.pg[:, 3:4], T.pf[:, 2:3], 12.0, None, A.add, None, ["pf"], ["pg3"])
-    ts(T.bd[:], T.u16[:], T.pf[:, 2:3], None, A.is_equal, None, ["u16", "pf"], ["bd"])
-    ts(T.mq[:, 0:4], T.u4[:, 0:16:4], T.pf[:, 5:6], None, A.is_equal, None, ["u4", "pf"], ["mq"])
-    ts(T.e0[:], T.uu[:], T.pf[:, 1:2], T.pg[:, 1:2], A.is_equal, A.mult, ["uu", "pf", "pg1"], ["e0"])
-    ts(T.e1[:], T.uu[:], T.pf[:, 1:2], T.pg[:, 0:1], A.is_equal, A.mult, ["uu", "pf", "pg0"], ["e1"])
-    ts(T.idf[:], T.uu[:, 0:128], T.pf[:, 0:1], None, A.is_equal, None, ["uu", "pf"], ["idf"])
-    ts(T.cz[:], T.u4[:], T.pg[:, 3:4], None, A.is_equal, None, ["u4", "pg3"], ["cz"])
+    ts(T.e0[:], T.uu[:, 0:160], T.pf[:, 0:1], T.pg[:, 1:2], A.is_equal, A.mult, ["uu", "pf", "pg1"], ["e0"])
+    ts(T.e1[:], T.uu[:, 0:160], T.pf[:, 0:1], T.pg[:, 0:1], A.is_equal, A.mult, ["uu", "pf", "pg0"], ["e1"])
+    ts(T.mq[:, 0:2], T.u4[:, 12:20:4], T.pf[:, 5:6], None, A.is_equal, None, ["u4", "pf"], ["mq"])
+    ts(T.mq[:, 2:6], T.uu[:, 16:20], T.pf[:, 6:7], None, A.is_equal, None, ["uu", "pf"], ["mr"])
     cp(T.xu[:, 0:16], T.wki[:], ["wki"], ["du"])
-    for q in range(4):
-        ts(T.ex[:, 128 * q:128 * q + 128], T.u16[:], T.pf[:, 2:3], T.mq[:, q:q + 1], A.is_equal, A.mult, ["u16", "pf", "mq"], ["ex%d" % q])
-    ts(T.sh[:], T.uu[:, 0:128], T.pf[:, 4:5], None, A.is_equal, None, ["uu", "pf"], ["sh"])
-    ts(T.nth[:, 0:1], T.thr[:, 0:1], -1.0, None, A.mult, None, ["thr"], ["nth"])
-    if vb:
-        cp(T.bb[:, 0:vb], T.b16[:, 0:vb], ["b16"], ["bbv"])
 
-    def quarters():
-        ts(T.mq[:, 4:8], T.uu[:, 0:4], T.pf[:, 6:7], None, A.is_equal, None, ["uu", "pf"], ["mr"])
-        ts(T.pg[:, 4:5], T.pf[:, 0:1], 3.0, None, A.add, None, ["pf"], ["pg4"])
+    far = ((T.uu[:], "uu", 0), (T.u16[:], "u16", 2), (T.uu[:, 1:161], "uu", 2), (T.u4[:], "u4", 2), (T.uu[:, 16:144], "uu", 4))
+
+    def distance(i):
+        row, rn, col = far[i]
+        act(T.ds[:, i, 0:row.shape[1]], row, F.Abs, [rn, "pf"], ["ds%d" % i], scale=-1.0, bias=T.pf[:, col:col + 1])
+
+    def match(out, on, i, c0, one=1.0, r=()):
+        act(out, T.ds[:, i, c0:c0 + out.shape[1]], F.Relu, ["ds%d" % i] + list(r), [on], scale=-one if r == () else -1.0, bias=one)
 
     def pattern():
-        for k, (cols, v) in enumerate(((T.pat[:, 0:64:4], 0.0), (T.pat[:, 1:64:4], 1.0), (T.pat[:, 2:32:4], 1.0), (T.pat[:, 34:64:4], 0.5), (T.pat[:, 3:64:4], 0.5))):
-            fill(cols, v, ["pat%d" % k])
+        for k, (c0, c1, v) in enumerate(((0, 64, 0.0), (1, 64, 1.0), (2, 32, 1.0), (34, 64, 0.5), (3, 64, 0.5))):
+            act(T.pat[:, c0:c1:4], T.kz[:, c0:c1:4], F.Identity, ["kz"], ["pat%d" % k], scale=0.0, bias=v)
 
-    def widen(name, src, sn):
+    def to_psum(name, src, sn):
         for j in range(2):
             mms([(T["%s%d" % (name, j)][:], T.idn[:], src[:, 512 * j:512 * j + 512], True, True)], ["idn", sn], ["%s%d" % (name, j)])
 
     late = {
-        "kidn": lambda: ts(T.idn[:], T.uu[:, 0:128], T.pf[:, 0:1], None, A.is_equal, None, ["uu", "pf"], ["idn"]),
-        "kh": lambda i: ts(T.idh[:, i, :], T.uu[:, 0:128], T.pf[:, 0:1], 1.0 - 2 * i, A.is_equal, A.mult, ["uu", "pf"], ["idh%d" % i]),
-        "kpr": lambda: widen("pr", T.r16, "r16"), "kpw": lambda: widen("pw", T.w16, "w16"), "kq": quarters,
-        "kz": lambda r: ts(T.zq[:, r, :], T.uu[:, 0:144], T.pg[:, 4:5], T.mq[:, 4 + r:5 + r], A.is_equal, A.mult, ["uu", "pg4", "mr"], ["zq%d" % r]),
-        "ksel": lambda: ts(T.sel[:], T.uu[:], T.pg[:, 2:3], 4096.0, A.is_equal, A.mult, ["uu", "pg2"], ["sel"]),
-        "ksl": lambda _: ts(T.sl2[:], T.uu[:], T.pg[:, 2:3], -0.03125, A.is_equal, A.mult, ["uu", "pg2"], ["sl2"]),
-        "kgt": lambda: fill(T.gt[:, :, 0], 0.0, ["gtz"]),
-        "kmk": lambda: ts(T.mk[:], T.mk0[:], 1.0, None, A.min, None, ["mk0"], ["mk"]), "kpat": pattern}
+        "ds": distance, "idf": lambda: match(T.idf[:], "idf", 0, 16), "idn": lambda: match(T.idn[:], "idn", 0, 16),
+        "zq": lambda r: match(T.zq[:, r, :], "zq%d" % r, 0, 13, T.mq[:, 2 + r:3 + r], ["mr"]),
+        "bd": lambda: match(T.bd[:], "bd", 1, 0), "ex": lambda q: match(T.ex[:, q, :], "ex%d" % q, 1, 0, T.mq[:, q:q + 1], ["mq"]),
+        "sel": lambda: match(T.sel[:], "sel", 2, 0, 4096.0), "cz": lambda: match(T.cz[:], "cz", 3, 0), "sh": lambda: match(T.sh[:], "sh", 4, 0),
+        "sl": lambda: act(T.sl[:], T.sel[:], F.Copy, ["sel"], ["sl"], scale=-2.0 ** -17),
+        "less": lambda: act(T.ndn[:], T.idn[:], F.Copy, ["idn"], ["ndn"], scale=-1.0),
+        "nth": lambda: act(T.nth[:, 0:1], T.thr[:, 0:1], F.Copy, ["thr"], ["nth"], scale=-1.0),
+        "gtz": lambda: act(T.gt[:, :, 0], T.kz[:], F.Copy, ["kz"], ["gtz"], scale=0.0),
+        "mask": lambda: act(T.mk[:], T.mk0[:], F.Sign, ["mk0"], ["mk"]), "pat": pattern,
+        "recp": lambda: to_psum("pr", T.r16, "r16"), "wp": lambda: to_psum("pw", T.w16, "w16"),
+        "widev": lambda: cp(T.bb[:, 0:VB], T.b16[:, 0:VB], ["b16"], ["bbv"])}
 
     dst, eng = neighbours(T, topo, rank)
     n_up = len(neighbours(T, topo, (rank - 1) % n)[1][0])
     n_dn = len(neighbours(T, topo, (rank + 1) % n)[1][1])
-    UP, DN = NK, NK + 1
-    PARTS = [(0, CFG["cut"]), (CFG["cut"], 16)]
-    CH = CFG["ch"]
+    du = T.xu[:, 0:16]
+    brs, nbs = ["br%d" % j for j in range(4)], ["nb%d" % j for j in range(4)]
+
+    def xl(a, c0=0, c1=16):
+        return T.xu[:, 16 + 16 * a + c0:16 + 16 * a + c1]
 
     for s in range(RO):
         last = s == RO - 1
-        du, dun = T.xu[:, 0:16], "du"
         hb0 = HW * s
         h, hn = T.hb[:, hb0 + LW:hb0 + LW + K], "h%d" % s
         lu, ld = T.lu[:, PW * s:PW * s + PW], T.ld[:, PW * s:PW * s + PW]
-        brs, hws = ["br%d" % j for j in range(4)], ["hw%d" % j for j in range(4)]
-
-        def buf(t, a):
-            return t[:, K * (a % NB):K * (a % NB) + K]
-
-        def xl(a, c0=0, c1=16):
-            return T.xu[:, 16 + 16 * a + c0:16 + 16 * a + c1]
-
-        def old_b():
-            act(T.bo[:], T.b16[:].indirect(du), F.Copy, ["b16", dun], ["bo"], scale=-1.0)
-
-        def delta():
-            if s == 0:
-                tt(T.dl[:], T.r16[:].indirect(du), T.bo[:], A.mult, ["r16", dun, "bo"], ["dl"])
-            else:
-                act(T.dl[:], T.br[:].indirect(du), F.Copy, brs + [dun], ["dl"], scale=-1.0)
 
         def make_h():
             if s == 0:
-                tt(h, T.w16[:].indirect(du), T.dl[:], A.mult, ["w16", dun, "dl"], [hn])
+                tt(h, T.w16[:].indirect(du), T.dl[:], A.mult, ["w16", "du", "dl"], [hn])
             else:
-                ts(h, T.hw[:].indirect(du), -1.0, None, A.mult, None, hws + [dun], [hn])
+                ts(h, T.hw[:].indirect(du), -1.0, None, A.mult, None, ["hw0", "hw1", "hw2", "hw3", "du"], [hn])
 
         def tables(lst, ln):
             cp(T.xg[:], T.tb[:].indirect(lst), ["tb0", "tbh", "tbu", "tbd", ln], ["xg"])
 
-        def to_lists(less=False):
+        def to_lists(less):
             if less:
-                mms([(T.px[:, 0:16, c], T.idh[:, 1, :], T.xh[:, 16 * (t % 6):16 * (t % 6) + 16], t == 0, False) for t, c in enumerate(COL + (5,))],
-                    ["idh1", "xh"], ["px.a"])
+                mms([(T.px[:, 0:16, c], T.ndn[:], T.xh[:, 16 * (t % 6):16 * (t % 6) + 16], t == 0, False) for t, c in enumerate(COL + (5,))],
+                    ["ndn", "xh"], ["px.a"])
             op("v", lambda e: e.transpose(T.yy[:], T.xg[:]), ["xg"], ["yy"])
             mms([(T.px[:, 0:16:2, 0:7], T.e0[:, 16:144], T.yy[:, :, 0:14:2], not less, False),
                  (T.px[:, 0:16:2, 0:7], T.e0[:, 0:128], T.yy[:, :, 16:30:2], False, False),
                  (T.px[:, 1:16:2, 0:7], T.e1[:, 32:160], T.yy[:, :, 0:14:2], False, False),
                  (T.px[:, 1:16:2, 0:7], T.e1[:, 16:144], T.yy[:, :, 16:30:2], False, True)], ["yy", "e0", "e1"], ["px.a"])
 
-        def payload_lists():
+        def payload():
             act(T.hb[:, hb0 + 3:hb0 + LW:4], T.px[:, 0:16, COL[UP]], F.Copy, ["px.a", "hb"], [hn + "u"])
             act(T.hb[:, hb0 + LW + K + 3:hb0 + HW:4], T.px[:, 0:16, COL[DN]], F.Copy, ["px.a", "hb"], [hn + "d"])
 
@@ -316,27 +310,27 @@ def rank_program(g, core, T, topo):
             op("g", None, ["sd%d" % s], ["lu%d" % s], ev=("au%d" % s, n_up))
             op("g", None, ["sd%d" % s], ["ld%d" % s], ev=("ad%d" % s, n_dn))
             if s == 0:
+                iota(T.d1[:], [[0, 7], [0, 64]], 0, 0, ["d1"])
                 iota(T.cc[:], [[0, W]], 0, 0, ["cc"])
                 iota(T.mk0[:], [[0, 16], [1, 4]], 0, 0, ["mk0"])
                 iota(T.kc[:], [[0, 16], [-W, NK]], (NK - 1) * W, 0, ["kc"])
-                iota(T.d1[:], [[0, 7], [0, 64]], 0, 0, ["d1"])
-                iota(T.mv[:], [[0, 128], [4096, 4]], 0, 0, ["mv"])
+                iota(T.mv[:], [[0, 64], [4096, 4]], 0, 0, ["mv"])
                 iota(T.k01[:], [[200, 2], [0, K]], 0, 0, ["k01"])
                 for m in (4, 3, 2, 1, 0):
                     iota(T.ee[:, m * W:(m + 1) * W], [[0, W]], 0, 0, ["ee%d" % m])
 
-        def cscat(i):
-            lst, dl = T.xu[:, 4 * i:4 * i + 4], T.dl[:, 64 * i:64 * i + 64]
-            if s == 0:
-                cp(T.cc[:].indirect(lst), dl, ["dl", dun], ["cc"])
-            else:
-                tt(T.cc[:].indirect(lst), T.cg[:, 64 * i:64 * i + 64], dl, A.add, ["cg", "dl", dun], ["cc"])
-            if last and i == 3:
+        def first_c(i):
+            cp(T.cc[:].indirect(T.xu[:, 4 * i:4 * i + 4]), T.dl[:, 64 * i:64 * i + 64], ["dl", "du"], ["cc"])
+            if i == 3:
                 dma("s", T.yc[:], T.cc[:], ["cc"], ["yc"], "st_c")
+
+        def grow_c():
+            op("g", lambda e: e.dma_start(T.nb[:], T.br[:], accum_op=A.add), brs + ["sd%d" % s], nbs, ev=("add%d" % (2 * s - 2), 16), dma=True)
+            op("g", lambda e: e.dma_start(T.yc[:], T.nb[:], accum_op=A.add), nbs, ["yc"], ev=("add%d" % (2 * s - 1), 16), dma=True)
 
         def xlist(a):
             if a < NK:
-                cp(xl(a), T.px[:, 0:16, 2 * a], ["px.a"], ["x%d" % a])
+                cp(xl(a), T.px[:, 0:16, COL[a]], ["px.a"], ["x%d" % a])
             elif a == UP:
                 mms([(T.px[:, 16, :], T.sh[:], lu[:, 3:LW:4], True, True)], ["sh", "lu%d" % s], ["px.l"])
                 cp(xl(a), T.px[:, 16, :], ["px.l"], ["x4"])
@@ -352,117 +346,80 @@ def rank_program(g, core, T, topo):
                 mms([(T.ph[:, 0:K], T.idf[:], ld[:, 0:K], True, True)], ["idf", "ld%d" % s], ["ph.0"])
 
         def weights(a):
-            act(buf(T.wx, a), T.w16[:].indirect(xl(a)), F.Copy, ["w16", "x%d" % a], ["wx%d" % (a % NB)])
+            act(T.wx[:, a % NB, :], T.w16[:].indirect(xl(a)), F.Copy, ["w16", "x%d" % a], ["wx%d" % (a % NB)])
 
         def grad(a):
             i = int(a == UP)
-            tt(buf(T.gg, a), buf(T.wx, a), T.ph[:, K * i:K * i + K], A.mult, ["wx%d" % (a % NB), "ph.%d" % i], ["g%d" % (a % NB)])
+            tt(T.gg[:, a % NB, :], T.wx[:, a % NB, :], T.ph[:, K * i:K * i + K], A.mult, ["wx%d" % (a % NB), "ph.%d" % i], ["g%d" % (a % NB)])
 
         def grad_gather(a):
-            tt(buf(T.gg, a), T.w16[:].indirect(xl(a)), h if a < NK else ld[:, 0:K], A.mult, ["w16", "x%d" % a, hn if a < NK else "ld%d" % s], ["g%d" % (a % NB)])
+            tt(T.gg[:, a, :], T.w16[:].indirect(xl(a)), h, A.mult, ["w16", "x%d" % a, hn], ["g%d" % a])
 
         def size(a):
-            act(buf(T.ab, a), buf(T.gg, a), F.Abs, ["g%d" % (a % NB)], ["ab%d" % (a % NB)])
+            act(T.ab[:, a % NB, :], T.gg[:, a % NB, :], F.Abs, ["g%d" % (a % NB)], ["ab%d" % (a % NB)])
 
         def excess(a):
-            act(buf(T.rl, a), buf(T.ab, a), F.Relu, ["ab%d" % (a % NB), "nth"], ["rl%d" % (a % NB)], bias=T.nth[:, 0:1])
+            act(T.rl[:, a % NB, :], T.ab[:, a % NB, :], F.Relu, ["ab%d" % (a % NB), "nth"], ["rl%d" % (a % NB)], bias=T.nth[:, 0:1])
 
         def over(a):
-            ts(buf(T.ov, a), buf(T.ab, a), T.thr[:, 0:1], None, A.is_gt, None, ["ab%d" % (a % NB), "thr"], ["ov%d" % (a % NB)])
-
-        def over_excess(a):
-            ts(buf(T.ov, a), buf(T.rl, a), 0.0, None, A.is_gt, None, ["rl%d" % (a % NB)], ["ov%d" % (a % NB)])
-
-        def sign_excess(a):
-            act(buf(T.ov, a), buf(T.rl, a), F.Sign, ["rl%d" % (a % NB)], ["ov%d" % (a % NB)])
+            act(T.ov[:, a % NB, :], T.rl[:, a % NB, :], F.Sign, ["rl%d" % (a % NB)], ["ov%d" % (a % NB)])
 
         def count(a):
-            mms([(T.px[:, 17:21, :], T.cz[:, 12 - 4 * q:140 - 4 * q], buf(T.ov, a)[:, 64 * q:64 * q + 64], q == 0, q == 3) for q in range(4)],
+            mms([(T.px[:, 17:21, :], T.cz[:, 12 - 4 * q:140 - 4 * q], T.ov[:, a % NB, 64 * q:64 * q + 64], q == 0, q == 1) for q in range(2)],
                 ["cz", "ov%d" % (a % NB)], ["px.c"])
 
         def strong(a):
             act(T.mn[:], T.px[:, 17:21, :], F.Relu, ["px.c"], ["mn"], bias=-8.0)
 
         def spread(a):
-            for i, (c0, c1) in enumerate(PARTS):
-                ps, items = T["ps%d" % i], []
-                for q in range(4):
-                    lo, hi = max(16 * c0, 64 * q), min(16 * c1, 64 * q + 64)
-                    if lo < hi:
-                        items.append((ps[:, lo - 16 * c0:hi - 16 * c0], T.ex[:, 128 * q:128 * q + 128], T.mn[:, lo - 64 * q:hi - 64 * q], not items, False))
-                mms(items, ["mn"] + ["ex%d" % q for q in range(4)], ["ps%d" % i])
+            mms([(T.ps0[:, 64 * q:64 * q + 64], T.ex[:, q, :], T.mn[:], q == 0, False) for q in range(2)], ["mn", "ex0", "ex1"], ["ps0"])
 
-        def held(a, i):
-            c0, c1 = PARTS[i]
-            act(T.nz[:, 16 * c0:16 * c1], T.bb[:].indirect(xl(a, c0, c1)), F.Abs, ["bb", "x%d" % a], ["nz%d" % i])
-            mms([(T["ps%d" % i][:, 0:16 * (c1 - c0)], T.bd[:], T.nz[:, 16 * c0:16 * c1], False, True)], ["bd", "nz%d" % i], ["ps%d" % i])
+        def count_rest(a):
+            mms([(T.ps1[:, 0:K - KS], T.bd[:], T.ov[:, a % NB, KS:K], True, False)], ["bd", "ov%d" % (a % NB)], ["ps1"])
+
+        def filled_s(a):
+            act(T.nz[:, 0:KS], T.bb[:].indirect(xl(a, 0, KS // 16)), F.Abs, ["bb", "x%d" % a], ["nz0"])
+            mms([(T.ps0[:, 0:KS], T.bd[:], T.nz[:, 0:KS], False, True)], ["bd", "nz0"], ["ps0"])
+
+        def filled_v(a):
+            ts(T.nz[:, KS:K], T.bb[:].indirect(xl(a, KS // 16, 16)), 0.0, 16.0, A.not_equal, A.mult, ["bb", "x%d" % a], ["nz1"])
+            mms([(T.ps1[:, 0:K - KS], T.bd[:], T.nz[:, KS:K], False, True)], ["bd", "nz1"], ["ps1"])
 
         def total(a):
-            tt(T.ss[:], T.bb[:].indirect(xl(a)), buf(T.gg, a), A.add, ["bb", "x%d" % a, "g%d" % (a % NB)], ["ss"])
+            tt(T.ss[:], T.bb[:].indirect(xl(a)), T.gg[:, a % NB, :], A.add, ["bb", "x%d" % a, "g%d" % (a % NB)], ["ss"])
 
-        def accept(i):
-            c0, c1 = PARTS[i]
-            act(T.ac[:, 16 * c0:16 * c1], T["ps%d" % i][:, 0:16 * (c1 - c0)], F.Sign, ["ps%d" % i], ["ac%d" % i])
-
-        def put(a, i):
-            c0, c1 = PARTS[i]
-            tt(T.bb[:].indirect(xl(a, c0, c1)), T.ss[:, 16 * c0:16 * c1], T.ac[:, 16 * c0:16 * c1], A.mult, ["ss", "x%d" % a, "ac%d" % i], ["bb"])
-
-        def held_first(a):
-            act(T.nz[:], T.bb[:].indirect(xl(a)), F.Abs, ["bb", "x%d" % a], ["nz0", "nz1"], scale=BIG)
-            mms([(T["ps%d" % a][:, 0:K], T.bd[:], T.nz[:], a == 0, a != 0)], ["bd", "nz0", "nz1"], ["ps%d" % a])
-
-        def sum_first(a):
-            mms([(T["ps%d" % a][:, 0:K], T.bd[:], buf(T.ov, a), a != 0, a == 0)], ["bd", "ov%d" % (a % NB)], ["ps%d" % a])
-
-        def over_first(a):
-            ts(buf(T.ov, a), buf(T.ab, a), T.thr[:, 0:1], TINY, A.is_gt, A.mult, ["ab%d" % (a % NB), "thr"], ["ov%d" % (a % NB)])
-
-        def excess_first(a):
-            ts(buf(T.ov, a), buf(T.rl, a), 0.0, TINY, A.is_gt, A.mult, ["rl%d" % (a % NB)], ["ov%d" % (a % NB)])
-
-        def both_sides(a):
-            ts(buf(T.ov, a), buf(T.gg, a), T.thr[:, 0:1], TINY, A.is_gt, A.mult, ["g%d" % (a % NB), "thr"], ["ov%d" % (a % NB)])
-            ts(buf(T.rl, a), buf(T.gg, a), T.nth[:, 0:1], TINY, A.is_lt, A.mult, ["g%d" % (a % NB), "nth"], ["rl%d" % (a % NB)])
-
-        def sum_both(a):
-            mms([(T.ps0[:, 0:K], T.bd[:], buf(T.ov, a), False, False)], ["bd", "ov%d" % (a % NB)], ["ps0"])
-            mms([(T.ps0[:, 0:K], T.bd[:], buf(T.rl, a), False, True)], ["bd", "rl%d" % (a % NB)], ["ps0"])
-
-        def accept_first(a):
-            ts(T.ac[:], T["ps%d" % a][:, 0:K], 8.5 * TINY, None, A.is_gt, None, ["ps%d" % a], ["ac0", "ac1"])
-
-        def put_first(a):
+        def put(a):
             tt(T.bb[:].indirect(xl(a)), T.ss[:], T.ac[:], A.mult, ["ss", "x%d" % a, "ac0", "ac1"], ["bb"])
 
+        def size_first(a):
+            act(T.nz[:], T.bb[:].indirect(xl(a)), F.Abs, ["bb", "x%d" % a], ["nz0", "nz1"], scale=BIG)
+            mms([(T.ps0[:, 0:K], T.bd[:], T.nz[:], True, False)], ["bd", "nz0", "nz1"], ["ps0"])
+
+        def both_sides(a):
+            ts(T.ov[:, a, :], T.gg[:, a, :], T.thr[:, 0:1], TINY, A.is_gt, A.mult, ["g0", "thr"], ["ov0"])
+            ts(T.rl[:, a, :], T.gg[:, a, :], T.nth[:, 0:1], TINY, A.is_lt, A.mult, ["g0", "nth"], ["rl0"])
+
+        def count_both(a):
+            mms([(T.ps0[:, 0:K], T.bd[:], T.ov[:, a, :], False, False)], ["bd", "ov0"], ["ps0"])
+            mms([(T.ps0[:, 0:K], T.bd[:], T.rl[:, a, :], False, True)], ["bd", "rl0"], ["ps0"])
+
+        def over_tiny(a):
+            b = a % NB
+            ts(T.ov[:, b, :], T.ab[:, b, :], T.thr[:, 0:1], TINY, A.is_gt, A.mult, ["ab%d" % b, "thr"], ["ov%d" % b])
+            mms([(T.ps0[:, 0:K], T.bd[:], T.ov[:, b, :], True, False)], ["bd", "ov%d" % b], ["ps0"])
+
+        def part_v(a):
+            ts(T.nz[:, KS:K], T.bb[:].indirect(xl(a, KS // 16, 16)), 0.0, None, A.not_equal, None, ["bb", "x%d" % a], ["nz1"])
+            mms([(T.ps0[:, KS:K], T.bd[:], T.nz[:, KS:K], False, False)], ["bd", "nz1"], ["ps0"])
+
+        def part_s(a):
+            act(T.nz[:, 0:KS], T.bb[:].indirect(xl(a, 0, KS // 16)), F.Abs, ["bb", "x%d" % a], ["nz0"], scale=BIG)
+            mms([(T.ps0[:, 0:KS], T.bd[:], T.nz[:, 0:KS], False, True)], ["bd", "nz0"], ["ps0"])
+
         pk, pt = T.ps1[:, K:K + 64], T.ps1[:, K + 64:K + 128]
-        kin = T.k01[:, K * s:K * s + K] if not last else None
+        mark = T.k01[:, K * (s % 2):K * (s % 2) + K]
         ee03, ee14 = ["ee0", "ee1", "ee2", "ee3"], ["ee1", "ee2", "ee3", "ee4", "eez"]
         win, lev = T.ee[:, W:5 * W + 16], 0.25 + 0.5 * s
-
-        def interleave():
-            for r in range(4):
-                mms([(T.px[:, 21:25, r:16:4], T.zq[:, r, 3 + r - k:131 + r - k], T.xh[:, 16 * k:16 * k + 16], k == 0, k == 3) for k in range(NK)],
-                    ["xh", "zq%d" % r], ["px.i"])
-
-        def top(i):
-            c0, c1 = CH[i]
-            return (T.ph, T.ps0)[i % 2][:, 0:64 * (c1 - c0)], ("ph.0", "ps0")[i % 2]
-
-        def largest(i):
-            c0, c1 = CH[i]
-            pm, pn = top(i)
-            scan(pm, T.mv[:, 0:64 * (c1 - c0)], T.aa[:, 64 * c0:64 * c1], A.min, A.max, ["mv", "a%d" % i], [pn] + ["ph.1"] * (i % 2 == 0))
-
-        def vote(i):
-            c0, c1 = CH[i]
-            pm, pn = top(i)
-            for k in range(NK):
-                tt(T.eq[:, c0:c1, k:64:4], T.aa[:, 64 * c0 + k:64 * c1:4], pm[:, 3:64 * (c1 - c0):4], A.is_equal, ["a%d" % i, pn], ["eq%d%d" % (k, i)])
-
-        def count_votes():
-            mms([(pk, T.sel[:, 15 - i:143 - i], T.eq[:, :, 16 * (i % 4) + 4 * (i // 4):16 * (i % 4) + 4 * (i // 4) + 4], False, i == 15) for i in range(16)],
-                ["sel"] + ["eq%d%d" % (k, i) for k in range(NK) for i in range(len(CH))], ["ps1"])
 
         def stay(i):
             if i == 0:
@@ -471,68 +428,98 @@ def rank_program(g, core, T, topo):
                 c0 = hb0 + (i - 1) * (LW + K)
                 act(T.d1[:, 4 + i, 3:64:4], T.hb[:, c0 + 3:c0 + LW:4], F.Copy, [hn + "ud"[i - 1], "d1"], ["old%d" % i])
 
-        def choose(t):
-            c0 = hb0 + HW + (t - 5) * (LW + K)
-            out, on = (T.sc[:, t, :], "sc%d" % t) if t < 5 else (T.hb[:, c0:c0 + LW], "h%d%s" % (s + 1, "ud"[t - 5]))
-            scan(out, pt, T.d1[:, t, :], A.mult, A.add, ["ps1", "dif%d" % t, "old%d" % max(0, t - 4)], [on])
+        def weave():
+            for r in range(4):
+                mms([(T.px[:, 21 + r, :], T.zq[:, r, 3 + r - k:131 + r - k], T.xh[:, 16 * k:16 * k + 16], k == 0, k == 3) for k in range(NK)],
+                    ["xh", "zq%d" % r], ["px.i"])
+
+        def top(r):
+            scan(T.ph[:, K * (r % 2):K * (r % 2) + K], T.mv[:], T.aa[:, K * r:K * r + K], A.min, A.max, ["mv", "a%d" % r], ["ph.%d" % (r % 2)])
+
+        def vote(r):
+            for k in range(NK):
+                tt(T.eq[:, 16 * r:16 * r + 16, k:16:4], T.aa[:, K * r + k:K * r + K:4], T.ph[:, K * (r % 2) + 3:K * (r % 2) + K:4], A.is_equal,
+                   ["a%d" % r, "ph.%d" % (r % 2)], ["eq%d%d" % (k, r)])
+
+        def keys():
+            mms([(pk, T.idn[:], T.kc[:], True, False)] + [(pk[:, k:64:4], T.idn[:], T.xh[:, 16 * k:16 * k + 16], False, False) for k in range(NK)],
+                ["idn", "xh", "kc"], ["ps1"])
+
+        def tally(r):
+            mms([(pk, T.sel[:, 15 - 4 * q - r:143 - 4 * q - r], T.eq[:, 16 * r:16 * r + 16, 4 * q:4 * q + 4], False, r == 3 and q == 3) for q in range(4)],
+                ["sel"] + ["eq%d%d" % (k, r) for k in range(NK)], ["ps1"])
 
         def dense(j, out, on, in0, in0n, ps):
             tt(out[:, K * j:K * j + K], in0[:, K * j:K * j + K], T["%s%d" % (ps, j // 2)][:, K * (j % 2):K * (j % 2) + K], A.mult,
                [in0n, "%s%d" % (ps, j // 2)], ["%s%d" % (on, j)])
 
-        def lookups():
+        def sections():
             for m in range(3):
                 ts(T.gl[:, 16 * m:16 * m + 16], T.ki[:, 0:16], float(m * W), float(ZC), A.add, A.min, ["ki1"], ["gl%d" % m])
 
-        def look_v(i):
+        def see_v(i):
             out, lst = ((T.gt[:, :, 1], T.gl[:, 0:16]), (T.gt[:, 0:128, 2], T.gl[:, 16:24]))[i]
             ts(out, win.indirect(lst), lev, 2.0, A.is_gt, A.mult, ee14 + ["gl%d" % i], ["gt%d" % i])
 
-        def look_s(i):
+        def see_s(i):
             out, lst = ((T.gt[:, 128:K, 2], T.gl[:, 24:32]), (T.gt[:, :, 3], T.gl[:, 32:48]))[i]
             act(out, win.indirect(lst), F.Sign, ee14 + ["gl%d" % (i + 1)], ["gt%d" % (i + 2)], bias=-lev)
 
+        def blocked():
+            mms([(pt, T.sl[:, 15 - i:143 - i], T.gt[:, i:K:16, :], False, i == 15) for i in range(16)], ["sl", "gtz", "gt0", "gt1", "gt2", "gt3"], ["ps1"])
+
+        def choose(t):
+            c0 = hb0 + HW + (t - 5) * (LW + K)
+            out, on = (T.sc[:, t, :], "sc%d" % t) if t < 5 else (T.hb[:, c0:c0 + LW], "h%d%s" % (s + 1, "ud"[t - 5]))
+            scan(out, pt, T.d1[:, t, :], A.mult, A.add, ["ps1", "dif%d" % t, "old%d" % max(0, t - 4)], [on])
+
+        def new_lists(i):
+            t0, t1 = ((0, 2), (2, 5))[i]
+            cp(T.xu[:, 16 * t0:16 * t1], T.sc[:, t0:t1, 3:64:4], ["sc%d" % t for t in range(t0, t1)], ["du", "x0", "x1", "x2", "x3"][t0:t1])
+
         stage = {
-            "bo": old_b, "cv": lambda: act(T.bb[:, vb:W], T.b16[:, vb:W], F.Copy, ["b16"], ["bb"]),
-            "zs": lambda: act(T.bb[:].indirect(du), T.kz[:], F.Sigmoid, ["kz", dun, "bbv"], ["bb"]),
-            "xg": lambda: tables(du, dun), "yy": to_lists, "dl": delta, "h": make_h, "hl": payload_lists, "tx": send,
-            "cg": lambda: act(T.cg[:], T.cc[:].indirect(du), F.Copy, ["cc", dun], ["cg"]), "c": cscat,
-            "L": xlist, "H": h_psum, "W": weights, "G": grad, "g": grad_gather, "B": size, "R": excess, "O": over, "o": over_excess, "s": sign_excess,
-            "C": count, "M": strong, "X": spread, "N": lambda a: held(a, 0), "n": lambda a: held(a, 1), "S": total,
-            "A": lambda a: accept(0), "a": lambda a: accept(1), "P": lambda a: put(a, 0), "p": lambda a: put(a, 1),
-            "Z": held_first, "Q": sum_first, "T": over_first, "t": excess_first, "D": both_sides, "q": sum_both, "V": accept_first, "U": put_first}
+            "oldb": lambda: act(T.bo[:], T.b16[:].indirect(du), F.Copy, ["b16", "du"], ["bo"], scale=-1.0),
+            "widen": lambda: act(T.bb[:, VB:W], T.b16[:, VB:W], F.Copy, ["b16"], ["bb"]),
+            "zero": lambda: act(T.bb[:].indirect(du), T.kz[:], F.Sigmoid, ["kz", "du", "bbv"], ["bb"]),
+            "tables": lambda: tables(du, "du"), "lists": lambda: to_lists(False), "h": make_h, "payload": payload, "send": send,
+            "delta": lambda: tt(T.dl[:], T.r16[:].indirect(du), T.bo[:], A.mult, ["r16", "du", "bo"], ["dl"]), "c": first_c,
+            "zbr": lambda: act(T.br[:].indirect(du), T.kz[:], F.Sigmoid, ["kz", "du"], brs), "grow": grow_c,
+            "list": xlist, "hps": h_psum, "wx": weights, "grad": grad, "gath": grad_gather, "abs": size, "exc": excess, "over": over,
+            "count": count, "strong": strong, "spread": spread, "rest": count_rest, "nzs": filled_s, "nzv": filled_v, "sum": total, "put": put,
+            "oks": lambda a: act(T.ac[:, 0:KS], T.ps0[:, 0:KS], F.Sign, ["ps0"], ["ac0"]),
+            "okv": lambda a: ts(T.ac[:, KS:K], T.ps1[:, 0:K - KS], 8.5, None, A.is_gt, None, ["ps1"], ["ac1"]),
+            "size": size_first, "both": both_sides, "counts": count_both, "partv": part_v, "tiny": over_tiny, "parts": part_s,
+            "ok": lambda a: ts(T.ac[:], T.ps0[:, 0:K], 8.5 * TINY, None, A.is_gt, None, ["ps0"], ["ac0", "ac1"])}
         move = {
-            "xh": lambda: cp(T.xh[:], T.d1[:, 1:7, 3:64:4], ["old0", "old1", "old2"], ["xh"]), "il": interleave,
-            "xi": lambda: cp(T.xi[:], T.px[:, 21:25, :], ["px.i"], ["xi"]),
-            "pk": lambda: mms([(pk, T.idn[:], T.kc[:], True, False)] + [(pk[:, k:64:4], T.idh[:, 0, :], T.xh[:, 16 * k:16 * k + 16], False, False) for k in range(NK)],
-                              ["idh0", "idn", "xh", "kc"], ["ps1"]),
-            "va": lambda i: act(T.aa[:, 64 * CH[i][0]:64 * CH[i][1]], T.bb[:].indirect(T.xi[:, 4 * CH[i][0]:4 * CH[i][1]]), F.Abs, ["bb", "xi"], ["a%d" % i]),
-            "em": lambda m: act(T.ee[:, m * W:(m + 1) * W].indirect(du), kin, F.Sigmoid, ["k01", dun], ["ee%d" % m]),
-            "df": stay, "vm": largest, "ve": vote, "un": count_votes,
-            "dr": lambda j: dense(j, T.br, "br", T.bb, "bb", "pr"), "dh": lambda j: dense(j, T.hw, "hw", T.br, "br%d" % j, "pw"),
-            "el": lambda: scan(T.ky[:], T.mk[:], pk, A.mult, A.max, ["mk", "ps1"], ["ky"]),
-            "pt": lambda: mms([(pt, T.idn[:], T.pat[:], True, False)], ["idn"] + ["pat%d" % k for k in range(5)], ["ps1"]),
-            "a1x": lambda: ts(T.ki[:, 0:16], T.ky[:, 3:64:4], NK * W - 1, None, A.bitwise_and, None, ["ky"], ["ki1"]),
-            "a2x": lambda: ts(T.ki[:, 16:32], T.ky[:, 3:64:4], W - 1, None, A.bitwise_and, None, ["ky"], ["ki2"]),
-            "eu": lambda: cp(T.eu[:], T.ki[:, 0:16], ["ki1"], ["eu"]), "wu": lambda: cp(T.wu[:], T.ki[:, 16:32], ["ki2"], ["wu"]),
-            "mk": lambda: act(T.ee[:, 0:4 * W].indirect(T.eu[:]), kin, F.Sigmoid, ["k01", "eu"], ee03),
-            "gl": lookups, "sx": lambda: tables(T.wu[:], "wu"), "sy": lambda: to_lists(True),
-            "dd": lambda: tt(T.d1[:, 0, 0:64:4], T.ki[:, 16:32], T.d1[:, 0, 3:64:4], A.subtract, ["ki2", "old0"], ["dif0"]),
-            "dx": lambda t: act(T.d1[:, t, 0:64:4], T.px[:, 0:16, COL[t - 1]], F.Copy, ["px.a"], ["dif%d" % t]),
-            "gv": look_v, "gs": look_s,
-            "uc": lambda: mms([(pt, T.sl2[:, 15 - i:143 - i], T.gt[:, i:K:16, :], False, i == 15) for i in range(16)],
-                              ["sl2", "gtz", "gt0", "gt1", "gt2", "gt3"], ["ps1"]),
-            "ch": choose,
-            "cd": lambda: cp(T.xu[:, 0:32], T.sc[:, 0:2, 3:64:4], ["sc0", "sc1"], ["du", "x0"]),
-            "cx": lambda: cp(T.xu[:, 32:80], T.sc[:, 2:5, 3:64:4], ["sc2", "sc3", "sc4"], ["x1", "x2", "x3"])}
-        for t in " ".join(CFG["plan"][s]).split():
-            tag[0] = ("plan", s, t)
+            "stay": stay, "half": lambda: cp(T.xh[:], T.d1[:, 1:7, 3:64:4], ["old0", "old1", "old2"], ["xh"]), "weave": weave,
+            "woven": lambda: cp(T.xi[:], T.px[:, 21:25, :], ["px.i"], ["xi"]),
+            "held": lambda m: act(T.ee[:, m * W:(m + 1) * W].indirect(du), mark, F.Sigmoid, ["k01", "du"], ["ee%d" % m]),
+            "look": lambda r: act(T.aa[:, K * r:K * r + K], T.bb[:].indirect(T.xi[:, 16 * r:16 * r + 16]), F.Abs, ["bb", "xi"], ["a%d" % r]),
+            "top": top, "vote": vote, "keys": keys, "tally": tally,
+            "br": lambda j: dense(j, T.br, "br", T.bb, "bb", "pr"), "hw": lambda j: dense(j, T.hw, "hw", T.br, "br%d" % j, "pw"),
+            "elect": lambda: scan(T.ky[:], T.mk[:], pk, A.mult, A.max, ["mk", "ps1"], ["ky"]),
+            "claim": lambda: ts(T.ki[:, 0:16], T.ky[:, 3:64:4], NK * W - 1, None, A.bitwise_and, None, ["ky"], ["ki1"]),
+            "wish": lambda: ts(T.ki[:, 16:32], T.ky[:, 3:64:4], W - 1, None, A.bitwise_and, None, ["ky"], ["ki2"]),
+            "claimu": lambda: cp(T.eu[:], T.ki[:, 0:16], ["ki1"], ["eu"]), "wishu": lambda: cp(T.wu[:], T.ki[:, 16:32], ["ki2"], ["wu"]),
+            "mark": lambda: act(T.ee[:, 0:4 * W].indirect(T.eu[:]), mark, F.Sigmoid, ["k01", "eu"], ee03),
+            "sections": sections, "seev": see_v, "sees": see_s, "blocked": blocked,
+            "free": lambda: mms([(pt, T.idn[:], T.pat[:], True, False)], ["idn"] + ["pat%d" % k for k in range(5)], ["ps1"]),
+            "ahead": lambda: tables(T.wu[:], "wu"), "aheadl": lambda: to_lists(True),
+            "step": lambda: tt(T.d1[:, 0, 0:64:4], T.ki[:, 16:32], T.d1[:, 0, 3:64:4], A.subtract, ["ki2", "old0"], ["dif0"]),
+            "diff": lambda t: act(T.d1[:, t, 0:64:4], T.px[:, 0:16, COL[t - 1]], F.Copy, ["px.a"], ["dif%d" % t]),
+            "neg": lambda j: act(T.nb[:, K * j:K * j + K], T.br[:, K * j:K * j + K], F.Copy, ["br%d" % j], ["nb%d" % j], scale=-1.0),
+            "choose": choose, "new": new_lists}
+        for t in plan(s):
+            at[0] = (s, t)
             name = t.rstrip("0123456789")
             if not (last and name in move):
                 fn = late.get(name) or move.get(name) or stage[name]
-                fn(int(t[len(name):])) if name != t else fn()
-        tag[0] = "r%d" % s
+                if name == t:
+                    fn()
+                else:
+                    fn(int(t[len(name):]))
 
+    at[0] = "end"
     dma("s", T.yb[:], T.bb[:], ["bb"], ["yb"], "st_b")
     op("s", None, ["yb", "yc"], [], end=True)
     op("g", None, ["sd%d" % s for s in range(RO)], [], end=True)

from concourse.bass import DstId, RemoteDMATransfer
from concourse.mybir import AluOpType, ActivationFunctionType

W, K, NK, RO = 1024, 256, 4, 3
UP, DN = NK, NK + 1
KS = K // 2
LW = 64
PW = K + LW
HW = K + 2 * LW
ZC = 4 * W
VB = 384
TV = 768
NB = 3
COL = (0, 2, 4, 6, 1, 3)
BIG, TINY = 2.0 ** 99, 2.0 ** -30

FIRST = ("ds1 widev ds3 bd oldb tables ds0 widen ds4 lists idf delta payload h send list0 list1 zero list2 hps1 nth "
         "gath0 gath1 ex1 size0 both0 counts0 abs1 list3 wx2 exc1 sum0 ok0 grad2 cz ex0 over1 sh count1 rest1 abs2 strong1 spread1 put0")
HEAD = "h send gath0 hps1 gath1 both0 zero size0 wx2 sum0 abs1 exc1 counts0 grad2 ok0 over1 abs2 count1 rest1 strong1 put0 spread1"
ARRIVAL = ("exc2 nzs1 nzv1 wx3 oks1 sum1 over2 count2 _ okv1 _ grad3 put1 rest2 abs3 strong2 spread2 "
           "nzv2 nzs2 sum2 okv2 exc3 _ list4 oks2 hps4 over3 put2 list5 _ _ count3 wx4 strong3 rest3 hps5 spread3 "
           "nzv3 nzs3 sum3 wx5 oks3 grad4 okv3 abs4 grad5 abs5 put3 _ "
           "tiny4 partv4 sum4 parts4 exc5 over5 _ rest5 ok4 _ _ put4 _ count5 strong5 spread5 "
           "nzv5 nzs5 sum5 okv5 _ oks5 put5 _")
SPARE = ("zbr stay0", "", "", "grow", "stay2 stay1 half", "weave", "", "woven held3", "", "", "", "held4")
SPARE0 = ("ds2 stay0 zq2 idn", "sel", "c0 zq1 stay2 stay1", "", "half zq3 zq0", "weave less", "wp recp sl", "woven", "held4 gtz", "c1", "c2 mask", "pat c3 held3")
MOVE = ("look0 keys look1 br0 br1 top0 look2 top1 vote0 vote1 top2 tally0 look3 top3 vote2 tally1 tally2 vote3 hw1 br2 tally3 elect free claim wish claimu wishu "
        "br3 neg0 mark ahead sections sees0 sees1 neg2 aheadl diff1 seev0 diff4 seev1 step diff3 hw2 blocked hw3 neg1 hw0 diff2 diff5 diff6 "
        "choose0 choose1 neg3 choose4 choose3 choose2 new0 choose6 choose5 new1")


def plan(s):
    out = (HEAD if s else FIRST).split()
    spare = list(SPARE if s else SPARE0)
    for t in ARRIVAL.split():
        out += spare.pop(0).split() if t == "_" else [t]
    return out + MOVE.split()


SCRATCH = {
    "b16": ("sbuf", [128, W], "bfloat16"), "w16": ("sbuf", [128, W], "bfloat16"), "r16": ("sbuf", [128, W], "bfloat16"),
    "thr": ("sbuf", [128, 4], "float32"), "nth": ("sbuf", [128, 4], "float32"), "tb": ("sbuf", [128, W], "int32"), "wki": ("sbuf", [128, 16], "int32"),
    "bb": ("sbuf", [128, W], "float32"), "cc": ("sbuf", [128, W], "float32"), "ee": ("sbuf", [128, 5 * W + 16], "float32"),
    "br": ("sbuf", [128, W], "float32"), "hw": ("sbuf", [128, W], "float32"),
    "kw": ("sbuf", [128, 16], "float32"), "kz": ("sbuf", [128, K], "float32"), "k01": ("sbuf", [128, 2 * K], "float32"),
    "uu": ("sbuf", [128, 176], "bfloat16"), "u16": ("sbuf", [128, 128], "bfloat16"), "u4": ("sbuf", [128, 144], "bfloat16"), "pi": ("sbuf", [128, 8], "int32"),
    "pf": ("sbuf", [128, 8], "float32"), "pg": ("sbuf", [128, 8], "float32"), "mq": ("sbuf", [128, 8], "float32"),
    "mk0": ("sbuf", [128, 64], "float32"), "mk": ("sbuf", [128, 64], "float32"), "mv": ("sbuf", [128, K], "float32"),
    "pat": ("sbuf", [128, 64], "bfloat16"), "kc": ("sbuf", [128, 64], "bfloat16"),
    "sel": ("sbuf", [128, 160], "bfloat16"), "sl": ("sbuf", [128, 160], "bfloat16"), "bd": ("sbuf", [128, 128], "bfloat16"), "idn": ("sbuf", [128, 128], "bfloat16"),
    "cz": ("sbuf", [128, 144], "bfloat16"), "ex": ("sbuf", [128, 2, 128], "bfloat16"), "zq": ("sbuf", [128, 4, 144], "bfloat16"), "ndn": ("sbuf", [128, 128], "bfloat16"),
    "ds": ("sbuf", [128, 5, 176], "bfloat16"),
    "e0": ("sbuf", [128, 160], "float16"), "e1": ("sbuf", [128, 160], "float16"), "sh": ("sbuf", [128, 128], "float32"), "idf": ("sbuf", [128, 128], "float32"),
    "xg": ("sbuf", [128, K], "float16"), "yy": ("sbuf", [128, 8, 32], "float16"), "xu": ("sbuf", [128, 112], "uint16"),
    "xh": ("sbuf", [128, 96], "float16"), "xi": ("sbuf", [128, 64], "uint16"), "wu": ("sbuf", [128, 16], "uint16"),
    "bo": ("sbuf", [128, K], "float32"), "dl": ("sbuf", [128, K], "float32"), "nb": ("sbuf", [128, W], "float32"),
    "hb": ("sbuf", [128, RO * HW], "float32"), "lu": ("sbuf", [128, RO * PW], "float32"), "ld": ("sbuf", [128, RO * PW], "float32"),
    "gg": ("sbuf", [128, NB, K], "float32"), "ab": ("sbuf", [128, NB, K], "float32"), "rl": ("sbuf", [128, NB, K], "bfloat16"),
    "ov": ("sbuf", [128, NB, K], "bfloat16"), "wx": ("sbuf", [128, NB, K], "float32"),
    "mn": ("sbuf", [128, 64], "bfloat16"), "nz": ("sbuf", [128, K], "bfloat16"), "ss": ("sbuf", [128, K], "float32"), "ac": ("sbuf", [128, K], "float32"),
    "aa": ("sbuf", [128, NK * K], "float32"), "eq": ("sbuf", [128, 64, 16], "bfloat16"),
    "ky": ("sbuf", [128, 64], "int32"), "ki": ("sbuf", [128, 32], "int32"), "eu": ("sbuf", [128, 16], "uint16"), "gl": ("sbuf", [128, 48], "uint16"),
    "gt": ("sbuf", [128, K, 4], "bfloat16"), "d1": ("sbuf", [128, 7, 64], "float32"), "sc": ("sbuf", [128, 5, 64], "float32"),
    "px": ("psum", [128, 32, 16], "float32"), "ps0": ("psum", [128, 512], "float32"), "ps1": ("psum", [128, 512], "float32"), "ph": ("psum", [128, 512], "float32"),
    "pr0": ("psum", [128, 512], "float32"), "pr1": ("psum", [128, 512], "float32"), "pw0": ("psum", [128, 512], "float32"), "pw1": ("psum", [128, 512], "float32"),
}
BANKS = ("px", "ps0", "ps1", "ph", "pr0", "pr1", "pw0", "pw1")
SEMAPHORES = (["qg", "qv", "qa", "qp", "qs", "l_wk", "l_rec", "l_th", "l_tb", "l_b", "l_w", "st_b", "st_c", "add0", "add1", "add2", "add3"]
              + ["au%d" % s for s in range(RO)] + ["ad%d" % s for s in range(RO)] + ["sent%d" % s for s in range(RO)])
A = AluOpType
F = ActivationFunctionType


def depends(ops):
    writer, readers, touch, deps = {}, {}, {}, []
    for i, op in enumerate(ops):
        d = set(writer[r] for r in op["r"] if r in writer)
        for w in op["w"]:
            d.update(readers.get(w, []))
            if w in writer:
                d.add(writer[w])
        for b in set(x.split(".")[0] for x in op["r"] + op["w"]):
            if b in BANKS:
                d.update(j for j in touch.setdefault(b, []) if ops[j]["q"] != op["q"])
                touch[b] = [j for j in touch[b] if ops[j]["q"] == op["q"]] + [i]
        for r in op["r"]:
            readers.setdefault(r, []).append(i)
        for w in op["w"]:
            writer[w] = i
            readers[w] = []
        deps.append(d)
    return deps


def emit(g, T, ops):
    deps = depends(ops)
    queue = {"g": g, "v": g.vector, "a": g.scalar, "p": g.tensor, "s": g.sync}
    clock, pos = {q: {} for q in queue}, {q: 0 for q in queue}
    for i, op in enumerate(ops):
        q = op["q"]
        if op["ev"] is None:
            pos[q] += 1
            op["key"], op["pos"] = "q" + q, pos[q]
        else:
            op["key"], op["pos"] = op["ev"]
        op["waits"] = []
        if op["fn"] is not None or op["end"]:
            for j in sorted(deps[i], reverse=True):
                d = ops[j]
                if q == "p" and d["q"] == "p":
                    continue
                if clock[q].get(d["key"], 0) >= d["pos"]:
                    continue
                op["waits"].append(j)
                d["need"] = True
                for k, v in d["clock"].items():
                    clock[q][k] = max(clock[q].get(k, 0), v)
        op["clock"] = dict(clock[q]) if op["fn"] is not None else {}
        op["clock"][op["key"]] = op["pos"]
    count = {}
    for op in ops:
        if op["ev"] is None and op.get("need"):
            count[op["key"]] = count.get(op["key"], 0) + 1
            op["val"] = count[op["key"]]
        elif op["ev"] is not None:
            op["val"] = op["pos"]
    for op in ops:
        e = queue[op["q"]]
        for j in op["waits"]:
            e.wait_ge(T.sem[ops[j]["key"]], ops[j]["val"])
        if op["fn"] is None:
            continue
        ins = op["fn"](e)
        if op["ev"] is None:
            if op.get("need"):
                ins.then_inc(T.sem[op["key"]], 1)
        elif op["dma"]:
            ins.then_inc(T.sem[op["key"]], 16)


def neighbours(T, topo, rank):
    n = len(T.cores)
    src = T.cores[rank]
    dst = [T.cores[(rank + 1) % n], T.cores[(rank - 1) % n]]
    may = [topo.engines(src, d) for d in dst]
    size = min(len(may[0]), len(may[1]), len(set(may[0]) | set(may[1])) // 2)
    i = 0 if len(may[0]) <= len(may[1]) else 1
    eng = [None, None]
    eng[i] = may[i][:size]
    eng[1 - i] = [e for e in may[1 - i] if e not in eng[i]][:size]
    return dst, eng


def rank_program(g, core, T, topo):
    rank = T.rank_of(core)
    if rank is None:
        return
    n = len(T.cores)
    ops, at = [], ["start"]

    def op(q, fn, r, w, ev=None, dma=False, end=False):
        ops.append({"stage": at[0], "q": q, "fn": fn, "r": list(r), "w": list(w), "ev": ev, "dma": dma, "end": end})

    def dma(q, out, in_, r, w, sem, val=16):
        op(q, lambda e: e.dma_start(out, in_), r, w, ev=(sem, val), dma=True)

    def ts(out, in0, s1, s2, op0, op1, r, w):
        if op1 is None:
            op("v", lambda e: e.tensor_scalar(out, in0, s1, None, op0), r, w)
        else:
            op("v", lambda e: e.tensor_scalar(out, in0, s1, s2, op0, op1), r, w)

    def tt(out, in0, in1, o, r, w):
        op("v", lambda e: e.tensor_tensor(out, in0, in1, o), r, w)

    def cp(out, in_, r, w):
        op("v", lambda e: e.tensor_copy(out, in_), r, w)

    def fill(out, v, w):
        op("v", lambda e: e.memset(out, v), [], w)

    def scan(out, d0, d1, o0, o1, r, w):
        op("v", lambda e: e.tensor_tensor_scan(out, d0, d1, 0.0, o0, o1), r, w)

    def act(out, in_, f, r, w, **kw):
        op("a", lambda e: e.activation(out, in_, f, **kw), r, w)

    def iota(out, pat, base, cm, w, flt=True):
        if flt:
            op("g", lambda e: e.iota(out, pat, base, cm, allow_small_or_imprecise_dtypes=True), [], w)
        else:
            op("g", lambda e: e.iota(out, pat, base, cm), [], w)

    def mms(items, r, w):
        def fn(e):
            ins = None
            for out, lhs, rhs, st, sp in items:
                ins = e.matmul(out, lhs, rhs, st, sp)
            return ins
        op("p", fn, r, w)

    fill(T.kw[:], -200.0, ["kw"])
    fill(T.tb[:, 0:TV], 0, ["tb0"])
    iota(T.pi[:, 0:2], [[16, 2]], 0, 1, ["pi0"], flt=False)
    iota(T.tb[:, TV:W], [[0, W - TV]], 0, 0, ["tb1"], flt=False)
    dma("s", T.wki[:], T.wk[:], [], ["wki"], "l_wk")
    dma("a", T.b16[:], T.b0[:], [], ["b16"], "l_b")
    dma("s", T.r16[:], T.rec[:], [], ["r16"], "l_rec")
    dma("a", T.thr[:, 0:1], T.th[:], [], ["thr"], "l_th")
    dma("s", T.tb[0:128:4, :], T.hop[:], ["tb0", "tb1"], ["tbh"], "l_tb", 48)
    dma("s", T.tb[2:128:16, :], T.up[:], ["tb0", "tb1"], ["tbu"], "l_tb", 48)
    dma("s", T.tb[6:128:16, :], T.dn[:], ["tb0", "tb1"], ["tbd"], "l_tb", 48)
    dma("s", T.w16[:], T.w[:], [], ["w16"], "l_w")
    iota(T.uu[:], [[1, 176]], -16, 0, ["uu"])
    iota(T.u16[:], [[16, 8], [0, 16]], 0, 0, ["u16"])
    iota(T.u4[:], [[4, 36], [0, 4]], -12, 0, ["u4"])
    iota(T.kz[:], [[0, K]], -200, 0, ["kz"])
    iota(T.hb[:, 0:HW], [[0, HW]], 0, 0, ["hb", "h0"])
    act(T.ee[:, 5 * W:5 * W + 16], T.kw[:], F.Sigmoid, ["kw"], ["eez"])
    ts(T.pi[:, 2:3], T.pi[:, 0:1], 112, None, A.bitwise_and, None, ["pi0"], ["pi2"])
    ts(T.pi[:, 3:4], T.pi[:, 0:1], 16, None, A.bitwise_and, None, ["pi0"], ["pi3"])
    ts(T.pi[:, 4:5], T.pi[:, 1:2], 127, None, A.bitwise_and, None, ["pi0"], ["pi4"])
    ts(T.pi[:, 5:6], T.pi[:, 0:1], 12, None, A.bitwise_and, None, ["pi0"], ["pi5"])
    ts(T.pi[:, 6:7], T.pi[:, 0:1], 3, None, A.bitwise_and, None, ["pi0"], ["pi6"])
    cp(T.pf[:, 0:7], T.pi[:, 0:7], ["pi0", "pi2", "pi3", "pi4", "pi5", "pi6"], ["pf"])
    ts(T.pg[:, 0:1], T.pf[:, 3:4], 0.0625, None, A.mult, None, ["pf"], ["pg0"])
    ts(T.pg[:, 1:2], T.pf[:, 3:4], -0.0625, 1.0, A.mult, A.add, ["pf"], ["pg1"])
    ts(T.e0[:], T.uu[:, 0:160], T.pf[:, 0:1], T.pg[:, 1:2], A.is_equal, A.mult, ["uu", "pf", "pg1"], ["e0"])
    ts(T.e1[:], T.uu[:, 0:160], T.pf[:, 0:1], T.pg[:, 0:1], A.is_equal, A.mult, ["uu", "pf", "pg0"], ["e1"])
    ts(T.mq[:, 0:2], T.u4[:, 12:20:4], T.pf[:, 5:6], None, A.is_equal, None, ["u4", "pf"], ["mq"])
    ts(T.mq[:, 2:6], T.uu[:, 16:20], T.pf[:, 6:7], None, A.is_equal, None, ["uu", "pf"], ["mr"])
    cp(T.xu[:, 0:16], T.wki[:], ["wki"], ["du"])

    far = ((T.uu[:], "uu", 0), (T.u16[:], "u16", 2), (T.uu[:, 1:161], "uu", 2), (T.u4[:], "u4", 2), (T.uu[:, 16:144], "uu", 4))

    def distance(i):
        row, rn, col = far[i]
        act(T.ds[:, i, 0:row.shape[1]], row, F.Abs, [rn, "pf"], ["ds%d" % i], scale=-1.0, bias=T.pf[:, col:col + 1])

    def match(out, on, i, c0, one=1.0, r=()):
        act(out, T.ds[:, i, c0:c0 + out.shape[1]], F.Relu, ["ds%d" % i] + list(r), [on], scale=-one if r == () else -1.0, bias=one)

    def pattern():
        for k, (c0, c1, v) in enumerate(((0, 64, 0.0), (1, 64, 1.0), (2, 32, 1.0), (34, 64, 0.5), (3, 64, 0.5))):
            act(T.pat[:, c0:c1:4], T.kz[:, c0:c1:4], F.Identity, ["kz"], ["pat%d" % k], scale=0.0, bias=v)

    def to_psum(name, src, sn):
        for j in range(2):
            mms([(T["%s%d" % (name, j)][:], T.idn[:], src[:, 512 * j:512 * j + 512], True, True)], ["idn", sn], ["%s%d" % (name, j)])

    late = {
        "ds": distance, "idf": lambda: match(T.idf[:], "idf", 0, 16), "idn": lambda: match(T.idn[:], "idn", 0, 16),
        "zq": lambda r: match(T.zq[:, r, :], "zq%d" % r, 0, 13, T.mq[:, 2 + r:3 + r], ["mr"]),
        "bd": lambda: match(T.bd[:], "bd", 1, 0), "ex": lambda q: match(T.ex[:, q, :], "ex%d" % q, 1, 0, T.mq[:, q:q + 1], ["mq"]),
        "sel": lambda: match(T.sel[:], "sel", 2, 0, 4096.0), "cz": lambda: match(T.cz[:], "cz", 3, 0), "sh": lambda: match(T.sh[:], "sh", 4, 0),
        "sl": lambda: act(T.sl[:], T.sel[:], F.Copy, ["sel"], ["sl"], scale=-2.0 ** -17),
        "less": lambda: act(T.ndn[:], T.idn[:], F.Copy, ["idn"], ["ndn"], scale=-1.0),
        "nth": lambda: act(T.nth[:, 0:1], T.thr[:, 0:1], F.Copy, ["thr"], ["nth"], scale=-1.0),
        "gtz": lambda: act(T.gt[:, :, 0], T.kz[:], F.Copy, ["kz"], ["gtz"], scale=0.0),
        "mask": lambda: act(T.mk[:], T.mk0[:], F.Sign, ["mk0"], ["mk"]), "pat": pattern,
        "recp": lambda: to_psum("pr", T.r16, "r16"), "wp": lambda: to_psum("pw", T.w16, "w16"),
        "widev": lambda: cp(T.bb[:, 0:VB], T.b16[:, 0:VB], ["b16"], ["bbv"])}

    dst, eng = neighbours(T, topo, rank)
    n_up = len(neighbours(T, topo, (rank - 1) % n)[1][0])
    n_dn = len(neighbours(T, topo, (rank + 1) % n)[1][1])
    du = T.xu[:, 0:16]
    brs, nbs = ["br%d" % j for j in range(4)], ["nb%d" % j for j in range(4)]

    def xl(a, c0=0, c1=16):
        return T.xu[:, 16 + 16 * a + c0:16 + 16 * a + c1]

    for s in range(RO):
        last = s == RO - 1
        hb0 = HW * s
        h, hn = T.hb[:, hb0 + LW:hb0 + LW + K], "h%d" % s
        lu, ld = T.lu[:, PW * s:PW * s + PW], T.ld[:, PW * s:PW * s + PW]

        def make_h():
            if s == 0:
                tt(h, T.w16[:].indirect(du), T.dl[:], A.mult, ["w16", "du", "dl"], [hn])
            else:
                ts(h, T.hw[:].indirect(du), -1.0, None, A.mult, None, ["hw0", "hw1", "hw2", "hw3", "du"], [hn])

        def tables(lst, ln):
            cp(T.xg[:], T.tb[:].indirect(lst), ["tb0", "tbh", "tbu", "tbd", ln], ["xg"])

        def to_lists(less):
            if less:
                mms([(T.px[:, 0:16, c], T.ndn[:], T.xh[:, 16 * (t % 6):16 * (t % 6) + 16], t == 0, False) for t, c in enumerate(COL + (5,))],
                    ["ndn", "xh"], ["px.a"])
            op("v", lambda e: e.transpose(T.yy[:], T.xg[:]), ["xg"], ["yy"])
            mms([(T.px[:, 0:16:2, 0:7], T.e0[:, 16:144], T.yy[:, :, 0:14:2], not less, False),
                 (T.px[:, 0:16:2, 0:7], T.e0[:, 0:128], T.yy[:, :, 16:30:2], False, False),
                 (T.px[:, 1:16:2, 0:7], T.e1[:, 32:160], T.yy[:, :, 0:14:2], False, False),
                 (T.px[:, 1:16:2, 0:7], T.e1[:, 16:144], T.yy[:, :, 16:30:2], False, True)], ["yy", "e0", "e1"], ["px.a"])

        def payload():
            act(T.hb[:, hb0 + 3:hb0 + LW:4], T.px[:, 0:16, COL[UP]], F.Copy, ["px.a", "hb"], [hn + "u"])
            act(T.hb[:, hb0 + LW + K + 3:hb0 + HW:4], T.px[:, 0:16, COL[DN]], F.Copy, ["px.a", "hb"], [hn + "d"])

        def send():
            tr = []
            for i, (land, from_, sem) in enumerate([(lu, T.hb[:, hb0:hb0 + PW], "au%d" % s), (ld, T.hb[:, hb0 + LW:hb0 + HW], "ad%d" % s)]):
                rid, pid = topo.addr(dst[i], core)
                tr.append(RemoteDMATransfer(dst_ids=[DstId(rid=rid, pnc=pid)], dma_engine_mask=sum(1 << x for x in eng[i]),
                                            remote_sem=T.sem[sem], src=from_, dst=land))
            sent = T.sem["sent%d" % s]
            op("g", lambda e: e.remote_dma_fused(tr, local_sem=sent), [hn, hn + "u", hn + "d"], ["sd%d" % s], ev=("sent%d" % s, len(eng[0]) + len(eng[1])))
            op("g", None, ["sd%d" % s], ["lu%d" % s], ev=("au%d" % s, n_up))
            op("g", None, ["sd%d" % s], ["ld%d" % s], ev=("ad%d" % s, n_dn))
            if s == 0:
                iota(T.d1[:], [[0, 7], [0, 64]], 0, 0, ["d1"])
                iota(T.cc[:], [[0, W]], 0, 0, ["cc"])
                iota(T.mk0[:], [[0, 16], [1, 4]], 0, 0, ["mk0"])
                iota(T.kc[:], [[0, 16], [-W, NK]], (NK - 1) * W, 0, ["kc"])
                iota(T.mv[:], [[0, 64], [4096, 4]], 0, 0, ["mv"])
                iota(T.k01[:], [[200, 2], [0, K]], 0, 0, ["k01"])
                for m in (4, 3, 2, 1, 0):
                    iota(T.ee[:, m * W:(m + 1) * W], [[0, W]], 0, 0, ["ee%d" % m])

        def first_c(i):
            cp(T.cc[:].indirect(T.xu[:, 4 * i:4 * i + 4]), T.dl[:, 64 * i:64 * i + 64], ["dl", "du"], ["cc"])
            if i == 3:
                dma("s", T.yc[:], T.cc[:], ["cc"], ["yc"], "st_c")

        def grow_c():
            op("g", lambda e: e.dma_start(T.nb[:], T.br[:], accum_op=A.add), brs + ["sd%d" % s], nbs, ev=("add%d" % (2 * s - 2), 16), dma=True)
            op("g", lambda e: e.dma_start(T.yc[:], T.nb[:], accum_op=A.add), nbs, ["yc"], ev=("add%d" % (2 * s - 1), 16), dma=True)

        def xlist(a):
            if a < NK:
                cp(xl(a), T.px[:, 0:16, COL[a]], ["px.a"], ["x%d" % a])
            elif a == UP:
                mms([(T.px[:, 16, :], T.sh[:], lu[:, 3:LW:4], True, True)], ["sh", "lu%d" % s], ["px.l"])
                cp(xl(a), T.px[:, 16, :], ["px.l"], ["x4"])
            else:
                cp(xl(a), ld[:, K + 3:PW:4], ["ld%d" % s], ["x5"])

        def h_psum(a):
            if a < NK:
                mms([(T.ph[:, 0:K], T.idf[:], h, True, True)], ["idf", hn], ["ph.0"])
            elif a == UP:
                mms([(T.ph[:, K:2 * K], T.sh[:], lu[:, LW:PW], True, True)], ["sh", "lu%d" % s], ["ph.1"])
            else:
                mms([(T.ph[:, 0:K], T.idf[:], ld[:, 0:K], True, True)], ["idf", "ld%d" % s], ["ph.0"])

        def weights(a):
            act(T.wx[:, a % NB, :], T.w16[:].indirect(xl(a)), F.Copy, ["w16", "x%d" % a], ["wx%d" % (a % NB)])

        def grad(a):
            i = int(a == UP)
            tt(T.gg[:, a % NB, :], T.wx[:, a % NB, :], T.ph[:, K * i:K * i + K], A.mult, ["wx%d" % (a % NB), "ph.%d" % i], ["g%d" % (a % NB)])

        def grad_gather(a):
            tt(T.gg[:, a, :], T.w16[:].indirect(xl(a)), h, A.mult, ["w16", "x%d" % a, hn], ["g%d" % a])

        def size(a):
            act(T.ab[:, a % NB, :], T.gg[:, a % NB, :], F.Abs, ["g%d" % (a % NB)], ["ab%d" % (a % NB)])

        def excess(a):
            act(T.rl[:, a % NB, :], T.ab[:, a % NB, :], F.Relu, ["ab%d" % (a % NB), "nth"], ["rl%d" % (a % NB)], bias=T.nth[:, 0:1])

        def over(a):
            act(T.ov[:, a % NB, :], T.rl[:, a % NB, :], F.Sign, ["rl%d" % (a % NB)], ["ov%d" % (a % NB)])

        def count(a):
            mms([(T.px[:, 17:21, :], T.cz[:, 12 - 4 * q:140 - 4 * q], T.ov[:, a % NB, 64 * q:64 * q + 64], q == 0, q == 1) for q in range(2)],
                ["cz", "ov%d" % (a % NB)], ["px.c"])

        def strong(a):
            act(T.mn[:], T.px[:, 17:21, :], F.Relu, ["px.c"], ["mn"], bias=-8.0)

        def spread(a):
            mms([(T.ps0[:, 64 * q:64 * q + 64], T.ex[:, q, :], T.mn[:], q == 0, False) for q in range(2)], ["mn", "ex0", "ex1"], ["ps0"])

        def count_rest(a):
            mms([(T.ps1[:, 0:K - KS], T.bd[:], T.ov[:, a % NB, KS:K], True, False)], ["bd", "ov%d" % (a % NB)], ["ps1"])

        def filled_s(a):
            act(T.nz[:, 0:KS], T.bb[:].indirect(xl(a, 0, KS // 16)), F.Abs, ["bb", "x%d" % a], ["nz0"])
            mms([(T.ps0[:, 0:KS], T.bd[:], T.nz[:, 0:KS], False, True)], ["bd", "nz0"], ["ps0"])

        def filled_v(a):
            ts(T.nz[:, KS:K], T.bb[:].indirect(xl(a, KS // 16, 16)), 0.0, 16.0, A.not_equal, A.mult, ["bb", "x%d" % a], ["nz1"])
            mms([(T.ps1[:, 0:K - KS], T.bd[:], T.nz[:, KS:K], False, True)], ["bd", "nz1"], ["ps1"])

        def total(a):
            tt(T.ss[:], T.bb[:].indirect(xl(a)), T.gg[:, a % NB, :], A.add, ["bb", "x%d" % a, "g%d" % (a % NB)], ["ss"])

        def put(a):
            tt(T.bb[:].indirect(xl(a)), T.ss[:], T.ac[:], A.mult, ["ss", "x%d" % a, "ac0", "ac1"], ["bb"])

        def size_first(a):
            act(T.nz[:], T.bb[:].indirect(xl(a)), F.Abs, ["bb", "x%d" % a], ["nz0", "nz1"], scale=BIG)
            mms([(T.ps0[:, 0:K], T.bd[:], T.nz[:], True, False)], ["bd", "nz0", "nz1"], ["ps0"])

        def both_sides(a):
            ts(T.ov[:, a, :], T.gg[:, a, :], T.thr[:, 0:1], TINY, A.is_gt, A.mult, ["g0", "thr"], ["ov0"])
            ts(T.rl[:, a, :], T.gg[:, a, :], T.nth[:, 0:1], TINY, A.is_lt, A.mult, ["g0", "nth"], ["rl0"])

        def count_both(a):
            mms([(T.ps0[:, 0:K], T.bd[:], T.ov[:, a, :], False, False)], ["bd", "ov0"], ["ps0"])
            mms([(T.ps0[:, 0:K], T.bd[:], T.rl[:, a, :], False, True)], ["bd", "rl0"], ["ps0"])

        def over_tiny(a):
            b = a % NB
            ts(T.ov[:, b, :], T.ab[:, b, :], T.thr[:, 0:1], TINY, A.is_gt, A.mult, ["ab%d" % b, "thr"], ["ov%d" % b])
            mms([(T.ps0[:, 0:K], T.bd[:], T.ov[:, b, :], True, False)], ["bd", "ov%d" % b], ["ps0"])

        def part_v(a):
            ts(T.nz[:, KS:K], T.bb[:].indirect(xl(a, KS // 16, 16)), 0.0, None, A.not_equal, None, ["bb", "x%d" % a], ["nz1"])
            mms([(T.ps0[:, KS:K], T.bd[:], T.nz[:, KS:K], False, False)], ["bd", "nz1"], ["ps0"])

        def part_s(a):
            act(T.nz[:, 0:KS], T.bb[:].indirect(xl(a, 0, KS // 16)), F.Abs, ["bb", "x%d" % a], ["nz0"], scale=BIG)
            mms([(T.ps0[:, 0:KS], T.bd[:], T.nz[:, 0:KS], False, True)], ["bd", "nz0"], ["ps0"])

        pk, pt = T.ps1[:, K:K + 64], T.ps1[:, K + 64:K + 128]
        mark = T.k01[:, K * (s % 2):K * (s % 2) + K]
        ee03, ee14 = ["ee0", "ee1", "ee2", "ee3"], ["ee1", "ee2", "ee3", "ee4", "eez"]
        win, lev = T.ee[:, W:5 * W + 16], 0.25 + 0.5 * s

        def stay(i):
            if i == 0:
                cp(T.d1[:, 0:5, 3:64:4], T.xu[:, 0:80], ["du", "x0", "x1", "x2", "x3", "d1"], ["old0"])
            else:
                c0 = hb0 + (i - 1) * (LW + K)
                act(T.d1[:, 4 + i, 3:64:4], T.hb[:, c0 + 3:c0 + LW:4], F.Copy, [hn + "ud"[i - 1], "d1"], ["old%d" % i])

        def weave():
            for r in range(4):
                mms([(T.px[:, 21 + r, :], T.zq[:, r, 3 + r - k:131 + r - k], T.xh[:, 16 * k:16 * k + 16], k == 0, k == 3) for k in range(NK)],
                    ["xh", "zq%d" % r], ["px.i"])

        def top(r):
            scan(T.ph[:, K * (r % 2):K * (r % 2) + K], T.mv[:], T.aa[:, K * r:K * r + K], A.min, A.max, ["mv", "a%d" % r], ["ph.%d" % (r % 2)])

        def vote(r):
            for k in range(NK):
                tt(T.eq[:, 16 * r:16 * r + 16, k:16:4], T.aa[:, K * r + k:K * r + K:4], T.ph[:, K * (r % 2) + 3:K * (r % 2) + K:4], A.is_equal,
                   ["a%d" % r, "ph.%d" % (r % 2)], ["eq%d%d" % (k, r)])

        def keys():
            mms([(pk, T.idn[:], T.kc[:], True, False)] + [(pk[:, k:64:4], T.idn[:], T.xh[:, 16 * k:16 * k + 16], False, False) for k in range(NK)],
                ["idn", "xh", "kc"], ["ps1"])

        def tally(r):
            mms([(pk, T.sel[:, 15 - 4 * q - r:143 - 4 * q - r], T.eq[:, 16 * r:16 * r + 16, 4 * q:4 * q + 4], False, r == 3 and q == 3) for q in range(4)],
                ["sel"] + ["eq%d%d" % (k, r) for k in range(NK)], ["ps1"])

        def dense(j, out, on, in0, in0n, ps):
            tt(out[:, K * j:K * j + K], in0[:, K * j:K * j + K], T["%s%d" % (ps, j // 2)][:, K * (j % 2):K * (j % 2) + K], A.mult,
               [in0n, "%s%d" % (ps, j // 2)], ["%s%d" % (on, j)])

        def sections():
            for m in range(3):
                ts(T.gl[:, 16 * m:16 * m + 16], T.ki[:, 0:16], float(m * W), float(ZC), A.add, A.min, ["ki1"], ["gl%d" % m])

        def see_v(i):
            out, lst = ((T.gt[:, :, 1], T.gl[:, 0:16]), (T.gt[:, 0:128, 2], T.gl[:, 16:24]))[i]
            ts(out, win.indirect(lst), lev, 2.0, A.is_gt, A.mult, ee14 + ["gl%d" % i], ["gt%d" % i])

        def see_s(i):
            out, lst = ((T.gt[:, 128:K, 2], T.gl[:, 24:32]), (T.gt[:, :, 3], T.gl[:, 32:48]))[i]
            act(out, win.indirect(lst), F.Sign, ee14 + ["gl%d" % (i + 1)], ["gt%d" % (i + 2)], bias=-lev)

        def blocked():
            mms([(pt, T.sl[:, 15 - i:143 - i], T.gt[:, i:K:16, :], False, i == 15) for i in range(16)], ["sl", "gtz", "gt0", "gt1", "gt2", "gt3"], ["ps1"])

        def choose(t):
            c0 = hb0 + HW + (t - 5) * (LW + K)
            out, on = (T.sc[:, t, :], "sc%d" % t) if t < 5 else (T.hb[:, c0:c0 + LW], "h%d%s" % (s + 1, "ud"[t - 5]))
            scan(out, pt, T.d1[:, t, :], A.mult, A.add, ["ps1", "dif%d" % t, "old%d" % max(0, t - 4)], [on])

        def new_lists(i):
            t0, t1 = ((0, 2), (2, 5))[i]
            cp(T.xu[:, 16 * t0:16 * t1], T.sc[:, t0:t1, 3:64:4], ["sc%d" % t for t in range(t0, t1)], ["du", "x0", "x1", "x2", "x3"][t0:t1])

        stage = {
            "oldb": lambda: act(T.bo[:], T.b16[:].indirect(du), F.Copy, ["b16", "du"], ["bo"], scale=-1.0),
            "widen": lambda: act(T.bb[:, VB:W], T.b16[:, VB:W], F.Copy, ["b16"], ["bb"]),
            "zero": lambda: act(T.bb[:].indirect(du), T.kz[:], F.Sigmoid, ["kz", "du", "bbv"], ["bb"]),
            "tables": lambda: tables(du, "du"), "lists": lambda: to_lists(False), "h": make_h, "payload": payload, "send": send,
            "delta": lambda: tt(T.dl[:], T.r16[:].indirect(du), T.bo[:], A.mult, ["r16", "du", "bo"], ["dl"]), "c": first_c,
            "zbr": lambda: act(T.br[:].indirect(du), T.kz[:], F.Sigmoid, ["kz", "du"], brs), "grow": grow_c,
            "list": xlist, "hps": h_psum, "wx": weights, "grad": grad, "gath": grad_gather, "abs": size, "exc": excess, "over": over,
            "count": count, "strong": strong, "spread": spread, "rest": count_rest, "nzs": filled_s, "nzv": filled_v, "sum": total, "put": put,
            "oks": lambda a: act(T.ac[:, 0:KS], T.ps0[:, 0:KS], F.Sign, ["ps0"], ["ac0"]),
            "okv": lambda a: ts(T.ac[:, KS:K], T.ps1[:, 0:K - KS], 8.5, None, A.is_gt, None, ["ps1"], ["ac1"]),
            "size": size_first, "both": both_sides, "counts": count_both, "partv": part_v, "tiny": over_tiny, "parts": part_s,
            "ok": lambda a: ts(T.ac[:], T.ps0[:, 0:K], 8.5 * TINY, None, A.is_gt, None, ["ps0"], ["ac0", "ac1"])}
        move = {
            "stay": stay, "half": lambda: cp(T.xh[:], T.d1[:, 1:7, 3:64:4], ["old0", "old1", "old2"], ["xh"]), "weave": weave,
            "woven": lambda: cp(T.xi[:], T.px[:, 21:25, :], ["px.i"], ["xi"]),
            "held": lambda m: act(T.ee[:, m * W:(m + 1) * W].indirect(du), mark, F.Sigmoid, ["k01", "du"], ["ee%d" % m]),
            "look": lambda r: act(T.aa[:, K * r:K * r + K], T.bb[:].indirect(T.xi[:, 16 * r:16 * r + 16]), F.Abs, ["bb", "xi"], ["a%d" % r]),
            "top": top, "vote": vote, "keys": keys, "tally": tally,
            "br": lambda j: dense(j, T.br, "br", T.bb, "bb", "pr"), "hw": lambda j: dense(j, T.hw, "hw", T.br, "br%d" % j, "pw"),
            "elect": lambda: scan(T.ky[:], T.mk[:], pk, A.mult, A.max, ["mk", "ps1"], ["ky"]),
            "claim": lambda: ts(T.ki[:, 0:16], T.ky[:, 3:64:4], NK * W - 1, None, A.bitwise_and, None, ["ky"], ["ki1"]),
            "wish": lambda: ts(T.ki[:, 16:32], T.ky[:, 3:64:4], W - 1, None, A.bitwise_and, None, ["ky"], ["ki2"]),
            "claimu": lambda: cp(T.eu[:], T.ki[:, 0:16], ["ki1"], ["eu"]), "wishu": lambda: cp(T.wu[:], T.ki[:, 16:32], ["ki2"], ["wu"]),
            "mark": lambda: act(T.ee[:, 0:4 * W].indirect(T.eu[:]), mark, F.Sigmoid, ["k01", "eu"], ee03),
            "sections": sections, "seev": see_v, "sees": see_s, "blocked": blocked,
            "free": lambda: mms([(pt, T.idn[:], T.pat[:], True, False)], ["idn"] + ["pat%d" % k for k in range(5)], ["ps1"]),
            "ahead": lambda: tables(T.wu[:], "wu"), "aheadl": lambda: to_lists(True),
            "step": lambda: tt(T.d1[:, 0, 0:64:4], T.ki[:, 16:32], T.d1[:, 0, 3:64:4], A.subtract, ["ki2", "old0"], ["dif0"]),
            "diff": lambda t: act(T.d1[:, t, 0:64:4], T.px[:, 0:16, COL[t - 1]], F.Copy, ["px.a"], ["dif%d" % t]),
            "neg": lambda j: act(T.nb[:, K * j:K * j + K], T.br[:, K * j:K * j + K], F.Copy, ["br%d" % j], ["nb%d" % j], scale=-1.0),
            "choose": choose, "new": new_lists}
        for t in plan(s):
            at[0] = (s, t)
            name = t.rstrip("0123456789")
            if not (last and name in move):
                fn = late.get(name) or move.get(name) or stage[name]
                if name == t:
                    fn()
                else:
                    fn(int(t[len(name):]))

    at[0] = "end"
    dma("s", T.yb[:], T.bb[:], ["bb"], ["yb"], "st_b")
    op("s", None, ["yb", "yc"], [], end=True)
    op("g", None, ["sd%d" % s for s in range(RO)], [], end=True)
    emit(g, T, ops)
